import numpy as np
import ml_dtypes


def mxq(x, axis, fmt="e4m3"):
    dtype, down = {"e4m3": (ml_dtypes.float8_e4m3fn, 7), "e5m2": (ml_dtypes.float8_e5m2, 14)}[fmt]
    v = np.moveaxis(np.asarray(x, np.float32).astype(ml_dtypes.bfloat16).astype(np.float64), axis, -1)
    blocks = v.reshape(v.shape[:-1] + (-1, 32))
    amax = np.abs(blocks).max(-1, keepdims=True)
    byte = np.maximum(np.where(amax > 0, np.frexp(amax)[1] - 1 + 127, 0) - down, 1)
    scale = np.exp2(byte - 127.0)
    codes = (blocks / scale).astype(np.float32).astype(dtype).astype(np.float64)
    return np.moveaxis((codes * scale).reshape(v.shape), -1, axis)


WIDE = False


def mx_kscale(k):
    if not WIDE:
        return np.ones(k)
    levels = np.array([18, -18])
    if k % 512:
        return np.exp2(np.random.permutation(np.resize(levels, k // 32))).repeat(32)
    a = np.empty((k // 512, 16))
    for p in range(k // 512):
        a[p, :8] = np.random.permutation(np.resize(levels, 8))
        for g in range(8):
            far = levels[np.abs(levels - a[p, g]) >= 10]
            a[p, g + 8] = far[np.random.randint(len(far))]
    return np.exp2(a.ravel()).repeat(32)


def f64(x):
    return np.asarray(x).astype(np.float64)


def striped(idx):
    return np.tile(np.asarray(idx).reshape(-1, 16).T, (8, 1)).astype(np.uint16)


def unstriped(offs):
    return offs[:16].T.reshape(-1).astype(np.int64)


B, N, T, D, DV, R = 1, 512, 2048, 512, 512, 1024


def setup_inputs():
    n = np.random.standard_normal
    idx = np.random.permutation(T)[:B * N]
    s = mx_kscale(D)[:, None]
    z = mx_kscale(R)[:, None]
    v = mx_kscale(DV)[:, None]
    q = n((B, D, R))
    do = n((B, DV, R))
    return {
        "qT": (q * s).astype(np.float32),
        "kT": (n((D, T)) * (1.00 / np.sqrt(D)) / s).astype(np.float32),
        "vT": (n((DV, T)) / np.sqrt(DV) / v).astype(np.float32),
        "doT": (do * v).astype(np.float32),
        "rw": (np.random.uniform(0.5, 1.5, (B, R, 1)) * 1.0 / np.sqrt(R) * z).astype(np.float32),
        "qm": (q.transpose(0, 2, 1) / z).astype(np.float32),
        "offs": striped(idx),
    }


def reference(qT, kT, vT, doT, rw, qm, offs):
    idx = unstriped(offs)
    pick = lambda x: x[:, idx].reshape(x.shape[0], B, N).transpose(1, 0, 2)
    a = mxq(f64(qT), 1, "e4m3").transpose(0, 2, 1) @ mxq(pick(f64(kT)), 1, "e4m3")
    dp = mxq(f64(doT), 1, "e5m2").transpose(0, 2, 1) @ mxq(pick(f64(vT)), 1, "e4m3")
    ds = f64(rw) * dp * 2.0 * np.maximum(a, 0.0)
    dk = mxq(f64(qm), 1, "e4m3").transpose(0, 2, 1) @ mxq(ds, 1, "e5m2")
    gk = np.zeros((D, T))
    gk[:, idx] = dk.transpose(1, 0, 2).reshape(D, B * N)
    return gk

@@ -1,0 +1,214 @@
+from contextlib import ExitStack
+
+import concourse.mybir as mybir
+
+N, T, D, DV, R = 512, 2048, 512, 512, 1024
+FLOPS = 2 * R * N * (D + DV + D)
+
+F32 = mybir.dt.float32
+BF16 = mybir.dt.bfloat16
+U32 = mybir.dt.uint32
+U16 = mybir.dt.uint16
+U8 = mybir.dt.uint8
+E4 = mybir.dt.float8_e4m3fn_x4
+E5 = mybir.dt.float8_e5m2_x4
+ALU = mybir.AluOpType
+COPY = mybir.ActivationFunctionType.Copy
+
+P = 128
+PACK = 4
+PASS = P * PACK
+PIECE = PASS // 2
+
+
+def tile_attend_gat_k_kernel(tc, qT, kT, vT, doT, rw, qm, offs, out):
+    nc = tc.nc
+    with ExitStack() as ctx:
+        lists = ctx.enter_context(tc.tile_pool(name="lists", bufs=1))
+        sb = ctx.enter_context(tc.tile_pool(name="sb", bufs=1))
+        ps = ctx.enter_context(tc.psum_pool(name="ps", bufs=4))
+
+        def tile(shape, dtype, name):
+            return sb.tile(shape, dtype, name=name, align_bytes=64)
+
+        def load_planes(pool, name):
+            planes = []
+            rows = pool.rearrange("(p j) t -> p j t", j=PACK)
+            for j in range(PACK):
+                plane = tile([P, T], F32, f"{name}{j}")
+                nc.sync.dma_start(out=plane[:], in_=rows[:, j, :])
+                planes.append(plane)
+            return planes
+
+        def load_pieces(src, g, name):
+            pieces = []
+            rows = src[0].rearrange("(p j) r -> p j r", j=PACK)
+            for h in range(2):
+                piece = tile([P, PACK, PIECE], F32, f"{name}{g}{h}")
+                r0 = g * PASS + h * PIECE
+                nc.sync.dma_start(out=piece[:], in_=rows[:, :, r0 : r0 + PIECE])
+                pieces.append(piece)
+            return pieces
+
+        offsets = lists.tile([P, N // 16], U16, name="offsets")
+        nc.sync.dma_start(offsets[:], offs)
+        v_planes = load_planes(vT, "v")
+        gate = tile([P, 2, PACK], F32, "gate")
+        nc.sync.dma_start(out=gate[:], in_=rw[0].rearrange("(g s t) o -> s g (t o)", g=2, t=PACK))
+        do_raw = [load_pieces(doT, 0, "do")]
+        k_planes = load_planes(kT, "k")
+        q_raw = [load_pieces(qT, 0, "q")]
+        do_raw.append(load_pieces(doT, 1, "do"))
+        q_raw.append(load_pieces(qT, 1, "q"))
+        qm_raw = []
+        for g in range(2):
+            raw = tile([P, PACK, D], F32, f"qm{g}")
+            nc.sync.dma_start(out=raw[:], in_=qm[0, g * PASS : (g + 1) * PASS, :].rearrange("(p j) d -> p j d", j=PACK))
+            qm_raw.append(raw)
+
+        windows = []
+        for j in range(D // P):
+            window = tile([P, T], F32, f"window{j}")
+            nc.vector.memset(window[:], 0.0)
+            windows.append(window)
+
+        def mx_pair(name, width):
+            return tile([P, width], U32, name + "_codes"), tile([P, width], U8, name + "_scales")
+
+        def quantize(pair, cols, src, fmt):
+            nc.vector.quantize_mx(out=pair[0][:, cols].bitcast(fmt), scales=pair[1][:, cols], in_=src)
+
+        def gather(planes, name):
+            words = tile([P, N, PACK], BF16, name + "_words")
+            for j in range(PACK):
+                nc.vector.tensor_copy(words[:, :, j], planes[j][:].indirect(offsets[:]))
+            pair = mx_pair(name, N)
+            quantize(pair, slice(0, N), words[:].rearrange("p n j -> p (n j)"), E4)
+            return pair
+
+        def deal(copy, dealt, piece, h):
+            copy(
+                dealt[:, :, h * (P // 2) : (h + 1) * (P // 2), :].rearrange("p t s j -> p s j t"),
+                piece[:].rearrange("p j (s t) -> p s j t", t=PACK),
+            )
+
+        def deal_quantize(dealt, name, fmt):
+            pair = mx_pair(name, PASS)
+            quantize(pair, slice(0, PASS), dealt[:].rearrange("p t s j -> p (t s j)"), fmt)
+            return pair
+
+        def mm(acc, lhs, lcols, lfmt, rhs, rcols, rfmt, start=True, stop=True):
+            nc.tensor.matmul_mx(
+                out=acc,
+                lhsT=lhs[0][:, lcols].bitcast(lfmt),
+                lhsT_scale=lhs[1][:, lcols],
+                rhs=rhs[0][:, rcols].bitcast(rfmt),
+                rhs_scale=rhs[1][:, rcols],
+                start=start,
+                stop=stop,
+            )
+
+        def block(i):
+            return slice(i * P, (i + 1) * P)
+
+        def dp_products(do_mx, v_mx):
+            banks = []
+            for t in range(PACK):
+                bank = ps.tile([P, N], F32, name="wide", tag="wide")
+                mm(bank[:], do_mx, block(t), E5, v_mx, slice(0, N), E4)
+                banks.append(bank)
+            return banks
+
+        def dp_out(banks, g, h):
+            half = tile([P, PACK, N // 2], F32, f"dp{g}{h}")
+            for t in range(PACK):
+                nc.scalar.activation(
+                    half[:, t, :], banks[t][:, h * (N // 2) : (h + 1) * (N // 2)], COPY, scale=gate2[:, g, t : t + 1]
+                )
+            return half
+
+        def scores(q_mx, k_mx, c):
+            bank = ps.tile([P, PACK, P], F32, name="score", tag="score")
+            for t in range(PACK):
+                mm(bank[:, t, :], q_mx, block(t), E4, k_mx, block(c), E4)
+            return bank
+
+        def ds_words(bank, dp_halves, g, c):
+            words = tile([P, P, PACK], BF16, f"ds{g}{c}")
+            nc.vector.scalar_tensor_tensor(
+                out=words[:],
+                in0=bank[:].rearrange("p t n -> p n t"),
+                scalar=0.0,
+                in1=dp_halves[c // 2][:, :, block(c % 2)].rearrange("p t n -> p n t"),
+                op0=ALU.max,
+                op1=ALU.mult,
+            )
+            return words
+
+        def ds_quantize(pair, words, c):
+            quantize(pair, block(c), words[:].rearrange("p n t -> p (n t)"), E5)
+
+        dealt = {name: tile([P, PACK, P, PACK], BF16, name + "_dealt") for name in ("do0", "do1", "q0", "q1")}
+
+        v_mx = gather(v_planes, "v")
+        gate2 = tile([P, 2, PACK], F32, "gate2")
+        nc.vector.tensor_scalar(gate2[:], gate[:], 2.0, None, ALU.mult)
+        for h in range(2):
+            deal(nc.scalar.copy, dealt["do0"], do_raw[0][h], h)
+        do_mx = deal_quantize(dealt["do0"], "do0", E5)
+        banks = dp_products(do_mx, v_mx)
+        dp0 = [dp_out(banks, 0, h) for h in range(2)]
+
+        k_mx = gather(k_planes, "k")
+        deal(nc.scalar.copy, dealt["q0"], q_raw[0][0], 0)
+        deal(nc.vector.tensor_copy, dealt["q0"], q_raw[0][1], 1)
+        for h in range(2):
+            deal(nc.scalar.copy, dealt["do1"], do_raw[1][h], h)
+        for h in range(2):
+            deal(nc.scalar.copy, dealt["q1"], q_raw[1][h], h)
+
+        q_mx = deal_quantize(dealt["q0"], "q0", E4)
+        score0 = [scores(q_mx, k_mx, c) for c in range(PACK)]
+        ds_mx = [mx_pair(f"ds{g}", N) for g in range(2)]
+        words = [ds_words(score0[c], dp0, 0, c) for c in range(2)]
+        do_mx = deal_quantize(dealt["do1"], "do1", E5)
+        banks = dp_products(do_mx, v_mx)
+        dp1 = [dp_out(banks, 1, h) for h in range(2)]
+        words.extend(ds_words(score0[c], dp0, 0, c) for c in range(2, PACK))
+        q_mx = deal_quantize(dealt["q1"], "q1", E4)
+        score1 = [scores(q_mx, k_mx, c) for c in range(PACK)]
+        for c in range(PACK):
+            ds_quantize(ds_mx[0], words[c], c)
+
+        qm_words = {}
+        for h in range(2):
+            for g in range(2):
+                qm_words[g, h] = tile([P, D // 2, PACK], BF16, f"qmw{g}{h}")
+                nc.scalar.copy(
+                    qm_words[g, h][:].rearrange("p (c i) j -> p c j i", i=4),
+                    qm_raw[g][:, :, h * (D // 2) : (h + 1) * (D // 2)].rearrange("p j (c i) -> p c j i", i=4),
+                )
+        qm_mx = {gh: mx_pair(f"qm{gh[0]}{gh[1]}", D // 2) for gh in qm_words}
+
+        def qm_quantize(g, h):
+            quantize(qm_mx[g, h], slice(0, D // 2), qm_words[g, h][:].rearrange("p d j -> p (d j)"), E4)
+
+        words = []
+        for c in range(PACK):
+            words.append(ds_words(score1[c], dp1, 1, c))
+            if c > 0:
+                ds_quantize(ds_mx[1], words[c - 1], c - 1)
+        qm_quantize(0, 0)
+        qm_quantize(1, 0)
+        ds_quantize(ds_mx[1], words[PACK - 1], PACK - 1)
+        qm_quantize(0, 1)
+        qm_quantize(1, 1)
+
+        for j in range(D // P):
+            bank = ps.tile([P, N], F32, name="wide", tag="wide")
+            for g in range(2):
+                mm(bank[:], qm_mx[g, j // 2], block(j % 2), E4, ds_mx[g], slice(0, N), E5, start=g == 0, stop=g == 1)
+            dk = tile([P, N], F32, f"dk{j}")
+            nc.scalar.copy(dk[:], bank[:])
+            nc.vector.tensor_copy(windows[j][:].indirect(offsets[:]), dk[:])
+            nc.sync.dma_start(out=out[block(j), :], in_=windows[j][:])

@@ -18,7 +18,7 @@ COPY = mybir.ActivationFunctionType.Copy
 P = 128
 PACK = 4
 PASS = P * PACK
-PIECE = PASS // 2
+SPLIT = 48
 
 
 def tile_attend_gat_k_kernel(tc, qT, kT, vT, doT, rw, qm, offs, out):
@@ -40,31 +40,23 @@ def tile_attend_gat_k_kernel(tc, qT, kT, vT, doT, rw, qm, offs, out):
                 planes.append(plane)
             return planes
 
-        def load_pieces(src, g, name):
-            pieces = []
-            rows = src[0].rearrange("(p j) r -> p j r", j=PACK)
-            for h in range(2):
-                piece = tile([P, PACK, PIECE], F32, f"{name}{g}{h}")
-                r0 = g * PASS + h * PIECE
-                nc.sync.dma_start(out=piece[:], in_=rows[:, :, r0 : r0 + PIECE])
-                pieces.append(piece)
-            return pieces
+        def load_columns(src, r0, width, name):
+            raw = tile([P, PACK, width], F32, name)
+            rows = src.rearrange("(p j) r -> p j r", j=PACK)
+            nc.sync.dma_start(out=raw[:], in_=rows[:, :, r0 : r0 + width])
+            return raw
 
         offsets = lists.tile([P, N // 16], U16, name="offsets")
         nc.sync.dma_start(offsets[:], offs)
         v_planes = load_planes(vT, "v")
         gate = tile([P, 2, PACK], F32, "gate")
         nc.sync.dma_start(out=gate[:], in_=rw[0].rearrange("(g s t) o -> s g (t o)", g=2, t=PACK))
-        do_raw = [load_pieces(doT, 0, "do")]
+        do_raw = [load_columns(doT[0], g * PASS, PASS, f"do{g}") for g in range(2)]
         k_planes = load_planes(kT, "k")
-        q_raw = [load_pieces(qT, 0, "q")]
-        do_raw.append(load_pieces(doT, 1, "do"))
-        q_raw.append(load_pieces(qT, 1, "q"))
-        qm_raw = []
-        for g in range(2):
-            raw = tile([P, PACK, D], F32, f"qm{g}")
-            nc.sync.dma_start(out=raw[:], in_=qm[0, g * PASS : (g + 1) * PASS, :].rearrange("(p j) d -> p j d", j=PACK))
-            qm_raw.append(raw)
+        q0_raw = load_columns(qT[0], 0, PASS, "q0")
+        q1_raw = load_columns(qT[0], PASS, PASS, "q1")
+        qm0_raw = load_columns(qm[0, 0:PASS, :], 0, D, "qm0")
+        qm1_raw = [load_columns(qm[0, PASS:R, :], h * (D // 2), D // 2, f"qm1{h}") for h in range(2)]
 
         windows = []
         for j in range(D // P):
@@ -86,10 +78,10 @@ def tile_attend_gat_k_kernel(tc, qT, kT, vT, doT, rw, qm, offs, out):
             quantize(pair, slice(0, N), words[:].rearrange("p n j -> p (n j)"), E4)
             return pair
 
-        def deal(copy, dealt, piece, h):
+        def deal(copy, dealt, s0, s1, raw):
             copy(
-                dealt[:, :, h * (P // 2) : (h + 1) * (P // 2), :].rearrange("p t s j -> p s j t"),
-                piece[:].rearrange("p j (s t) -> p s j t", t=PACK),
+                dealt[:, :, s0:s1, :].rearrange("p t s j -> p s j t"),
+                raw.rearrange("p j (s t) -> p s j t", t=PACK),
             )
 
         def deal_quantize(dealt, name, fmt):
@@ -111,21 +103,25 @@ def tile_attend_gat_k_kernel(tc, qT, kT, vT, doT, rw, qm, offs, out):
         def block(i):
             return slice(i * P, (i + 1) * P)
 
-        def dp_products(do_mx, v_mx):
-            banks = []
+        def dp_rows(do_mx, v_mx, g):
+            rows = tile([P, PACK, N], F32, f"dp{g}")
             for t in range(PACK):
                 bank = ps.tile([P, N], F32, name="wide", tag="wide")
                 mm(bank[:], do_mx, block(t), E5, v_mx, slice(0, N), E4)
-                banks.append(bank)
-            return banks
+                nc.scalar.activation(rows[:, t, :], bank[:], COPY, scale=gate2[:, g, t : t + 1])
+            return rows
 
-        def dp_out(banks, g, h):
-            half = tile([P, PACK, N // 2], F32, f"dp{g}{h}")
-            for t in range(PACK):
-                nc.scalar.activation(
-                    half[:, t, :], banks[t][:, h * (N // 2) : (h + 1) * (N // 2)], COPY, scale=gate2[:, g, t : t + 1]
-                )
-            return half
+        def weave(dst, src):
+            nc.scalar.copy(
+                dst.rearrange("p (c i) j -> p c j i", i=4),
+                src.rearrange("p j (c i) -> p c j i", i=4),
+            )
+
+        def dp_weave(rows, g):
+            woven = tile([P, N, PACK], F32, f"do{g}")
+            for c in range(PACK):
+                weave(woven[:, block(c), :], rows[:, :, block(c)])
+            return woven
 
         def scores(q_mx, k_mx, c):
             bank = ps.tile([P, PACK, P], F32, name="score", tag="score")
@@ -133,13 +129,13 @@ def tile_attend_gat_k_kernel(tc, qT, kT, vT, doT, rw, qm, offs, out):
                 mm(bank[:, t, :], q_mx, block(t), E4, k_mx, block(c), E4)
             return bank
 
-        def ds_words(bank, dp_halves, g, c):
+        def ds_words(bank, dp, g, c):
             words = tile([P, P, PACK], BF16, f"ds{g}{c}")
             nc.vector.scalar_tensor_tensor(
                 out=words[:],
                 in0=bank[:].rearrange("p t n -> p n t"),
                 scalar=0.0,
-                in1=dp_halves[c // 2][:, :, block(c % 2)].rearrange("p t n -> p n t"),
+                in1=dp[:, block(c), :],
                 op0=ALU.max,
                 op1=ALU.mult,
             )
@@ -153,61 +149,52 @@ def tile_attend_gat_k_kernel(tc, qT, kT, vT, doT, rw, qm, offs, out):
         v_mx = gather(v_planes, "v")
         gate2 = tile([P, 2, PACK], F32, "gate2")
         nc.vector.tensor_scalar(gate2[:], gate[:], 2.0, None, ALU.mult)
-        for h in range(2):
-            deal(nc.scalar.copy, dealt["do0"], do_raw[0][h], h)
-        do_mx = deal_quantize(dealt["do0"], "do0", E5)
-        banks = dp_products(do_mx, v_mx)
-        dp0 = [dp_out(banks, 0, h) for h in range(2)]
+        dp = []
+        for g in range(2):
+            deal(nc.vector.tensor_copy, dealt[f"do{g}"], 0, P, do_raw[g][:])
+            do_mx = deal_quantize(dealt[f"do{g}"], f"do{g}", E5)
+            dp.append(dp_rows(do_mx, v_mx, g))
+        dp = [dp_weave(dp[g], g) for g in range(2)]
 
         k_mx = gather(k_planes, "k")
-        deal(nc.scalar.copy, dealt["q0"], q_raw[0][0], 0)
-        deal(nc.vector.tensor_copy, dealt["q0"], q_raw[0][1], 1)
-        for h in range(2):
-            deal(nc.scalar.copy, dealt["do1"], do_raw[1][h], h)
-        for h in range(2):
-            deal(nc.scalar.copy, dealt["q1"], q_raw[1][h], h)
+        deal(nc.scalar.copy, dealt["q0"], 0, SPLIT, q0_raw[:, :, 0 : PACK * SPLIT])
+        deal(nc.vector.tensor_copy, dealt["q0"], SPLIT, P, q0_raw[:, :, PACK * SPLIT : PASS])
+        deal(nc.scalar.copy, dealt["q1"], 0, P, q1_raw[:])
 
         q_mx = deal_quantize(dealt["q0"], "q0", E4)
-        score0 = [scores(q_mx, k_mx, c) for c in range(PACK)]
+        score = [scores(q_mx, k_mx, c) for c in range(PACK)]
         ds_mx = [mx_pair(f"ds{g}", N) for g in range(2)]
-        words = [ds_words(score0[c], dp0, 0, c) for c in range(2)]
-        do_mx = deal_quantize(dealt["do1"], "do1", E5)
-        banks = dp_products(do_mx, v_mx)
-        dp1 = [dp_out(banks, 1, h) for h in range(2)]
-        words.extend(ds_words(score0[c], dp0, 0, c) for c in range(2, PACK))
+        words = [ds_words(score[c], dp[0], 0, c) for c in range(PACK)]
         q_mx = deal_quantize(dealt["q1"], "q1", E4)
-        score1 = [scores(q_mx, k_mx, c) for c in range(PACK)]
+        score = [scores(q_mx, k_mx, c) for c in range(PACK)]
         for c in range(PACK):
             ds_quantize(ds_mx[0], words[c], c)
 
+        qm_mx = [mx_pair(f"qm{g}", D) for g in range(2)]
         qm_words = {}
-        for h in range(2):
-            for g in range(2):
-                qm_words[g, h] = tile([P, D // 2, PACK], BF16, f"qmw{g}{h}")
-                nc.scalar.copy(
-                    qm_words[g, h][:].rearrange("p (c i) j -> p c j i", i=4),
-                    qm_raw[g][:, :, h * (D // 2) : (h + 1) * (D // 2)].rearrange("p j (c i) -> p c j i", i=4),
-                )
-        qm_mx = {gh: mx_pair(f"qm{gh[0]}{gh[1]}", D // 2) for gh in qm_words}
+        for j in range(D // P):
+            for g, raw in enumerate((qm0_raw[:, :, block(j)], qm1_raw[j // 2][:, :, block(j % 2)])):
+                qm_words[g, j] = tile([P, P, PACK], BF16, f"qm_words{g}{j}")
+                weave(qm_words[g, j][:], raw)
 
-        def qm_quantize(g, h):
-            quantize(qm_mx[g, h], slice(0, D // 2), qm_words[g, h][:].rearrange("p d j -> p (d j)"), E4)
+        def qm_quantize(j):
+            for g in range(2):
+                quantize(qm_mx[g], block(j), qm_words[g, j][:].rearrange("p d j -> p (d j)"), E4)
 
         words = []
         for c in range(PACK):
-            words.append(ds_words(score1[c], dp1, 1, c))
+            words.append(ds_words(score[c], dp[1], 1, c))
             if c > 0:
                 ds_quantize(ds_mx[1], words[c - 1], c - 1)
-        qm_quantize(0, 0)
-        qm_quantize(1, 0)
+        qm_quantize(0)
         ds_quantize(ds_mx[1], words[PACK - 1], PACK - 1)
-        qm_quantize(0, 1)
-        qm_quantize(1, 1)
 
         for j in range(D // P):
+            if j > 0:
+                qm_quantize(j)
             bank = ps.tile([P, N], F32, name="wide", tag="wide")
             for g in range(2):
-                mm(bank[:], qm_mx[g, j // 2], block(j % 2), E4, ds_mx[g], slice(0, N), E5, start=g == 0, stop=g == 1)
+                mm(bank[:], qm_mx[g], block(j), E4, ds_mx[g], slice(0, N), E5, start=g == 0, stop=g == 1)
             dk = tile([P, N], F32, f"dk{j}")
             nc.scalar.copy(dk[:], bank[:])
             nc.vector.tensor_copy(windows[j][:].indirect(offsets[:]), dk[:])

@@ -18,7 +18,6 @@ COPY = mybir.ActivationFunctionType.Copy
 P = 128
 PACK = 4
 PASS = P * PACK
-SPLIT = 48
 
 
 def tile_attend_gat_k_kernel(tc, qT, kT, vT, doT, rw, qm, offs, out):
@@ -31,14 +30,10 @@ def tile_attend_gat_k_kernel(tc, qT, kT, vT, doT, rw, qm, offs, out):
         def tile(shape, dtype, name):
             return sb.tile(shape, dtype, name=name, align_bytes=64)
 
-        def load_planes(pool, name):
-            planes = []
-            rows = pool.rearrange("(p j) t -> p j t", j=PACK)
-            for j in range(PACK):
-                plane = tile([P, T], F32, f"{name}{j}")
-                nc.sync.dma_start(out=plane[:], in_=rows[:, j, :])
-                planes.append(plane)
-            return planes
+        def load_planes(pool, name, j0, count):
+            held = tile([P, count, T], F32, f"{name}{j0}")
+            nc.sync.dma_start(out=held[:], in_=pool.rearrange("(p j) t -> p j t", j=PACK)[:, j0 : j0 + count, :])
+            return [held[:, i, :] for i in range(count)]
 
         def load_columns(src, r0, width, name):
             raw = tile([P, PACK, width], F32, name)
@@ -46,13 +41,14 @@ def tile_attend_gat_k_kernel(tc, qT, kT, vT, doT, rw, qm, offs, out):
             nc.sync.dma_start(out=raw[:], in_=rows[:, :, r0 : r0 + width])
             return raw
 
+        v_planes = load_planes(vT, "v", 0, 2)
         offsets = lists.tile([P, N // 16], U16, name="offsets")
         nc.sync.dma_start(offsets[:], offs)
-        v_planes = load_planes(vT, "v")
         gate = tile([P, 2, PACK], F32, "gate")
         nc.sync.dma_start(out=gate[:], in_=rw[0].rearrange("(g s t) o -> s g (t o)", g=2, t=PACK))
-        do_raw = [load_columns(doT[0], g * PASS, PASS, f"do{g}") for g in range(2)]
-        k_planes = load_planes(kT, "k")
+        v_planes.extend(load_planes(vT, "v", 2, 2))
+        do_raw = load_columns(doT[0], 0, R, "do")
+        k_planes = [load_planes(kT, "k", j, 1)[0] for j in range(PACK)]
         q0_raw = load_columns(qT[0], 0, PASS, "q0")
         q1_raw = load_columns(qT[0], PASS, PASS, "q1")
         qm0_raw = load_columns(qm[0, 0:PASS, :], 0, D, "qm0")
@@ -73,20 +69,26 @@ def tile_attend_gat_k_kernel(tc, qT, kT, vT, doT, rw, qm, offs, out):
         def gather(planes, name):
             words = tile([P, N, PACK], BF16, name + "_words")
             for j in range(PACK):
-                nc.vector.tensor_copy(words[:, :, j], planes[j][:].indirect(offsets[:]))
+                nc.vector.tensor_copy(words[:, :, j], planes[j].indirect(offsets[:]))
             pair = mx_pair(name, N)
             quantize(pair, slice(0, N), words[:].rearrange("p n j -> p (n j)"), E4)
             return pair
 
-        def deal(copy, dealt, s0, s1, raw):
-            copy(
-                dealt[:, :, s0:s1, :].rearrange("p t s j -> p s j t"),
-                raw.rearrange("p j (s t) -> p s j t", t=PACK),
-            )
+        def deal(raw, name, copies):
+            halves = []
+            for u, copy in enumerate(copies):
+                half = tile([P, 2, P, PACK], BF16, f"{name}_dealt{u}")
+                copy(
+                    half[:].rearrange("p t s j -> p s j t"),
+                    raw.rearrange("p j (s t) -> p s j t", t=PACK)[:, :, :, 2 * u : 2 * u + 2],
+                )
+                halves.append(half)
+            return halves
 
-        def deal_quantize(dealt, name, fmt):
+        def deal_quantize(halves, name, fmt):
             pair = mx_pair(name, PASS)
-            quantize(pair, slice(0, PASS), dealt[:].rearrange("p t s j -> p (t s j)"), fmt)
+            for u, half in enumerate(halves):
+                quantize(pair, slice(2 * u * P, 2 * (u + 1) * P), half[:].rearrange("p t s j -> p (t s j)"), fmt)
             return pair
 
         def mm(acc, lhs, lcols, lfmt, rhs, rcols, rfmt, start=True, stop=True):
@@ -106,95 +108,107 @@ def tile_attend_gat_k_kernel(tc, qT, kT, vT, doT, rw, qm, offs, out):
         def dp_rows(do_mx, v_mx, g):
             rows = tile([P, PACK, N], F32, f"dp{g}")
             for t in range(PACK):
-                bank = ps.tile([P, N], F32, name="wide", tag="wide")
+                bank = ps.tile([P, N], F32, name="dp_bank", bufs=4)
                 mm(bank[:], do_mx, block(t), E5, v_mx, slice(0, N), E4)
                 nc.scalar.activation(rows[:, t, :], bank[:], COPY, scale=gate2[:, g, t : t + 1])
             return rows
 
-        def weave(dst, src):
-            nc.scalar.copy(
+        def weave(copy, dst, src):
+            copy(
                 dst.rearrange("p (c i) j -> p c j i", i=4),
                 src.rearrange("p j (c i) -> p c j i", i=4),
             )
 
-        def dp_weave(rows, g):
-            woven = tile([P, N, PACK], F32, f"do{g}")
-            for c in range(PACK):
-                weave(woven[:, block(c), :], rows[:, :, block(c)])
-            return woven
-
         def scores(q_mx, k_mx, c):
-            bank = ps.tile([P, PACK, P], F32, name="score", tag="score")
+            bank = ps.tile([P, PACK, P], F32, name="score", bufs=3)
             for t in range(PACK):
                 mm(bank[:, t, :], q_mx, block(t), E4, k_mx, block(c), E4)
             return bank
 
-        def ds_words(bank, dp, g, c):
-            words = tile([P, P, PACK], BF16, f"ds{g}{c}")
+        def ds_words(words, bank, g, c):
             nc.vector.scalar_tensor_tensor(
-                out=words[:],
+                out=words,
                 in0=bank[:].rearrange("p t n -> p n t"),
                 scalar=0.0,
-                in1=dp[:, block(c), :],
+                in1=woven[g, c],
                 op0=ALU.max,
                 op1=ALU.mult,
             )
-            return words
 
-        def ds_quantize(pair, words, c):
-            quantize(pair, block(c), words[:].rearrange("p n t -> p (n t)"), E5)
-
-        dealt = {name: tile([P, PACK, P, PACK], BF16, name + "_dealt") for name in ("do0", "do1", "q0", "q1")}
+        both = (nc.vector.tensor_copy, nc.scalar.copy)
 
         v_mx = gather(v_planes, "v")
         gate2 = tile([P, 2, PACK], F32, "gate2")
         nc.vector.tensor_scalar(gate2[:], gate[:], 2.0, None, ALU.mult)
         dp = []
         for g in range(2):
-            deal(nc.vector.tensor_copy, dealt[f"do{g}"], 0, P, do_raw[g][:])
-            do_mx = deal_quantize(dealt[f"do{g}"], f"do{g}", E5)
+            dealt = deal(do_raw[:, :, g * PASS : (g + 1) * PASS], f"do{g}", both)
+            do_mx = deal_quantize(dealt, f"do{g}", E5)
             dp.append(dp_rows(do_mx, v_mx, g))
-        dp = [dp_weave(dp[g], g) for g in range(2)]
+        early = tile([P, 2 * PACK - 1, P, PACK], F32, "do")
+        woven = {(g, c): early[:, g * PACK + c, :, :] for g in range(2) for c in range(PACK) if g + c < PACK}
+
+        def dp_weave(copy, g, c):
+            weave(copy, woven[g, c], dp[g][:, :, block(c)])
+
+        for c in range(PACK):
+            dp_weave(nc.scalar.copy if c == 0 else nc.vector.tensor_copy, 0, c)
 
         k_mx = gather(k_planes, "k")
-        deal(nc.scalar.copy, dealt["q0"], 0, SPLIT, q0_raw[:, :, 0 : PACK * SPLIT])
-        deal(nc.vector.tensor_copy, dealt["q0"], SPLIT, P, q0_raw[:, :, PACK * SPLIT : PASS])
-        deal(nc.scalar.copy, dealt["q1"], 0, P, q1_raw[:])
+        q0_dealt = deal(q0_raw[:], "q0", both)
+        for c in range(PACK - 1):
+            dp_weave(nc.scalar.copy, 1, c)
+        q1_dealt = deal(q1_raw[:], "q1", (nc.scalar.copy, nc.scalar.copy))
+        late = tile([P, P, PACK], F32, "q1")
+        woven[1, PACK - 1] = late[:]
+        dp_weave(nc.scalar.copy, 1, PACK - 1)
 
-        q_mx = deal_quantize(dealt["q0"], "q0", E4)
+        q_mx = deal_quantize(q0_dealt, "q0", E4)
         score = [scores(q_mx, k_mx, c) for c in range(PACK)]
         ds_mx = [mx_pair(f"ds{g}", N) for g in range(2)]
-        words = [ds_words(score[c], dp[0], 0, c) for c in range(PACK)]
-        q_mx = deal_quantize(dealt["q1"], "q1", E4)
-        score = [scores(q_mx, k_mx, c) for c in range(PACK)]
+        ds0 = tile([P, N, PACK], BF16, "ds0")
         for c in range(PACK):
-            ds_quantize(ds_mx[0], words[c], c)
+            ds_words(ds0[:, block(c), :], score[c], 0, c)
+        q_mx = deal_quantize(q1_dealt, "q1", E4)
+        score = [scores(q_mx, k_mx, c) for c in range(PACK)]
+        quantize(ds_mx[0], slice(0, N), ds0[:].rearrange("p n t -> p (n t)"), E5)
 
-        qm_mx = [mx_pair(f"qm{g}", D) for g in range(2)]
+        qm_scales = tile([P, 2, D], U8, "qm_scales")
+        first_codes = tile([P, 2, P], U32, "qm_first_codes")
+        qm_mx = {(g, 0): (first_codes[:, g, :], qm_scales[:, g, block(0)]) for g in range(2)}
         qm_words = {}
         for j in range(D // P):
             for g, raw in enumerate((qm0_raw[:, :, block(j)], qm1_raw[j // 2][:, :, block(j % 2)])):
                 qm_words[g, j] = tile([P, P, PACK], BF16, f"qm_words{g}{j}")
-                weave(qm_words[g, j][:], raw)
+                weave(nc.scalar.copy, qm_words[g, j][:], raw)
 
         def qm_quantize(j):
             for g in range(2):
-                quantize(qm_mx[g], block(j), qm_words[g, j][:].rearrange("p d j -> p (d j)"), E4)
+                quantize(qm_mx[g, j], block(0), qm_words[g, j][:].rearrange("p d j -> p (d j)"), E4)
 
-        words = []
-        for c in range(PACK):
-            words.append(ds_words(score[c], dp[1], 1, c))
-            if c > 0:
-                ds_quantize(ds_mx[1], words[c - 1], c - 1)
+        ds1 = tile([P, N, PACK], BF16, "ds1")
+
+        def ds1_quantize(cols):
+            quantize(ds_mx[1], cols, ds1[:, cols, :].rearrange("p n t -> p (n t)"), E5)
+
+        for c in range(PACK - 1):
+            ds_words(ds1[:, block(c), :], score[c], 1, c)
+        ds1_quantize(slice(0, N // 2))
         qm_quantize(0)
-        ds_quantize(ds_mx[1], words[PACK - 1], PACK - 1)
+        ds_words(ds1[:, block(3), :], score[3], 1, 3)
+        ds1_quantize(block(2))
+        ds1_quantize(block(3))
+        later_codes = tile([P, 2, D // P - 1, P], U32, "ds1")
+        for j in range(1, D // P):
+            for g in range(2):
+                qm_mx[g, j] = (later_codes[:, g, j - 1, :], qm_scales[:, g, block(j)])
 
         for j in range(D // P):
             if j > 0:
                 qm_quantize(j)
-            bank = ps.tile([P, N], F32, name="wide", tag="wide")
+            bank = ps.tile([P, N], F32, name="dk_bank", bufs=1)
             for g in range(2):
-                mm(bank[:], qm_mx[g], block(j), E4, ds_mx[g], slice(0, N), E5, start=g == 0, stop=g == 1)
+                mm(bank[:], qm_mx[g, j], block(0), E4, ds_mx[g], slice(0, N), E5, start=g == 0, stop=g == 1)
             dk = tile([P, N], F32, f"dk{j}")
             nc.scalar.copy(dk[:], bank[:])
             nc.vector.tensor_copy(windows[j][:].indirect(offsets[:]), dk[:])

@@ -145,23 +145,23 @@ def tile_attend_gat_k_kernel(tc, qT, kT, vT, doT, rw, qm, offs, out):
             dealt = deal(do_raw[:, :, g * PASS : (g + 1) * PASS], f"do{g}", both)
             do_mx = deal_quantize(dealt, f"do{g}", E5)
             dp.append(dp_rows(do_mx, v_mx, g))
-        early = tile([P, 2 * PACK - 1, P, PACK], F32, "do")
-        woven = {(g, c): early[:, g * PACK + c, :, :] for g in range(2) for c in range(PACK) if g + c < PACK}
+        woven = {}
 
-        def dp_weave(copy, g, c):
-            weave(copy, woven[g, c], dp[g][:, :, block(c)])
+        def dp_weave(quarters, host):
+            held = tile([P, len(quarters), P, PACK], F32, host)
+            for i, (g, c) in enumerate(quarters):
+                woven[g, c] = held[:, i, :, :]
+                copy = nc.vector.tensor_copy if (g, c) == (0, PACK - 1) else nc.scalar.copy
+                weave(copy, woven[g, c], dp[g][:, :, block(c)])
 
-        for c in range(PACK):
-            dp_weave(nc.scalar.copy if c == 0 else nc.vector.tensor_copy, 0, c)
+        quarters = [(g, c) for g in range(2) for c in range(PACK)]
+        dp_weave(quarters[:5], "do")
 
         k_mx = gather(k_planes, "k")
         q0_dealt = deal(q0_raw[:], "q0", both)
-        for c in range(PACK - 1):
-            dp_weave(nc.scalar.copy, 1, c)
+        dp_weave(quarters[5:6], "q0")
         q1_dealt = deal(q1_raw[:], "q1", (nc.scalar.copy, nc.scalar.copy))
-        late = tile([P, P, PACK], F32, "q1")
-        woven[1, PACK - 1] = late[:]
-        dp_weave(nc.scalar.copy, 1, PACK - 1)
+        dp_weave(quarters[6:], "q1")
 
         q_mx = deal_quantize(q0_dealt, "q0", E4)
         score = [scores(q_mx, k_mx, c) for c in range(PACK)]
@@ -179,12 +179,17 @@ def tile_attend_gat_k_kernel(tc, qT, kT, vT, doT, rw, qm, offs, out):
         qm_words = {}
         for j in range(D // P):
             for g, raw in enumerate((qm0_raw[:, :, block(j)], qm1_raw[j // 2][:, :, block(j % 2)])):
-                qm_words[g, j] = tile([P, P, PACK], BF16, f"qm_words{g}{j}")
-                weave(nc.scalar.copy, qm_words[g, j][:], raw)
+                if g == 0 and j == 1:
+                    held = tile([P, D // P - 1, P, PACK], BF16, "q1_dealt0")
+                if g == 0 and j > 0:
+                    qm_words[g, j] = held[:, j - 1, :, :]
+                else:
+                    qm_words[g, j] = tile([P, P, PACK], BF16, f"qm_words{g}{j}")[:]
+                weave(nc.scalar.copy, qm_words[g, j], raw)
 
         def qm_quantize(j):
             for g in range(2):
-                quantize(qm_mx[g, j], block(0), qm_words[g, j][:].rearrange("p d j -> p (d j)"), E4)
+                quantize(qm_mx[g, j], block(0), qm_words[g, j].rearrange("p d j -> p (d j)"), E4)
 
         ds1 = tile([P, N, PACK], BF16, "ds1")
 

@@ -18,6 +18,7 @@ COPY = mybir.ActivationFunctionType.Copy
 P = 128
 PACK = 4
 PASS = P * PACK
+SPLIT = 96
 
 
 def tile_attend_gat_k_kernel(tc, qT, kT, vT, doT, rw, qm, offs, out):
@@ -74,15 +75,13 @@ def tile_attend_gat_k_kernel(tc, qT, kT, vT, doT, rw, qm, offs, out):
             quantize(pair, slice(0, N), words[:].rearrange("p n j -> p (n j)"), E4)
             return pair
 
-        def deal(raw, name, copies):
-            halves = []
-            for u, copy in enumerate(copies):
-                half = tile([P, 2, P, PACK], BF16, f"{name}_dealt{u}")
+        def deal(raw, name, shares):
+            halves = [tile([P, 2, P, PACK], BF16, f"{name}_dealt{u}") for u in range(2)]
+            for copy, u, s0, s1 in shares:
                 copy(
-                    half[:].rearrange("p t s j -> p s j t"),
-                    raw.rearrange("p j (s t) -> p s j t", t=PACK)[:, :, :, 2 * u : 2 * u + 2],
+                    halves[u][:, :, s0:s1, :].rearrange("p t s j -> p s j t"),
+                    raw.rearrange("p j (s t) -> p s j t", t=PACK)[:, s0:s1, :, 2 * u : 2 * u + 2],
                 )
-                halves.append(half)
             return halves
 
         def deal_quantize(halves, name, fmt):
@@ -135,7 +134,8 @@ def tile_attend_gat_k_kernel(tc, qT, kT, vT, doT, rw, qm, offs, out):
                 op1=ALU.mult,
             )
 
-        both = (nc.vector.tensor_copy, nc.scalar.copy)
+        both = ((nc.vector.tensor_copy, 0, 0, P), (nc.scalar.copy, 1, 0, P))
+        q0_shares = ((nc.scalar.copy, 1, 0, SPLIT), (nc.vector.tensor_copy, 0, 0, P), (nc.vector.tensor_copy, 1, SPLIT, P))
 
         v_mx = gather(v_planes, "v")
         gate2 = tile([P, 2, PACK], F32, "gate2")
@@ -158,9 +158,9 @@ def tile_attend_gat_k_kernel(tc, qT, kT, vT, doT, rw, qm, offs, out):
         dp_weave(quarters[:5], "do")
 
         k_mx = gather(k_planes, "k")
-        q0_dealt = deal(q0_raw[:], "q0", both)
+        q0_dealt = deal(q0_raw[:], "q0", q0_shares)
         dp_weave(quarters[5:6], "q0")
-        q1_dealt = deal(q1_raw[:], "q1", (nc.scalar.copy, nc.scalar.copy))
+        q1_dealt = deal(q1_raw[:], "q1", ((nc.scalar.copy, 0, 0, P), (nc.scalar.copy, 1, 0, P)))
         dp_weave(quarters[6:], "q1")
 
         q_mx = deal_quantize(q0_dealt, "q0", E4)
@@ -193,16 +193,10 @@ def tile_attend_gat_k_kernel(tc, qT, kT, vT, doT, rw, qm, offs, out):
 
         ds1 = tile([P, N, PACK], BF16, "ds1")
 
-        def ds1_quantize(cols):
-            quantize(ds_mx[1], cols, ds1[:, cols, :].rearrange("p n t -> p (n t)"), E5)
-
-        for c in range(PACK - 1):
+        for c in range(PACK):
             ds_words(ds1[:, block(c), :], score[c], 1, c)
-        ds1_quantize(slice(0, N // 2))
         qm_quantize(0)
-        ds_words(ds1[:, block(3), :], score[3], 1, 3)
-        ds1_quantize(block(2))
-        ds1_quantize(block(3))
+        quantize(ds_mx[1], slice(0, N), ds1[:].rearrange("p n t -> p (n t)"), E5)
         later_codes = tile([P, 2, D // P - 1, P], U32, "ds1")
         for j in range(1, D // P):
             for g in range(2):

@@ -19,6 +19,8 @@ P = 128
 PACK = 4
 PASS = P * PACK
 SPLIT = 96
+VECTOR_WEAVES = 3
+SCORE_BANKS = 3
 
 
 def tile_attend_gat_k_kernel(tc, qT, kT, vT, doT, rw, qm, offs, out):
@@ -49,11 +51,14 @@ def tile_attend_gat_k_kernel(tc, qT, kT, vT, doT, rw, qm, offs, out):
         nc.sync.dma_start(out=gate[:], in_=rw[0].rearrange("(g s t) o -> s g (t o)", g=2, t=PACK))
         v_planes.extend(load_planes(vT, "v", 2, 2))
         do_raw = load_columns(doT[0], 0, R, "do")
-        k_planes = [load_planes(kT, "k", j, 1)[0] for j in range(PACK)]
+        k_planes = []
+        for j in range(PACK):
+            k_planes.append(tile([P, T], F32, f"k{j}"))
+            nc.sync.dma_start(out=k_planes[j][:], in_=kT.rearrange("(p j) t -> p j t", j=PACK)[:, j, :])
         q0_raw = load_columns(qT[0], 0, PASS, "q0")
         q1_raw = load_columns(qT[0], PASS, PASS, "q1")
-        qm0_raw = load_columns(qm[0, 0:PASS, :], 0, D, "qm0")
-        qm1_raw = [load_columns(qm[0, PASS:R, :], h * (D // 2), D // 2, f"qm1{h}") for h in range(2)]
+        qm0_raw = load_columns(qm[0, 0:PASS, :], 0, D, "v0")
+        qm1_raw = [load_columns(qm[0, PASS:R, :], h * (D // 2), D // 2, ("v2", "qm1b")[h]) for h in range(2)]
 
         windows = []
         for j in range(D // P):
@@ -75,13 +80,16 @@ def tile_attend_gat_k_kernel(tc, qT, kT, vT, doT, rw, qm, offs, out):
             quantize(pair, slice(0, N), words[:].rearrange("p n j -> p (n j)"), E4)
             return pair
 
-        def deal(raw, name, shares):
-            halves = [tile([P, 2, P, PACK], BF16, f"{name}_dealt{u}") for u in range(2)]
+        def deal_into(halves, raw, shares):
             for copy, u, s0, s1 in shares:
                 copy(
                     halves[u][:, :, s0:s1, :].rearrange("p t s j -> p s j t"),
                     raw.rearrange("p j (s t) -> p s j t", t=PACK)[:, s0:s1, :, 2 * u : 2 * u + 2],
                 )
+
+        def deal(raw, name, shares):
+            halves = [tile([P, 2, P, PACK], BF16, f"{name}_dealt{u}") for u in range(2)]
+            deal_into(halves, raw, shares)
             return halves
 
         def deal_quantize(halves, name, fmt):
@@ -118,8 +126,8 @@ def tile_attend_gat_k_kernel(tc, qT, kT, vT, doT, rw, qm, offs, out):
                 src.rearrange("p j (c i) -> p c j i", i=4),
             )
 
-        def scores(q_mx, k_mx, c):
-            bank = ps.tile([P, PACK, P], F32, name="score", bufs=3)
+        def scores(q_mx, k_mx, g, c):
+            bank = ps.tile([P, PACK, P], F32, name=f"score{(g * PACK + c) % SCORE_BANKS}", bufs=1)
             for t in range(PACK):
                 mm(bank[:, t, :], q_mx, block(t), E4, k_mx, block(c), E4)
             return bank
@@ -134,81 +142,97 @@ def tile_attend_gat_k_kernel(tc, qT, kT, vT, doT, rw, qm, offs, out):
                 op1=ALU.mult,
             )
 
-        both = ((nc.vector.tensor_copy, 0, 0, P), (nc.scalar.copy, 1, 0, P))
+        on_scalar = ((nc.scalar.copy, 0, 0, P), (nc.scalar.copy, 1, 0, P))
         q0_shares = ((nc.scalar.copy, 1, 0, SPLIT), (nc.vector.tensor_copy, 0, 0, P), (nc.vector.tensor_copy, 1, SPLIT, P))
 
-        v_mx = gather(v_planes, "v")
+        ds1_mx = mx_pair("ds1", N)
+        nc.vector.memset(ds1_mx[0][:, N // 2 : N], 0)
+        nc.vector.memset(ds1_mx[1][:, N // 2 : N], 0)
         gate2 = tile([P, 2, PACK], F32, "gate2")
         nc.vector.tensor_scalar(gate2[:], gate[:], 2.0, None, ALU.mult)
-        dp = []
-        for g in range(2):
-            dealt = deal(do_raw[:, :, g * PASS : (g + 1) * PASS], f"do{g}", both)
-            do_mx = deal_quantize(dealt, f"do{g}", E5)
-            dp.append(dp_rows(do_mx, v_mx, g))
-        woven = {}
+        v_mx = gather(v_planes, "v")
+        both = ((nc.vector.tensor_copy, 0, 0, P), (nc.scalar.copy, 1, 0, P))
+        do_dealt = [deal(do_raw[:, :, g * PASS : (g + 1) * PASS], f"do{g}", both) for g in range(2)]
+        do_mx = [deal_quantize(do_dealt[g], f"do{g}", E5) for g in range(2)]
+        dp = [dp_rows(do_mx[g], v_mx, g) for g in range(2)]
 
-        def dp_weave(quarters, host):
-            held = tile([P, len(quarters), P, PACK], F32, host)
-            for i, (g, c) in enumerate(quarters):
-                woven[g, c] = held[:, i, :, :]
-                copy = nc.vector.tensor_copy if (g, c) == (0, PACK - 1) else nc.scalar.copy
+        k_rows = tile([P, PACK - 1, N], BF16, "k_rows")
+        k_words = tile([P, N, PACK], BF16, "k_words")
+        for j in range(PACK - 1):
+            nc.vector.tensor_copy(k_rows[:, j, :], k_planes[j][:].indirect(offsets[:]))
+        weave(nc.vector.tensor_copy, k_words[:, :, 0 : PACK - 1], k_rows[:])
+        nc.vector.tensor_copy(k_words[:, :, PACK - 1], k_planes[PACK - 1][:].indirect(offsets[:]))
+        k_mx = mx_pair("k", N)
+        quantize(k_mx, slice(0, N), k_words[:].rearrange("p n j -> p (n j)"), E4)
+        q0_dealt = deal(q0_raw[:], "q0", q0_shares)
+        q1_dealt = deal(q1_raw[:], "q1", on_scalar)
+
+        woven = {}
+        for g in range(2):
+            for c in range(PACK):
+                woven[g, c] = tile([P, P, PACK], F32, f"woven{g}{c}")[:]
+                copy = nc.vector.tensor_copy if g == 0 and c < VECTOR_WEAVES else nc.scalar.copy
                 weave(copy, woven[g, c], dp[g][:, :, block(c)])
 
-        quarters = [(g, c) for g in range(2) for c in range(PACK)]
-        dp_weave(quarters[:5], "do")
-
-        k_mx = gather(k_planes, "k")
-        q0_dealt = deal(q0_raw[:], "q0", q0_shares)
-        dp_weave(quarters[5:6], "q0")
-        q1_dealt = deal(q1_raw[:], "q1", ((nc.scalar.copy, 0, 0, P), (nc.scalar.copy, 1, 0, P)))
-        dp_weave(quarters[6:], "q1")
-
         q_mx = deal_quantize(q0_dealt, "q0", E4)
-        score = [scores(q_mx, k_mx, c) for c in range(PACK)]
-        ds_mx = [mx_pair(f"ds{g}", N) for g in range(2)]
+        score = [scores(q_mx, k_mx, 0, c) for c in range(PACK)]
         ds0 = tile([P, N, PACK], BF16, "ds0")
         for c in range(PACK):
             ds_words(ds0[:, block(c), :], score[c], 0, c)
         q_mx = deal_quantize(q1_dealt, "q1", E4)
-        score = [scores(q_mx, k_mx, c) for c in range(PACK)]
-        quantize(ds_mx[0], slice(0, N), ds0[:].rearrange("p n t -> p (n t)"), E5)
-
-        qm_scales = tile([P, 2, D], U8, "qm_scales")
-        first_codes = tile([P, 2, P], U32, "qm_first_codes")
-        qm_mx = {(g, 0): (first_codes[:, g, :], qm_scales[:, g, block(0)]) for g in range(2)}
+        score = [scores(q_mx, k_mx, 1, c) for c in range(PACK)]
         qm_words = {}
-        for j in range(D // P):
-            for g, raw in enumerate((qm0_raw[:, :, block(j)], qm1_raw[j // 2][:, :, block(j % 2)])):
-                if g == 0 and j == 1:
-                    held = tile([P, D // P - 1, P, PACK], BF16, "q1_dealt0")
-                if g == 0 and j > 0:
-                    qm_words[g, j] = held[:, j - 1, :, :]
-                else:
-                    qm_words[g, j] = tile([P, P, PACK], BF16, f"qm_words{g}{j}")[:]
-                weave(nc.scalar.copy, qm_words[g, j], raw)
+        qm_mx = {}
 
-        def qm_quantize(j):
+        def qm_weave(j, g):
+            raw = qm0_raw[:, :, block(j)] if g == 0 else qm1_raw[j // 2][:, :, block(j % 2)]
+            weave(nc.scalar.copy, qm_words[j][:, g, :, :], raw)
+
+        def qm_quantize(j, g0, g1, host):
+            pair = (tile([P, (g1 - g0) * P], U32, host), tile([P, (g1 - g0) * P], U8, f"qm_scales{j}{g0}"))
+            quantize(pair, slice(0, (g1 - g0) * P), qm_words[j][:, g0:g1, :, :].rearrange("p g d j -> p (g d j)"), E4)
+            for g in range(g0, g1):
+                qm_mx[j, g] = (pair[0][:, block(g - g0)], pair[1][:, block(g - g0)])
+
+        def dk_columns(j, cols, bank_name, name):
+            bank = ps.tile([P, N], F32, name=bank_name, bufs=1)
             for g in range(2):
-                quantize(qm_mx[g, j], block(0), qm_words[g, j].rearrange("p d j -> p (d j)"), E4)
+                mm(bank[:], qm_mx[j, g], slice(0, P), E4, ds_mx[g], slice(0, N), E5, start=g == 0, stop=g == 1)
+            dk = tile([P, cols.stop - cols.start], F32, name)
+            nc.scalar.copy(dk[:], bank[:, cols])
+            return dk
 
+        def scatter(j, cols, dk):
+            nc.vector.tensor_copy(windows[j][:].indirect(offsets[:, cols.start // 16 : cols.stop // 16]), dk[:])
+
+        for j in range(D // P):
+            qm_words[j] = tile([P, 2, P, PACK], BF16, f"qm_words{j}")
+        for j, g in ((0, 0), (1, 0), (0, 1), (1, 1), (2, 0), (2, 1)):
+            qm_weave(j, g)
+        ds_mx = [(tile([P, N], U32, "q1_dealt1"), tile([P, N], U8, "ds0_scales")), ds1_mx]
+        quantize(ds_mx[0], slice(0, N), ds0[:].rearrange("p n t -> p (n t)"), E5)
+        qm_quantize(0, 0, 1, "qm_codes00")
+
+        low, high = slice(0, N // 2), slice(N // 2, N)
         ds1 = tile([P, N, PACK], BF16, "ds1")
-
-        for c in range(PACK):
+        for c in (0, 1):
             ds_words(ds1[:, block(c), :], score[c], 1, c)
-        qm_quantize(0)
-        quantize(ds_mx[1], slice(0, N), ds1[:].rearrange("p n t -> p (n t)"), E5)
-        later_codes = tile([P, 2, D // P - 1, P], U32, "ds1")
+        qm_quantize(0, 1, 2, "woven10")
+        quantize(ds1_mx, low, ds1[:, low, :].rearrange("p n t -> p (n t)"), E5)
+        dk_low = dk_columns(0, low, "dk_bank", "dk_low")
+        qm_weave(3, 0)
+        qm_weave(3, 1)
+        for c in (2, 3):
+            ds_words(ds1[:, block(c), :], score[c], 1, c)
+        qm_quantize(1, 0, 2, "woven12")
+        quantize(ds1_mx, high, ds1[:, high, :].rearrange("p n t -> p (n t)"), E5)
+        dk_high = dk_columns(0, high, "score0", "dk_high")
+        scatter(0, low, dk_low)
+        qm_quantize(2, 0, 2, "qm_codes2")
+        scatter(0, high, dk_high)
+        nc.sync.dma_start(out=out[block(0), :], in_=windows[0][:])
         for j in range(1, D // P):
-            for g in range(2):
-                qm_mx[g, j] = (later_codes[:, g, j - 1, :], qm_scales[:, g, block(j)])
-
-        for j in range(D // P):
-            if j > 0:
-                qm_quantize(j)
-            bank = ps.tile([P, N], F32, name="dk_bank", bufs=1)
-            for g in range(2):
-                mm(bank[:], qm_mx[g, j], block(0), E4, ds_mx[g], slice(0, N), E5, start=g == 0, stop=g == 1)
-            dk = tile([P, N], F32, f"dk{j}")
-            nc.scalar.copy(dk[:], bank[:])
-            nc.vector.tensor_copy(windows[j][:].indirect(offsets[:]), dk[:])
+            if j == D // P - 1:
+                qm_quantize(j, 0, 2, "qm_codes3")
+            scatter(j, slice(0, N), dk_columns(j, slice(0, N), ("score1", "dk_bank", "score2")[j - 1], f"k{j}"))
             nc.sync.dma_start(out=out[block(j), :], in_=windows[j][:])

@@ -19,8 +19,9 @@ P = 128
 PACK = 4
 PASS = P * PACK
 SPLIT = 96
-VECTOR_WEAVES = 3
+VECTOR_WEAVES = 2
 SCORE_BANKS = 3
+WARM_UPS = 3
 
 
 def tile_attend_gat_k_kernel(tc, qT, kT, vT, doT, rw, qm, offs, out):
@@ -44,12 +45,13 @@ def tile_attend_gat_k_kernel(tc, qT, kT, vT, doT, rw, qm, offs, out):
             nc.sync.dma_start(out=raw[:], in_=rows[:, :, r0 : r0 + width])
             return raw
 
-        v_planes = load_planes(vT, "v", 0, 2)
+        v_planes = load_planes(vT, "v", 0, 1)
         offsets = lists.tile([P, N // 16], U16, name="offsets")
         nc.sync.dma_start(offsets[:], offs)
         gate = tile([P, 2, PACK], F32, "gate")
         nc.sync.dma_start(out=gate[:], in_=rw[0].rearrange("(g s t) o -> s g (t o)", g=2, t=PACK))
-        v_planes.extend(load_planes(vT, "v", 2, 2))
+        for j in range(1, PACK):
+            v_planes.extend(load_planes(vT, "v", j, 1))
         do_raw = load_columns(doT[0], 0, R, "do")
         k_planes = []
         for j in range(PACK):
@@ -58,7 +60,7 @@ def tile_attend_gat_k_kernel(tc, qT, kT, vT, doT, rw, qm, offs, out):
         q0_raw = load_columns(qT[0], 0, PASS, "q0")
         q1_raw = load_columns(qT[0], PASS, PASS, "q1")
         qm0_raw = load_columns(qm[0, 0:PASS, :], 0, D, "v0")
-        qm1_raw = [load_columns(qm[0, PASS:R, :], h * (D // 2), D // 2, ("v2", "qm1b")[h]) for h in range(2)]
+        qm1_raw = [load_columns(qm[0, PASS:R, :], h * (D // 2), D // 2, f"v{1 + h}") for h in range(2)]
 
         windows = []
         for j in range(D // P):
@@ -142,6 +144,11 @@ def tile_attend_gat_k_kernel(tc, qT, kT, vT, doT, rw, qm, offs, out):
                 op1=ALU.mult,
             )
 
+        low, high = slice(0, N // 2), slice(N // 2, N)
+
+        def listed(cols):
+            return offsets[:, cols.start // 16 : cols.stop // 16]
+
         on_scalar = ((nc.scalar.copy, 0, 0, P), (nc.scalar.copy, 1, 0, P))
         q0_shares = ((nc.scalar.copy, 1, 0, SPLIT), (nc.vector.tensor_copy, 0, 0, P), (nc.vector.tensor_copy, 1, SPLIT, P))
 
@@ -161,9 +168,14 @@ def tile_attend_gat_k_kernel(tc, qT, kT, vT, doT, rw, qm, offs, out):
         for j in range(PACK - 1):
             nc.vector.tensor_copy(k_rows[:, j, :], k_planes[j][:].indirect(offsets[:]))
         weave(nc.vector.tensor_copy, k_words[:, :, 0 : PACK - 1], k_rows[:])
-        nc.vector.tensor_copy(k_words[:, :, PACK - 1], k_planes[PACK - 1][:].indirect(offsets[:]))
         k_mx = mx_pair("k", N)
-        quantize(k_mx, slice(0, N), k_words[:].rearrange("p n j -> p (n j)"), E4)
+        for cols in (low, high):
+            nc.vector.tensor_copy(k_words[:, cols, PACK - 1], k_planes[PACK - 1][:].indirect(listed(cols)))
+        for cols in (low, high):
+            quantize(k_mx, cols, k_words[:, cols, :].rearrange("p n j -> p (n j)"), E4)
+        warm = ps.tile([P, N], F32, name="dk_bank", bufs=1)
+        for i in range(WARM_UPS):
+            mm(warm[:], k_mx, block(0), E4, v_mx, slice(0, N), E4)
         q0_dealt = deal(q0_raw[:], "q0", q0_shares)
         q1_dealt = deal(q1_raw[:], "q1", on_scalar)
 
@@ -203,7 +215,7 @@ def tile_attend_gat_k_kernel(tc, qT, kT, vT, doT, rw, qm, offs, out):
             return dk
 
         def scatter(j, cols, dk):
-            nc.vector.tensor_copy(windows[j][:].indirect(offsets[:, cols.start // 16 : cols.stop // 16]), dk[:])
+            nc.vector.tensor_copy(windows[j][:].indirect(listed(cols)), dk[:])
 
         for j in range(D // P):
             qm_words[j] = tile([P, 2, P, PACK], BF16, f"qm_words{j}")
@@ -213,7 +225,6 @@ def tile_attend_gat_k_kernel(tc, qT, kT, vT, doT, rw, qm, offs, out):
         quantize(ds_mx[0], slice(0, N), ds0[:].rearrange("p n t -> p (n t)"), E5)
         qm_quantize(0, 0, 1, "qm_codes00")
 
-        low, high = slice(0, N // 2), slice(N // 2, N)
         ds1 = tile([P, N, PACK], BF16, "ds1")
         for c in (0, 1):
             ds_words(ds1[:, block(c), :], score[c], 1, c)
@@ -235,4 +246,8 @@ def tile_attend_gat_k_kernel(tc, qT, kT, vT, doT, rw, qm, offs, out):
             if j == D // P - 1:
                 qm_quantize(j, 0, 2, "qm_codes3")
             scatter(j, slice(0, N), dk_columns(j, slice(0, N), ("score1", "dk_bank", "score2")[j - 1], f"k{j}"))
-            nc.sync.dma_start(out=out[block(j), :], in_=windows[j][:])
+            if j < D // P - 1:
+                nc.sync.dma_start(out=out[block(j), :], in_=windows[j][:])
+            else:
+                nc.sync.dma_start(out=out[block(j), 0 : T // 2], in_=windows[j][:, 0 : T // 2])
+                nc.scalar.dma_start(out=out[block(j), T // 2 : T], in_=windows[j][:, T // 2 : T])

@@ -19,9 +19,10 @@ P = 128
 PACK = 4
 PASS = P * PACK
 SPLIT = 96
-VECTOR_WEAVES = 2
+VECTOR_WEAVES = 1
+LATE_WEAVES = 2
 SCORE_BANKS = 3
-WARM_UPS = 3
+WARM_UPS = 2
 
 
 def tile_attend_gat_k_kernel(tc, qT, kT, vT, doT, rw, qm, offs, out):
@@ -45,12 +46,12 @@ def tile_attend_gat_k_kernel(tc, qT, kT, vT, doT, rw, qm, offs, out):
             nc.sync.dma_start(out=raw[:], in_=rows[:, :, r0 : r0 + width])
             return raw
 
-        v_planes = load_planes(vT, "v", 0, 1)
+        v_planes = load_planes(vT, "v", 0, 2)
         offsets = lists.tile([P, N // 16], U16, name="offsets")
         nc.sync.dma_start(offsets[:], offs)
         gate = tile([P, 2, PACK], F32, "gate")
         nc.sync.dma_start(out=gate[:], in_=rw[0].rearrange("(g s t) o -> s g (t o)", g=2, t=PACK))
-        for j in range(1, PACK):
+        for j in range(2, PACK):
             v_planes.extend(load_planes(vT, "v", j, 1))
         do_raw = load_columns(doT[0], 0, R, "do")
         k_planes = []
@@ -60,7 +61,7 @@ def tile_attend_gat_k_kernel(tc, qT, kT, vT, doT, rw, qm, offs, out):
         q0_raw = load_columns(qT[0], 0, PASS, "q0")
         q1_raw = load_columns(qT[0], PASS, PASS, "q1")
         qm0_raw = load_columns(qm[0, 0:PASS, :], 0, D, "v0")
-        qm1_raw = [load_columns(qm[0, PASS:R, :], h * (D // 2), D // 2, f"v{1 + h}") for h in range(2)]
+        qm1_raw = [load_columns(qm[0, PASS:R, :], h * (D // 2), D // 2, f"v{2 + h}") for h in range(2)]
 
         windows = []
         for j in range(D // P):
@@ -131,7 +132,7 @@ def tile_attend_gat_k_kernel(tc, qT, kT, vT, doT, rw, qm, offs, out):
         def scores(q_mx, k_mx, g, c):
             bank = ps.tile([P, PACK, P], F32, name=f"score{(g * PACK + c) % SCORE_BANKS}", bufs=1)
             for t in range(PACK):
-                mm(bank[:, t, :], q_mx, block(t), E4, k_mx, block(c), E4)
+                mm(bank[:, t, :], q_mx, block(t), E4, k_mx[c // 2], block(c % 2), E4)
             return bank
 
         def ds_words(words, bank, g, c):
@@ -168,25 +169,30 @@ def tile_attend_gat_k_kernel(tc, qT, kT, vT, doT, rw, qm, offs, out):
         for j in range(PACK - 1):
             nc.vector.tensor_copy(k_rows[:, j, :], k_planes[j][:].indirect(offsets[:]))
         weave(nc.vector.tensor_copy, k_words[:, :, 0 : PACK - 1], k_rows[:])
-        k_mx = mx_pair("k", N)
         for cols in (low, high):
             nc.vector.tensor_copy(k_words[:, cols, PACK - 1], k_planes[PACK - 1][:].indirect(listed(cols)))
-        for cols in (low, high):
-            quantize(k_mx, cols, k_words[:, cols, :].rearrange("p n j -> p (n j)"), E4)
+        k_mx = [mx_pair("k_low", N // 2)]
+        quantize(k_mx[0], low, k_words[:, low, :].rearrange("p n j -> p (n j)"), E4)
         warm = ps.tile([P, N], F32, name="dk_bank", bufs=1)
         for i in range(WARM_UPS):
-            mm(warm[:], k_mx, block(0), E4, v_mx, slice(0, N), E4)
+            mm(warm[:], k_mx[0], block(0), E4, v_mx, slice(0, N), E4)
         q0_dealt = deal(q0_raw[:], "q0", q0_shares)
         q1_dealt = deal(q1_raw[:], "q1", on_scalar)
 
         woven = {}
+        late = tile([P, LATE_WEAVES, P, PACK], F32, "q0")
         for g in range(2):
             for c in range(PACK):
-                woven[g, c] = tile([P, P, PACK], F32, f"woven{g}{c}")[:]
+                if g == 1 and c >= PACK - LATE_WEAVES:
+                    woven[g, c] = late[:, c - (PACK - LATE_WEAVES), :, :]
+                else:
+                    woven[g, c] = tile([P, P, PACK], F32, f"woven{g}{c}")[:]
                 copy = nc.vector.tensor_copy if g == 0 and c < VECTOR_WEAVES else nc.scalar.copy
                 weave(copy, woven[g, c], dp[g][:, :, block(c)])
 
         q_mx = deal_quantize(q0_dealt, "q0", E4)
+        k_mx.append((tile([P, N // 2], U32, "q0_dealt1"), tile([P, N // 2], U8, "k_high_scales")))
+        quantize(k_mx[1], low, k_words[:, high, :].rearrange("p n j -> p (n j)"), E4)
         score = [scores(q_mx, k_mx, 0, c) for c in range(PACK)]
         ds0 = tile([P, N, PACK], BF16, "ds0")
         for c in range(PACK):
@@ -235,7 +241,7 @@ def tile_attend_gat_k_kernel(tc, qT, kT, vT, doT, rw, qm, offs, out):
         qm_weave(3, 1)
         for c in (2, 3):
             ds_words(ds1[:, block(c), :], score[c], 1, c)
-        qm_quantize(1, 0, 2, "woven12")
+        qm_quantize(1, 0, 2, "woven11")
         quantize(ds1_mx, high, ds1[:, high, :].rearrange("p n t -> p (n t)"), E5)
         dk_high = dk_columns(0, high, "score0", "dk_high")
         scatter(0, low, dk_low)

@@ -19,9 +19,10 @@ P = 128
 PACK = 4
 PASS = P * PACK
 SPLIT = 96
-VECTOR_WEAVES = 1
-LATE_WEAVES = 2
+VECTOR_WEAVES = 2
 SCORE_BANKS = 3
+EARLY_QM = ((0, 0), (0, 1), (1, 0), (1, 1), (2, 0))
+LATE_QM = ((2, 1), (3, 0), (3, 1))
 WARM_UPS = 2
 
 
@@ -59,9 +60,12 @@ def tile_attend_gat_k_kernel(tc, qT, kT, vT, doT, rw, qm, offs, out):
             k_planes.append(tile([P, T], F32, f"k{j}"))
             nc.sync.dma_start(out=k_planes[j][:], in_=kT.rearrange("(p j) t -> p j t", j=PACK)[:, j, :])
         q0_raw = load_columns(qT[0], 0, PASS, "q0")
-        q1_raw = load_columns(qT[0], PASS, PASS, "q1")
-        qm0_raw = load_columns(qm[0, 0:PASS, :], 0, D, "v0")
-        qm1_raw = [load_columns(qm[0, PASS:R, :], h * (D // 2), D // 2, f"v{2 + h}") for h in range(2)]
+        q1_raw = [load_columns(qT[0], PASS + h * (PASS // 2), PASS // 2, f"q1{h}") for h in range(2)]
+        qm_raw = {}
+        for h in range(2):
+            for g in range(2):
+                rows = qm[0, g * PASS : (g + 1) * PASS, :]
+                qm_raw[h, g] = load_columns(rows, h * (D // 2), D // 2, ("v0", "v2", "v3", "do")[2 * h + g])
 
         windows = []
         for j in range(D // P):
@@ -150,7 +154,6 @@ def tile_attend_gat_k_kernel(tc, qT, kT, vT, doT, rw, qm, offs, out):
         def listed(cols):
             return offsets[:, cols.start // 16 : cols.stop // 16]
 
-        on_scalar = ((nc.scalar.copy, 0, 0, P), (nc.scalar.copy, 1, 0, P))
         q0_shares = ((nc.scalar.copy, 1, 0, SPLIT), (nc.vector.tensor_copy, 0, 0, P), (nc.vector.tensor_copy, 1, SPLIT, P))
 
         ds1_mx = mx_pair("ds1", N)
@@ -177,16 +180,18 @@ def tile_attend_gat_k_kernel(tc, qT, kT, vT, doT, rw, qm, offs, out):
         for i in range(WARM_UPS):
             mm(warm[:], k_mx[0], block(0), E4, v_mx, slice(0, N), E4)
         q0_dealt = deal(q0_raw[:], "q0", q0_shares)
-        q1_dealt = deal(q1_raw[:], "q1", on_scalar)
+        q1_dealt = tile([P, PACK, P, PACK], BF16, "q1_dealt")
+        for h in range(2):
+            for u in range(2):
+                nc.scalar.copy(
+                    q1_dealt[:, 2 * u : 2 * u + 2, h * (P // 2) : (h + 1) * (P // 2), :].rearrange("p t s j -> p s j t"),
+                    q1_raw[h][:].rearrange("p j (s t) -> p s j t", t=PACK)[:, :, :, 2 * u : 2 * u + 2],
+                )
 
         woven = {}
-        late = tile([P, LATE_WEAVES, P, PACK], F32, "q0")
         for g in range(2):
             for c in range(PACK):
-                if g == 1 and c >= PACK - LATE_WEAVES:
-                    woven[g, c] = late[:, c - (PACK - LATE_WEAVES), :, :]
-                else:
-                    woven[g, c] = tile([P, P, PACK], F32, f"woven{g}{c}")[:]
+                woven[g, c] = tile([P, P, PACK], F32, f"woven{g}{c}")[:]
                 copy = nc.vector.tensor_copy if g == 0 and c < VECTOR_WEAVES else nc.scalar.copy
                 weave(copy, woven[g, c], dp[g][:, :, block(c)])
 
@@ -197,20 +202,18 @@ def tile_attend_gat_k_kernel(tc, qT, kT, vT, doT, rw, qm, offs, out):
         ds0 = tile([P, N, PACK], BF16, "ds0")
         for c in range(PACK):
             ds_words(ds0[:, block(c), :], score[c], 0, c)
-        q_mx = deal_quantize(q1_dealt, "q1", E4)
+        q_mx = (tile([P, PASS], U32, "woven02"), tile([P, PASS], U8, "q1_scales"))
+        quantize(q_mx, slice(0, PASS), q1_dealt[:].rearrange("p t s j -> p (t s j)"), E4)
         score = [scores(q_mx, k_mx, 1, c) for c in range(PACK)]
         qm_words = {}
         qm_mx = {}
 
         def qm_weave(j, g):
-            raw = qm0_raw[:, :, block(j)] if g == 0 else qm1_raw[j // 2][:, :, block(j % 2)]
-            weave(nc.scalar.copy, qm_words[j][:, g, :, :], raw)
+            weave(nc.scalar.copy, qm_words[j, g], qm_raw[j // 2, g][:, :, block(j % 2)])
 
-        def qm_quantize(j, g0, g1, host):
-            pair = (tile([P, (g1 - g0) * P], U32, host), tile([P, (g1 - g0) * P], U8, f"qm_scales{j}{g0}"))
-            quantize(pair, slice(0, (g1 - g0) * P), qm_words[j][:, g0:g1, :, :].rearrange("p g d j -> p (g d j)"), E4)
-            for g in range(g0, g1):
-                qm_mx[j, g] = (pair[0][:, block(g - g0)], pair[1][:, block(g - g0)])
+        def qm_quantize(j, g, host):
+            qm_mx[j, g] = (tile([P, P], U32, host), tile([P, P], U8, f"qm_scales{j}{g}"))
+            quantize(qm_mx[j, g], slice(0, P), qm_words[j, g].rearrange("p d j -> p (d j)"), E4)
 
         def dk_columns(j, cols, bank_name, name):
             bank = ps.tile([P, N], F32, name=bank_name, bufs=1)
@@ -223,34 +226,38 @@ def tile_attend_gat_k_kernel(tc, qT, kT, vT, doT, rw, qm, offs, out):
         def scatter(j, cols, dk):
             nc.vector.tensor_copy(windows[j][:].indirect(listed(cols)), dk[:])
 
-        for j in range(D // P):
-            qm_words[j] = tile([P, 2, P, PACK], BF16, f"qm_words{j}")
-        for j, g in ((0, 0), (1, 0), (0, 1), (1, 1), (2, 0), (2, 1)):
+        for j, g in EARLY_QM:
+            qm_words[j, g] = tile([P, P, PACK], BF16, f"qm_words{j}{g}")[:]
+        for j, g in EARLY_QM:
             qm_weave(j, g)
-        ds_mx = [(tile([P, N], U32, "q1_dealt1"), tile([P, N], U8, "ds0_scales")), ds1_mx]
+        ds_mx = [(tile([P, N], U32, "q1_dealt"), tile([P, N], U8, "ds0_scales")), ds1_mx]
         quantize(ds_mx[0], slice(0, N), ds0[:].rearrange("p n t -> p (n t)"), E5)
-        qm_quantize(0, 0, 1, "qm_codes00")
+        qm_quantize(0, 0, "qm_codes00")
 
         ds1 = tile([P, N, PACK], BF16, "ds1")
         for c in (0, 1):
             ds_words(ds1[:, block(c), :], score[c], 1, c)
-        qm_quantize(0, 1, 2, "woven10")
+        qm_quantize(0, 1, "woven10")
         quantize(ds1_mx, low, ds1[:, low, :].rearrange("p n t -> p (n t)"), E5)
         dk_low = dk_columns(0, low, "dk_bank", "dk_low")
-        qm_weave(3, 0)
-        qm_weave(3, 1)
         for c in (2, 3):
             ds_words(ds1[:, block(c), :], score[c], 1, c)
-        qm_quantize(1, 0, 2, "woven11")
+        qm_quantize(1, 0, "woven12")
+        qm_quantize(1, 1, "qm_codes11")
         quantize(ds1_mx, high, ds1[:, high, :].rearrange("p n t -> p (n t)"), E5)
         dk_high = dk_columns(0, high, "score0", "dk_high")
+        later_words = tile([P, len(LATE_QM), P, PACK], BF16, "ds1")
+        for i, (j, g) in enumerate(LATE_QM):
+            qm_words[j, g] = later_words[:, i, :, :]
+            qm_weave(j, g)
         scatter(0, low, dk_low)
-        qm_quantize(2, 0, 2, "qm_codes2")
+        qm_quantize(2, 0, "qm_codes20")
         scatter(0, high, dk_high)
         nc.sync.dma_start(out=out[block(0), :], in_=windows[0][:])
         for j in range(1, D // P):
-            if j == D // P - 1:
-                qm_quantize(j, 0, 2, "qm_codes3")
+            for i, g in LATE_QM:
+                if i == j:
+                    qm_quantize(j, g, f"qm_codes{j}{g}")
             scatter(j, slice(0, N), dk_columns(j, slice(0, N), ("score1", "dk_bank", "score2")[j - 1], f"k{j}"))
             if j < D // P - 1:
                 nc.sync.dma_start(out=out[block(j), :], in_=windows[j][:])

@@ -18,8 +18,9 @@ COPY = mybir.ActivationFunctionType.Copy
 P = 128
 PACK = 4
 PASS = P * PACK
-SPLIT = 96
+SPLIT = 48
 VECTOR_WEAVES = 2
+LATE_WEAVES = 2
 SCORE_BANKS = 3
 EARLY_QM = ((0, 0), (0, 1), (1, 0), (1, 1), (2, 0))
 LATE_QM = ((2, 1), (3, 0), (3, 1))
@@ -51,7 +52,7 @@ def tile_attend_gat_k_kernel(tc, qT, kT, vT, doT, rw, qm, offs, out):
         offsets = lists.tile([P, N // 16], U16, name="offsets")
         nc.sync.dma_start(offsets[:], offs)
         gate = tile([P, 2, PACK], F32, "gate")
-        nc.sync.dma_start(out=gate[:], in_=rw[0].rearrange("(g s t) o -> s g (t o)", g=2, t=PACK))
+        nc.scalar.dma_start(out=gate[:], in_=rw[0].rearrange("(g s t) o -> s g (t o)", g=2, t=PACK))
         for j in range(2, PACK):
             v_planes.extend(load_planes(vT, "v", j, 1))
         do_raw = load_columns(doT[0], 0, R, "do")
@@ -59,8 +60,7 @@ def tile_attend_gat_k_kernel(tc, qT, kT, vT, doT, rw, qm, offs, out):
         for j in range(PACK):
             k_planes.append(tile([P, T], F32, f"k{j}"))
             nc.sync.dma_start(out=k_planes[j][:], in_=kT.rearrange("(p j) t -> p j t", j=PACK)[:, j, :])
-        q0_raw = load_columns(qT[0], 0, PASS, "q0")
-        q1_raw = [load_columns(qT[0], PASS + h * (PASS // 2), PASS // 2, f"q1{h}") for h in range(2)]
+        q_raw = [load_columns(qT[0], i * (PASS // 2), PASS // 2, f"q{i}") for i in range(4)]
         qm_raw = {}
         for h in range(2):
             for g in range(2):
@@ -154,7 +154,13 @@ def tile_attend_gat_k_kernel(tc, qT, kT, vT, doT, rw, qm, offs, out):
         def listed(cols):
             return offsets[:, cols.start // 16 : cols.stop // 16]
 
-        q0_shares = ((nc.scalar.copy, 1, 0, SPLIT), (nc.vector.tensor_copy, 0, 0, P), (nc.vector.tensor_copy, 1, SPLIT, P))
+        q0_shares = (
+            (nc.scalar.copy, 0, 0, 0, P // 2),
+            (nc.scalar.copy, 0, 1, 0, P // 2),
+            (nc.scalar.copy, 1, 1, 0, SPLIT),
+            (nc.vector.tensor_copy, 1, 0, 0, P // 2),
+            (nc.vector.tensor_copy, 1, 1, SPLIT, P // 2),
+        )
 
         ds1_mx = mx_pair("ds1", N)
         nc.vector.memset(ds1_mx[0][:, N // 2 : N], 0)
@@ -179,18 +185,23 @@ def tile_attend_gat_k_kernel(tc, qT, kT, vT, doT, rw, qm, offs, out):
         warm = ps.tile([P, N], F32, name="dk_bank", bufs=1)
         for i in range(WARM_UPS):
             mm(warm[:], k_mx[0], block(0), E4, v_mx, slice(0, N), E4)
-        q0_dealt = deal(q0_raw[:], "q0", q0_shares)
+        q0_dealt = [tile([P, 2, P, PACK], BF16, f"q0_dealt{u}") for u in range(2)]
+        for copy, h, u, s0, s1 in q0_shares:
+            copy(
+                q0_dealt[u][:, :, h * (P // 2) + s0 : h * (P // 2) + s1, :].rearrange("p t s j -> p s j t"),
+                q_raw[h][:].rearrange("p j (s t) -> p s j t", t=PACK)[:, s0:s1, :, 2 * u : 2 * u + 2],
+            )
         q1_dealt = tile([P, PACK, P, PACK], BF16, "q1_dealt")
         for h in range(2):
             for u in range(2):
                 nc.scalar.copy(
                     q1_dealt[:, 2 * u : 2 * u + 2, h * (P // 2) : (h + 1) * (P // 2), :].rearrange("p t s j -> p s j t"),
-                    q1_raw[h][:].rearrange("p j (s t) -> p s j t", t=PACK)[:, :, :, 2 * u : 2 * u + 2],
+                    q_raw[2 + h][:].rearrange("p j (s t) -> p s j t", t=PACK)[:, :, :, 2 * u : 2 * u + 2],
                 )
 
         woven = {}
         for g in range(2):
-            for c in range(PACK):
+            for c in range(PACK - g * LATE_WEAVES):
                 woven[g, c] = tile([P, P, PACK], F32, f"woven{g}{c}")[:]
                 copy = nc.vector.tensor_copy if g == 0 and c < VECTOR_WEAVES else nc.scalar.copy
                 weave(copy, woven[g, c], dp[g][:, :, block(c)])
@@ -228,7 +239,13 @@ def tile_attend_gat_k_kernel(tc, qT, kT, vT, doT, rw, qm, offs, out):
 
         for j, g in EARLY_QM:
             qm_words[j, g] = tile([P, P, PACK], BF16, f"qm_words{j}{g}")[:]
-        for j, g in EARLY_QM:
+        late = tile([P, LATE_WEAVES, P, PACK], F32, "q3")
+        for j, g in EARLY_QM[:2]:
+            qm_weave(j, g)
+        for i, c in enumerate(range(PACK - LATE_WEAVES, PACK)):
+            woven[1, c] = late[:, i, :, :]
+            weave(nc.scalar.copy, woven[1, c], dp[1][:, :, block(c)])
+        for j, g in EARLY_QM[2:]:
             qm_weave(j, g)
         ds_mx = [(tile([P, N], U32, "q1_dealt"), tile([P, N], U8, "ds0_scales")), ds1_mx]
         quantize(ds_mx[0], slice(0, N), ds0[:].rearrange("p n t -> p (n t)"), E5)
@@ -242,7 +259,7 @@ def tile_attend_gat_k_kernel(tc, qT, kT, vT, doT, rw, qm, offs, out):
         dk_low = dk_columns(0, low, "dk_bank", "dk_low")
         for c in (2, 3):
             ds_words(ds1[:, block(c), :], score[c], 1, c)
-        qm_quantize(1, 0, "woven12")
+        qm_quantize(1, 0, "woven11")
         qm_quantize(1, 1, "qm_codes11")
         quantize(ds1_mx, high, ds1[:, high, :].rearrange("p n t -> p (n t)"), E5)
         dk_high = dk_columns(0, high, "score0", "dk_high")

@@ -24,7 +24,6 @@ LATE_WEAVES = 2
 SCORE_BANKS = 3
 EARLY_QM = ((0, 0), (0, 1), (1, 0), (1, 1), (2, 0))
 LATE_QM = ((2, 1), (3, 0), (3, 1))
-WARM_UPS = 2
 
 
 def tile_attend_gat_k_kernel(tc, qT, kT, vT, doT, rw, qm, offs, out):
@@ -182,9 +181,6 @@ def tile_attend_gat_k_kernel(tc, qT, kT, vT, doT, rw, qm, offs, out):
             nc.vector.tensor_copy(k_words[:, cols, PACK - 1], k_planes[PACK - 1][:].indirect(listed(cols)))
         k_mx = [mx_pair("k_low", N // 2)]
         quantize(k_mx[0], low, k_words[:, low, :].rearrange("p n j -> p (n j)"), E4)
-        warm = ps.tile([P, N], F32, name="dk_bank", bufs=1)
-        for i in range(WARM_UPS):
-            mm(warm[:], k_mx[0], block(0), E4, v_mx, slice(0, N), E4)
         q0_dealt = [tile([P, 2, P, PACK], BF16, f"q0_dealt{u}") for u in range(2)]
         for copy, h, u, s0, s1 in q0_shares:
             copy(
@@ -206,7 +202,12 @@ def tile_attend_gat_k_kernel(tc, qT, kT, vT, doT, rw, qm, offs, out):
                 copy = nc.vector.tensor_copy if g == 0 and c < VECTOR_WEAVES else nc.scalar.copy
                 weave(copy, woven[g, c], dp[g][:, :, block(c)])
 
-        q_mx = deal_quantize(q0_dealt, "q0", E4)
+        q_mx = mx_pair("q0", PASS)
+        for h in range(2):
+            for t in range(PACK):
+                s0 = h * (P // 2)
+                words = q0_dealt[t // 2][:, t % 2, s0 : s0 + P // 2, :].rearrange("p s j -> p (s j)")
+                quantize(q_mx, slice(t * P + s0, t * P + s0 + P // 2), words, E4)
         k_mx.append((tile([P, N // 2], U32, "q0_dealt1"), tile([P, N // 2], U8, "k_high_scales")))
         quantize(k_mx[1], low, k_words[:, high, :].rearrange("p n j -> p (n j)"), E4)
         score = [scores(q_mx, k_mx, 0, c) for c in range(PACK)]

@@ -1,6 +1,7 @@
 from contextlib import ExitStack
 
 import concourse.mybir as mybir
+from concourse.masks import make_identity
 
 N, T, D, DV, R = 512, 2048, 512, 512, 1024
 FLOPS = 2 * R * N * (D + DV + D)
@@ -47,13 +48,15 @@ def tile_attend_gat_k_kernel(tc, qT, kT, vT, doT, rw, qm, offs, out):
             nc.sync.dma_start(out=raw[:], in_=rows[:, :, r0 : r0 + width])
             return raw
 
+        gate_rows = tile([P, PASS], F32, "gate_rows")
+        nc.gpsimd.memset(gate_rows[:], 0.0)
         v_planes = load_planes(vT, "v", 0, 2)
         offsets = lists.tile([P, N // 16], U16, name="offsets")
         nc.sync.dma_start(offsets[:], offs)
-        gate = tile([P, 2, PACK], F32, "gate")
-        nc.scalar.dma_start(out=gate[:], in_=rw[0].rearrange("(g s t) o -> s g (t o)", g=2, t=PACK))
-        for j in range(2, PACK):
-            v_planes.extend(load_planes(vT, "v", j, 1))
+        nc.sync.dma_start(out=gate_rows[0:2, :], in_=rw[0].rearrange("(g r) o -> g (r o)", g=2))
+        identity = tile([P, P], F32, "identity")
+        make_identity(nc, identity[:])
+        v_planes.extend(load_planes(vT, "v", 2, 2))
         do_raw = load_columns(doT[0], 0, R, "do")
         k_planes = []
         for j in range(PACK):
@@ -64,7 +67,7 @@ def tile_attend_gat_k_kernel(tc, qT, kT, vT, doT, rw, qm, offs, out):
         for h in range(2):
             for g in range(2):
                 rows = qm[0, g * PASS : (g + 1) * PASS, :]
-                qm_raw[h, g] = load_columns(rows, h * (D // 2), D // 2, ("v0", "v2", "v3", "do")[2 * h + g])
+                qm_raw[h, g] = load_columns(rows, h * (D // 2), D // 2, ("v0", "v2", "qm10", "do")[2 * h + g])
 
         windows = []
         for j in range(D // P):
@@ -165,7 +168,10 @@ def tile_attend_gat_k_kernel(tc, qT, kT, vT, doT, rw, qm, offs, out):
         nc.vector.memset(ds1_mx[0][:, N // 2 : N], 0)
         nc.vector.memset(ds1_mx[1][:, N // 2 : N], 0)
         gate2 = tile([P, 2, PACK], F32, "gate2")
-        nc.vector.tensor_scalar(gate2[:], gate[:], 2.0, None, ALU.mult)
+        turned = ps.tile([P, PACK, P], F32, name="dk_bank", bufs=1)
+        for t in range(PACK):
+            nc.tensor.transpose(turned[:, t, :], gate_rows[:, t:PASS:PACK], identity[:])
+        nc.vector.tensor_scalar(gate2[:], turned[:, :, 0:2].rearrange("p t g -> p g t"), 2.0, None, ALU.mult)
         v_mx = gather(v_planes, "v")
         both = ((nc.vector.tensor_copy, 0, 0, P), (nc.scalar.copy, 1, 0, P))
         do_dealt = [deal(do_raw[:, :, g * PASS : (g + 1) * PASS], f"do{g}", both) for g in range(2)]

@@ -20,9 +20,11 @@ P = 128
 PACK = 4
 PASS = P * PACK
 SPLIT = 48
+ASIDE = 40
 VECTOR_WEAVES = 2
 LATE_WEAVES = 2
 SCORE_BANKS = 3
+WARM_UPS = 2
 EARLY_QM = ((0, 0), (0, 1), (1, 0), (1, 1), (2, 0))
 LATE_QM = ((2, 1), (3, 0), (3, 1))
 
@@ -187,6 +189,9 @@ def tile_attend_gat_k_kernel(tc, qT, kT, vT, doT, rw, qm, offs, out):
             nc.vector.tensor_copy(k_words[:, cols, PACK - 1], k_planes[PACK - 1][:].indirect(listed(cols)))
         k_mx = [mx_pair("k_low", N // 2)]
         quantize(k_mx[0], low, k_words[:, low, :].rearrange("p n j -> p (n j)"), E4)
+        warm = ps.tile([P, N], F32, name="dk_bank", bufs=1)
+        for i in range(WARM_UPS):
+            mm(warm[:], k_mx[0], block(i % 2), E4, v_mx, slice(0, N), E4)
         q0_dealt = [tile([P, 2, P, PACK], BF16, f"q0_dealt{u}") for u in range(2)]
         for copy, h, u, s0, s1 in q0_shares:
             copy(
@@ -194,12 +199,23 @@ def tile_attend_gat_k_kernel(tc, qT, kT, vT, doT, rw, qm, offs, out):
                 q_raw[h][:].rearrange("p j (s t) -> p s j t", t=PACK)[:, s0:s1, :, 2 * u : 2 * u + 2],
             )
         q1_dealt = tile([P, PACK, P, PACK], BF16, "q1_dealt")
-        for h in range(2):
-            for u in range(2):
-                nc.scalar.copy(
-                    q1_dealt[:, 2 * u : 2 * u + 2, h * (P // 2) : (h + 1) * (P // 2), :].rearrange("p t s j -> p s j t"),
-                    q_raw[2 + h][:].rearrange("p j (s t) -> p s j t", t=PACK)[:, :, :, 2 * u : 2 * u + 2],
-                )
+
+        def round_aside(dst, src):
+            in_order = "p s j t -> p t s j"
+            nc.gpsimd.tensor_scalar(dst.rearrange(in_order), src.rearrange(in_order), 1.0, 0.0, ALU.mult, ALU.add)
+
+        q1_shares = (
+            (nc.scalar.copy, 0, 0, 0, P // 2),
+            (nc.scalar.copy, 0, 1, 0, P // 2),
+            (nc.scalar.copy, 1, 0, 0, P // 2),
+            (nc.scalar.copy, 1, 1, 0, P // 2 - ASIDE),
+            (round_aside, 1, 1, P // 2 - ASIDE, P // 2),
+        )
+        for copy, h, u, s0, s1 in q1_shares:
+            copy(
+                q1_dealt[:, 2 * u : 2 * u + 2, h * (P // 2) + s0 : h * (P // 2) + s1, :].rearrange("p t s j -> p s j t"),
+                q_raw[2 + h][:].rearrange("p j (s t) -> p s j t", t=PACK)[:, s0:s1, :, 2 * u : 2 * u + 2],
+            )
 
         woven = {}
         for g in range(2):
@@ -283,8 +299,4 @@ def tile_attend_gat_k_kernel(tc, qT, kT, vT, doT, rw, qm, offs, out):
                 if i == j:
                     qm_quantize(j, g, f"qm_codes{j}{g}")
             scatter(j, slice(0, N), dk_columns(j, slice(0, N), ("score1", "dk_bank", "score2")[j - 1], f"k{j}"))
-            if j < D // P - 1:
-                nc.sync.dma_start(out=out[block(j), :], in_=windows[j][:])
-            else:
-                nc.sync.dma_start(out=out[block(j), 0 : T // 2], in_=windows[j][:, 0 : T // 2])
-                nc.scalar.dma_start(out=out[block(j), T // 2 : T], in_=windows[j][:, T // 2 : T])
+            nc.sync.dma_start(out=out[block(j), :], in_=windows[j][:])

@@ -24,7 +24,7 @@ ASIDE = 40
 VECTOR_WEAVES = 2
 LATE_WEAVES = 2
 SCORE_BANKS = 3
-WARM_UPS = 2
+WARM_UPS = 3
 EARLY_QM = ((0, 0), (0, 1), (1, 0), (1, 1), (2, 0))
 LATE_QM = ((2, 1), (3, 0), (3, 1))
 
@@ -185,13 +185,16 @@ def tile_attend_gat_k_kernel(tc, qT, kT, vT, doT, rw, qm, offs, out):
         for j in range(PACK - 1):
             nc.vector.tensor_copy(k_rows[:, j, :], k_planes[j][:].indirect(offsets[:]))
         weave(nc.vector.tensor_copy, k_words[:, :, 0 : PACK - 1], k_rows[:])
+        warm = ps.tile([P, N], F32, name="dk_bank", bufs=1)
+        pairs = k_words[:, high, :].rearrange("p n j -> p (n j)").bitcast(F32)
+        nc.tensor.transpose(warm[:, 0:P], pairs[:, 0 : 2 * P : 2], identity[:])
+        for i in range(WARM_UPS):
+            mm(warm[:], v_mx, block(i), E4, v_mx, slice(0, N), E4)
         for cols in (low, high):
             nc.vector.tensor_copy(k_words[:, cols, PACK - 1], k_planes[PACK - 1][:].indirect(listed(cols)))
         k_mx = [mx_pair("k_low", N // 2)]
         quantize(k_mx[0], low, k_words[:, low, :].rearrange("p n j -> p (n j)"), E4)
-        warm = ps.tile([P, N], F32, name="dk_bank", bufs=1)
-        for i in range(WARM_UPS):
-            mm(warm[:], k_mx[0], block(i % 2), E4, v_mx, slice(0, N), E4)
+        mm(warm[:], k_mx[0], block(0), E4, v_mx, slice(0, N), E4)
         q0_dealt = [tile([P, 2, P, PACK], BF16, f"q0_dealt{u}") for u in range(2)]
         for copy, h, u, s0, s1 in q0_shares:
             copy(

@@ -34,6 +34,7 @@ def tile_attend_gat_k_kernel(tc, qT, kT, vT, doT, rw, qm, offs, out):
     with ExitStack() as ctx:
         lists = ctx.enter_context(tc.tile_pool(name="lists", bufs=1))
         sb = ctx.enter_context(tc.tile_pool(name="sb", bufs=1))
+        shared = ctx.enter_context(tc.tile_pool(name="shared", bufs=1))
         ps = ctx.enter_context(tc.psum_pool(name="ps", bufs=4))
 
         def tile(shape, dtype, name):
@@ -64,12 +65,17 @@ def tile_attend_gat_k_kernel(tc, qT, kT, vT, doT, rw, qm, offs, out):
         for j in range(PACK):
             k_planes.append(tile([P, T], F32, f"k{j}"))
             nc.sync.dma_start(out=k_planes[j][:], in_=kT.rearrange("(p j) t -> p j t", j=PACK)[:, j, :])
-        q_raw = [load_columns(qT[0], i * (PASS // 2), PASS // 2, f"q{i}") for i in range(4)]
+        q_raw = [load_columns(qT[0], i * (PASS // 2), PASS // 2, f"q{i}") for i in range(3)]
+        q_raw.append(shared.tile([P, PACK, PASS // 2], F32, name="q3", align_bytes=64, offset=0))
+        nc.sync.dma_start(out=q_raw[3][:], in_=qT[0].rearrange("(p j) r -> p j r", j=PACK)[:, :, R - PASS // 2 : R])
         qm_raw = {}
-        for h in range(2):
+        for j in range(2):
             for g in range(2):
-                rows = qm[0, g * PASS : (g + 1) * PASS, :]
-                qm_raw[h, g] = load_columns(rows, h * (D // 2), D // 2, ("v0", "v2", "qm10", "do")[2 * h + g])
+                qm_raw[j, g] = load_columns(qm[0, g * PASS : (g + 1) * PASS, :], j * P, P, f"qm{j}{g}")[:]
+        for g in range(2):
+            held = load_columns(qm[0, g * PASS : (g + 1) * PASS, :], D // 2, D // 2, ("v0", "v2")[g])
+            for j in range(2, 4):
+                qm_raw[j, g] = held[:, :, (j - 2) * P : (j - 1) * P]
 
         windows = []
         for j in range(D // P):
@@ -201,6 +207,8 @@ def tile_attend_gat_k_kernel(tc, qT, kT, vT, doT, rw, qm, offs, out):
                 q0_dealt[u][:, :, h * (P // 2) + s0 : h * (P // 2) + s1, :].rearrange("p t s j -> p s j t"),
                 q_raw[h][:].rearrange("p j (s t) -> p s j t", t=PACK)[:, s0:s1, :, 2 * u : 2 * u + 2],
             )
+        woven = {(1, 2): tile([P, P, PACK], F32, "q0")[:]}
+        weave(nc.scalar.copy, woven[1, 2], dp[1][:, :, block(2)])
         q1_dealt = tile([P, PACK, P, PACK], BF16, "q1_dealt")
 
         def round_aside(dst, src):
@@ -220,7 +228,6 @@ def tile_attend_gat_k_kernel(tc, qT, kT, vT, doT, rw, qm, offs, out):
                 q_raw[2 + h][:].rearrange("p j (s t) -> p s j t", t=PACK)[:, s0:s1, :, 2 * u : 2 * u + 2],
             )
 
-        woven = {}
         for g in range(2):
             for c in range(PACK - g * LATE_WEAVES):
                 woven[g, c] = tile([P, P, PACK], F32, f"woven{g}{c}")[:]
@@ -246,11 +253,17 @@ def tile_attend_gat_k_kernel(tc, qT, kT, vT, doT, rw, qm, offs, out):
         qm_mx = {}
 
         def qm_weave(j, g):
-            weave(nc.scalar.copy, qm_words[j, g], qm_raw[j // 2, g][:, :, block(j % 2)])
+            weave(nc.scalar.copy, qm_words[j, g], qm_raw[j, g])
 
         def qm_quantize(j, g, host):
             qm_mx[j, g] = (tile([P, P], U32, host), tile([P, P], U8, f"qm_scales{j}{g}"))
             quantize(qm_mx[j, g], slice(0, P), qm_words[j, g].rearrange("p d j -> p (d j)"), E4)
+
+        def qm_quantize_both(j, words, host):
+            codes, scales = tile([P, 2 * P], U32, host), tile([P, 2 * P], U8, f"qm_scales{j}")
+            quantize((codes, scales), slice(0, 2 * P), words.rearrange("p g d j -> p (g d j)"), E4)
+            for g in range(2):
+                qm_mx[j, g] = (codes[:, block(g)], scales[:, block(g)])
 
         def dk_columns(j, cols, bank_name, name):
             bank = ps.tile([P, N], F32, name=bank_name, bufs=1)
@@ -263,17 +276,15 @@ def tile_attend_gat_k_kernel(tc, qT, kT, vT, doT, rw, qm, offs, out):
         def scatter(j, cols, dk):
             nc.vector.tensor_copy(windows[j][:].indirect(listed(cols)), dk[:])
 
+        early_words = tile([P, len(EARLY_QM), P, PACK], BF16, "early_words")
         for j, g in EARLY_QM:
-            qm_words[j, g] = tile([P, P, PACK], BF16, f"qm_words{j}{g}")[:]
-        late = tile([P, LATE_WEAVES, P, PACK], F32, "q3")
-        for j, g in EARLY_QM[:2]:
+            qm_words[j, g] = early_words[:, 2 * j + g, :, :]
+        woven[1, 3] = shared.tile([P, P, PACK], F32, name="woven13", align_bytes=64, offset=0)[:]
+        weave(nc.scalar.copy, woven[1, 3], dp[1][:, :, block(3)])
+        for j, g in EARLY_QM:
             qm_weave(j, g)
-        for i, c in enumerate(range(PACK - LATE_WEAVES, PACK)):
-            woven[1, c] = late[:, i, :, :]
-            weave(nc.scalar.copy, woven[1, c], dp[1][:, :, block(c)])
-        for j, g in EARLY_QM[2:]:
-            qm_weave(j, g)
-        ds_mx = [(tile([P, N], U32, "q1_dealt"), tile([P, N], U8, "ds0_scales")), ds1_mx]
+        ds0_codes = shared.tile([P, N], U32, name="ds0_codes", align_bytes=64, offset=4 * PASS)
+        ds_mx = [(ds0_codes, tile([P, N], U8, "ds0_scales")), ds1_mx]
         quantize(ds_mx[0], slice(0, N), ds0[:].rearrange("p n t -> p (n t)"), E5)
         qm_quantize(0, 0, "qm_codes00")
 
@@ -285,8 +296,7 @@ def tile_attend_gat_k_kernel(tc, qT, kT, vT, doT, rw, qm, offs, out):
         dk_low = dk_columns(0, low, "dk_bank", "dk_low")
         for c in (2, 3):
             ds_words(ds1[:, block(c), :], score[c], 1, c)
-        qm_quantize(1, 0, "woven11")
-        qm_quantize(1, 1, "qm_codes11")
+        qm_quantize_both(1, early_words[:, 2:4], "woven11")
         quantize(ds1_mx, high, ds1[:, high, :].rearrange("p n t -> p (n t)"), E5)
         dk_high = dk_columns(0, high, "score0", "dk_high")
         later_words = tile([P, len(LATE_QM), P, PACK], BF16, "ds1")
@@ -298,8 +308,9 @@ def tile_attend_gat_k_kernel(tc, qT, kT, vT, doT, rw, qm, offs, out):
         scatter(0, high, dk_high)
         nc.sync.dma_start(out=out[block(0), :], in_=windows[0][:])
         for j in range(1, D // P):
-            for i, g in LATE_QM:
-                if i == j:
-                    qm_quantize(j, g, f"qm_codes{j}{g}")
+            if j == 2:
+                qm_quantize(2, 1, "qm_codes21")
+            if j == 3:
+                qm_quantize_both(3, later_words[:, 1:3], "qm_codes3")
             scatter(j, slice(0, N), dk_columns(j, slice(0, N), ("score1", "dk_bank", "score2")[j - 1], f"k{j}"))
             nc.sync.dma_start(out=out[block(j), :], in_=windows[j][:])

@@ -25,8 +25,6 @@ VECTOR_WEAVES = 2
 LATE_WEAVES = 2
 SCORE_BANKS = 3
 WARM_UPS = 3
-EARLY_QM = ((0, 0), (0, 1), (1, 0), (1, 1), (2, 0))
-LATE_QM = ((2, 1), (3, 0), (3, 1))
 
 
 def tile_attend_gat_k_kernel(tc, qT, kT, vT, doT, rw, qm, offs, out):
@@ -35,6 +33,7 @@ def tile_attend_gat_k_kernel(tc, qT, kT, vT, doT, rw, qm, offs, out):
         lists = ctx.enter_context(tc.tile_pool(name="lists", bufs=1))
         sb = ctx.enter_context(tc.tile_pool(name="sb", bufs=1))
         shared = ctx.enter_context(tc.tile_pool(name="shared", bufs=1))
+        late = ctx.enter_context(tc.tile_pool(name="late", bufs=1))
         ps = ctx.enter_context(tc.psum_pool(name="ps", bufs=4))
 
         def tile(shape, dtype, name):
@@ -65,17 +64,15 @@ def tile_attend_gat_k_kernel(tc, qT, kT, vT, doT, rw, qm, offs, out):
         for j in range(PACK):
             k_planes.append(tile([P, T], F32, f"k{j}"))
             nc.sync.dma_start(out=k_planes[j][:], in_=kT.rearrange("(p j) t -> p j t", j=PACK)[:, j, :])
-        q_raw = [load_columns(qT[0], i * (PASS // 2), PASS // 2, f"q{i}") for i in range(3)]
+        q_raw = [shared.tile([P, PACK, PASS // 2], F32, name="q0", align_bytes=64, offset=4096)]
+        nc.sync.dma_start(out=q_raw[0][:], in_=qT[0].rearrange("(p j) r -> p j r", j=PACK)[:, :, 0 : PASS // 2])
+        q_raw.extend(load_columns(qT[0], i * (PASS // 2), PASS // 2, f"q{i}") for i in (1, 2))
         q_raw.append(shared.tile([P, PACK, PASS // 2], F32, name="q3", align_bytes=64, offset=0))
         nc.sync.dma_start(out=q_raw[3][:], in_=qT[0].rearrange("(p j) r -> p j r", j=PACK)[:, :, R - PASS // 2 : R])
         qm_raw = {}
-        for j in range(2):
+        for j in range(D // P):
             for g in range(2):
-                qm_raw[j, g] = load_columns(qm[0, g * PASS : (g + 1) * PASS, :], j * P, P, f"qm{j}{g}")[:]
-        for g in range(2):
-            held = load_columns(qm[0, g * PASS : (g + 1) * PASS, :], D // 2, D // 2, ("v0", "v2")[g])
-            for j in range(2, 4):
-                qm_raw[j, g] = held[:, :, (j - 2) * P : (j - 1) * P]
+                qm_raw[j, g] = load_columns(qm[0, g * PASS : (g + 1) * PASS, :], j * P, P, f"qm{j}{g}" if j < 2 else ("v0", "v2", "k0", "k1")[2 * j + g - 4])[:]
 
         windows = []
         for j in range(D // P):
@@ -173,8 +170,6 @@ def tile_attend_gat_k_kernel(tc, qT, kT, vT, doT, rw, qm, offs, out):
         )
 
         ds1_mx = mx_pair("ds1", N)
-        nc.vector.memset(ds1_mx[0][:, N // 2 : N], 0)
-        nc.vector.memset(ds1_mx[1][:, N // 2 : N], 0)
         gate2 = tile([P, 2, PACK], F32, "gate2")
         turned = ps.tile([P, PACK, P], F32, name="dk_bank", bufs=1)
         for t in range(PACK):
@@ -207,7 +202,7 @@ def tile_attend_gat_k_kernel(tc, qT, kT, vT, doT, rw, qm, offs, out):
                 q0_dealt[u][:, :, h * (P // 2) + s0 : h * (P // 2) + s1, :].rearrange("p t s j -> p s j t"),
                 q_raw[h][:].rearrange("p j (s t) -> p s j t", t=PACK)[:, s0:s1, :, 2 * u : 2 * u + 2],
             )
-        woven = {(1, 2): tile([P, P, PACK], F32, "q0")[:]}
+        woven = {(1, 2): shared.tile([P, P, PACK], F32, name="woven12", align_bytes=64, offset=4096)[:]}
         weave(nc.scalar.copy, woven[1, 2], dp[1][:, :, block(2)])
         q1_dealt = tile([P, PACK, P, PACK], BF16, "q1_dealt")
 
@@ -252,65 +247,73 @@ def tile_attend_gat_k_kernel(tc, qT, kT, vT, doT, rw, qm, offs, out):
         qm_words = {}
         qm_mx = {}
 
-        def qm_weave(j, g):
-            weave(nc.scalar.copy, qm_words[j, g], qm_raw[j, g])
-
-        def qm_quantize(j, g, host):
-            qm_mx[j, g] = (tile([P, P], U32, host), tile([P, P], U8, f"qm_scales{j}{g}"))
-            quantize(qm_mx[j, g], slice(0, P), qm_words[j, g].rearrange("p d j -> p (d j)"), E4)
-
-        def qm_quantize_both(j, words, host):
-            codes, scales = tile([P, 2 * P], U32, host), tile([P, 2 * P], U8, f"qm_scales{j}")
+        def qm_quantize_both(j, words, codes):
+            scales = tile([P, 2 * P], U8, f"qm_scales{j}")
             quantize((codes, scales), slice(0, 2 * P), words.rearrange("p g d j -> p (g d j)"), E4)
             for g in range(2):
                 qm_mx[j, g] = (codes[:, block(g)], scales[:, block(g)])
 
-        def dk_columns(j, cols, bank_name, name):
-            bank = ps.tile([P, N], F32, name=bank_name, bufs=1)
+        def dk_columns(j, cols, bank_name, bufs, dk, copy):
+            width = cols.stop - cols.start
+            bank = ps.tile([P, width], F32, name=bank_name, bufs=bufs)
             for g in range(2):
-                mm(bank[:], qm_mx[j, g], slice(0, P), E4, ds_mx[g], slice(0, N), E5, start=g == 0, stop=g == 1)
-            dk = tile([P, cols.stop - cols.start], F32, name)
-            nc.scalar.copy(dk[:], bank[:, cols])
+                mm(bank[:], qm_mx[j, g], slice(0, P), E4, ds_mx[g], cols, E5, start=g == 0, stop=g == 1)
+            copy(dk[:], bank[:])
             return dk
 
-        def scatter(j, cols, dk):
-            nc.vector.tensor_copy(windows[j][:].indirect(listed(cols)), dk[:])
+        def scatter_low(j):
+            dk = dk_columns(j, low, "dp_bank", 4, tile([P, N // 2], F32, ("dk_low0", "do0_dealt0", "do0_dealt1", "do1_dealt0")[j]), nc.scalar.copy)
+            nc.scalar.activation(windows[j][:].indirect(listed(low)), dk[:], COPY)
 
-        early_words = tile([P, len(EARLY_QM), P, PACK], BF16, "early_words")
-        for j, g in EARLY_QM:
-            qm_words[j, g] = early_words[:, 2 * j + g, :, :]
+        for j in range(2):
+            qm_words[j] = late.tile([P, 2, P, PACK], BF16, name=f"qm_words{j}", align_bytes=64, offset=j * 2048)
         woven[1, 3] = shared.tile([P, P, PACK], F32, name="woven13", align_bytes=64, offset=0)[:]
         weave(nc.scalar.copy, woven[1, 3], dp[1][:, :, block(3)])
-        for j, g in EARLY_QM:
-            qm_weave(j, g)
+        for j in range(2):
+            for g in range(2):
+                weave(nc.scalar.copy, qm_words[j][:, g], qm_raw[j, g])
+        words20 = tile([P, P, PACK], BF16, "words20")
+        weave(nc.scalar.copy, words20[:], qm_raw[2, 0])
         ds0_codes = shared.tile([P, N], U32, name="ds0_codes", align_bytes=64, offset=4 * PASS)
         ds_mx = [(ds0_codes, tile([P, N], U8, "ds0_scales")), ds1_mx]
         quantize(ds_mx[0], slice(0, N), ds0[:].rearrange("p n t -> p (n t)"), E5)
-        qm_quantize(0, 0, "qm_codes00")
 
-        ds1 = tile([P, N, PACK], BF16, "ds1")
+        ds1_low = tile([P, N // 2, PACK], BF16, "ds1_low")
         for c in (0, 1):
-            ds_words(ds1[:, block(c), :], score[c], 1, c)
-        qm_quantize(0, 1, "woven10")
-        quantize(ds1_mx, low, ds1[:, low, :].rearrange("p n t -> p (n t)"), E5)
-        dk_low = dk_columns(0, low, "dk_bank", "dk_low")
+            ds_words(ds1_low[:, block(c), :], score[c], 1, c)
+        qm_quantize_both(0, qm_words[0][:], tile([P, 2 * P], U32, "woven10"))
+        quantize(ds1_mx, low, ds1_low[:].rearrange("p n t -> p (n t)"), E5)
+        scatter_low(0)
+        ds1_high = late.tile([P, N // 2, PACK], BF16, name="ds1_high", align_bytes=64, offset=0)
         for c in (2, 3):
-            ds_words(ds1[:, block(c), :], score[c], 1, c)
-        qm_quantize_both(1, early_words[:, 2:4], "woven11")
-        quantize(ds1_mx, high, ds1[:, high, :].rearrange("p n t -> p (n t)"), E5)
-        dk_high = dk_columns(0, high, "score0", "dk_high")
-        later_words = tile([P, len(LATE_QM), P, PACK], BF16, "ds1")
-        for i, (j, g) in enumerate(LATE_QM):
-            qm_words[j, g] = later_words[:, i, :, :]
-            qm_weave(j, g)
-        scatter(0, low, dk_low)
-        qm_quantize(2, 0, "qm_codes20")
-        scatter(0, high, dk_high)
-        nc.sync.dma_start(out=out[block(0), :], in_=windows[0][:])
-        for j in range(1, D // P):
-            if j == 2:
-                qm_quantize(2, 1, "qm_codes21")
-            if j == 3:
-                qm_quantize_both(3, later_words[:, 1:3], "qm_codes3")
-            scatter(j, slice(0, N), dk_columns(j, slice(0, N), ("score1", "dk_bank", "score2")[j - 1], f"k{j}"))
+            ds_words(ds1_high[:, block(c - 2), :], score[c], 1, c)
+        qm_quantize_both(1, qm_words[1][:], shared.tile([P, 2 * P], U32, name="codes1", align_bytes=64, offset=4096))
+        quantize(ds1_mx, high, ds1_high[:].rearrange("p n t -> p (n t)"), E5)
+        words21 = shared.tile([P, P, PACK], BF16, name="words21", align_bytes=64, offset=0)
+        weave(nc.vector.tensor_copy, words21[:], qm_raw[2, 1])
+        codes20 = shared.tile([P, P], U32, name="codes20", align_bytes=64, offset=4096 + 1024)
+        qm_mx[2, 0] = (codes20, tile([P, P], U8, "scales20"))
+        quantize(qm_mx[2, 0], slice(0, P), words20[:].rearrange("p d j -> p (d j)"), E4)
+        for j in range(D // P):
+            dk = tile([P, N // 2], F32, ("k2", "k1", "do1_dealt1", "dk_high3")[j])
+            copy = nc.scalar.copy if j > 1 else nc.vector.tensor_copy
+            dk_columns(j, high, ("dk_bank", "score0", "score1", "score2")[j], 1, dk, copy)
+            if j == 0:
+                qm_mx[2, 1] = mx_pair("qm21", P)
+                quantize(qm_mx[2, 1], slice(0, P), words21[:].rearrange("p d j -> p (d j)"), E4)
+                qm_words[3] = shared.tile([P, 2, P, PACK], BF16, name="qm_words3", align_bytes=64, offset=0)
+                for g in range(2):
+                    nc.gpsimd.tensor_scalar(
+                        qm_words[3][:, g].rearrange("p (c i) j -> p c i j", i=4),
+                        qm_raw[3, g].rearrange("p j (c i) -> p c i j", i=4),
+                        1.0,
+                        0.0,
+                        ALU.mult,
+                        ALU.add,
+                    )
+            if j == 1:
+                qm_quantize_both(3, qm_words[3][:], tile([P, 2 * P], U32, "qm_codes3"))
+            nc.vector.tensor_copy(windows[j][:].indirect(listed(high)), dk[:])
             nc.sync.dma_start(out=out[block(j), :], in_=windows[j][:])
+            if j + 1 < D // P:
+                scatter_low(j + 1)

@@ -70,9 +70,12 @@ def tile_attend_gat_k_kernel(tc, qT, kT, vT, doT, rw, qm, offs, out):
         q_raw.append(shared.tile([P, PACK, PASS // 2], F32, name="q3", align_bytes=64, offset=0))
         nc.sync.dma_start(out=q_raw[3][:], in_=qT[0].rearrange("(p j) r -> p j r", j=PACK)[:, :, R - PASS // 2 : R])
         qm_raw = {}
-        for j in range(D // P):
+        for u in range(2):
             for g in range(2):
-                qm_raw[j, g] = load_columns(qm[0, g * PASS : (g + 1) * PASS, :], j * P, P, f"qm{j}{g}" if j < 2 else ("v0", "v2", "k0", "k1")[2 * j + g - 4])[:]
+                name = (("qm0", "qm1"), ("v0", "v2"))[u][g]
+                held = load_columns(qm[0, g * PASS : (g + 1) * PASS, :], u * (D // 2), D // 2, name)
+                for i in range(2):
+                    qm_raw[2 * u + i, g] = held[:, :, i * P : (i + 1) * P]
 
         windows = []
         for j in range(D // P):
@@ -261,17 +264,18 @@ def tile_attend_gat_k_kernel(tc, qT, kT, vT, doT, rw, qm, offs, out):
             copy(dk[:], bank[:])
             return dk
 
-        def scatter_low(j):
+        def scatter_low(j, between=None):
             dk = dk_columns(j, low, "dp_bank", 4, tile([P, N // 2], F32, ("dk_low0", "do0_dealt0", "do0_dealt1", "do1_dealt0")[j]), nc.scalar.copy)
+            if between:
+                between()
             nc.scalar.activation(windows[j][:].indirect(listed(low)), dk[:], COPY)
 
         for j in range(2):
             qm_words[j] = late.tile([P, 2, P, PACK], BF16, name=f"qm_words{j}", align_bytes=64, offset=j * 2048)
         woven[1, 3] = shared.tile([P, P, PACK], F32, name="woven13", align_bytes=64, offset=0)[:]
         weave(nc.scalar.copy, woven[1, 3], dp[1][:, :, block(3)])
-        for j in range(2):
-            for g in range(2):
-                weave(nc.scalar.copy, qm_words[j][:, g], qm_raw[j, g])
+        for j, g in ((0, 0), (1, 0), (0, 1), (1, 1)):
+            weave(nc.scalar.copy, qm_words[j][:, g], qm_raw[j, g])
         words20 = tile([P, P, PACK], BF16, "words20")
         weave(nc.scalar.copy, words20[:], qm_raw[2, 0])
         ds0_codes = shared.tile([P, N], U32, name="ds0_codes", align_bytes=64, offset=4 * PASS)
@@ -284,6 +288,15 @@ def tile_attend_gat_k_kernel(tc, qT, kT, vT, doT, rw, qm, offs, out):
         qm_quantize_both(0, qm_words[0][:], tile([P, 2 * P], U32, "woven10"))
         quantize(ds1_mx, low, ds1_low[:].rearrange("p n t -> p (n t)"), E5)
         scatter_low(0)
+        words30 = tile([P, P, PACK], BF16, "ds1_low")
+        nc.gpsimd.tensor_scalar(
+            words30[:].rearrange("p (c i) j -> p c i j", i=4),
+            qm_raw[3, 0].rearrange("p j (c i) -> p c i j", i=4),
+            1.0,
+            0.0,
+            ALU.mult,
+            ALU.add,
+        )
         ds1_high = late.tile([P, N // 2, PACK], BF16, name="ds1_high", align_bytes=64, offset=0)
         for c in (2, 3):
             ds_words(ds1_high[:, block(c - 2), :], score[c], 1, c)
@@ -294,26 +307,24 @@ def tile_attend_gat_k_kernel(tc, qT, kT, vT, doT, rw, qm, offs, out):
         codes20 = shared.tile([P, P], U32, name="codes20", align_bytes=64, offset=4096 + 1024)
         qm_mx[2, 0] = (codes20, tile([P, P], U8, "scales20"))
         quantize(qm_mx[2, 0], slice(0, P), words20[:].rearrange("p d j -> p (d j)"), E4)
+        words31 = tile([P, P, PACK], BF16, "words20")
         for j in range(D // P):
-            dk = tile([P, N // 2], F32, ("k2", "k1", "do1_dealt1", "dk_high3")[j])
-            copy = nc.scalar.copy if j > 1 else nc.vector.tensor_copy
-            dk_columns(j, high, ("dk_bank", "score0", "score1", "score2")[j], 1, dk, copy)
+            if j < 2:
+                dk = shared.tile([P, N // 2], F32, name=f"dk_high{j}", align_bytes=64, offset=(1024, 0)[j])
+            else:
+                dk = tile([P, N // 2], F32, f"k{j}")
+            dk_columns(j, high, ("dk_bank", "score0", "score1", "score2")[j], 1, dk, nc.vector.tensor_copy)
             if j == 0:
                 qm_mx[2, 1] = mx_pair("qm21", P)
                 quantize(qm_mx[2, 1], slice(0, P), words21[:].rearrange("p d j -> p (d j)"), E4)
-                qm_words[3] = shared.tile([P, 2, P, PACK], BF16, name="qm_words3", align_bytes=64, offset=0)
-                for g in range(2):
-                    nc.gpsimd.tensor_scalar(
-                        qm_words[3][:, g].rearrange("p (c i) j -> p c i j", i=4),
-                        qm_raw[3, g].rearrange("p j (c i) -> p c i j", i=4),
-                        1.0,
-                        0.0,
-                        ALU.mult,
-                        ALU.add,
-                    )
             if j == 1:
-                qm_quantize_both(3, qm_words[3][:], tile([P, 2 * P], U32, "qm_codes3"))
+                for g, words in enumerate((words30, words31)):
+                    codes = shared.tile([P, P], U32, name=f"codes3{g}", align_bytes=64, offset=1024 + 512 * g)
+                    qm_mx[3, g] = (codes, tile([P, P], U8, f"scales3{g}"))
+                    quantize(qm_mx[3, g], slice(0, P), words[:].rearrange("p d j -> p (d j)"), E4)
             nc.vector.tensor_copy(windows[j][:].indirect(listed(high)), dk[:])
             nc.sync.dma_start(out=out[block(j), :], in_=windows[j][:])
-            if j + 1 < D // P:
+            if j == 0:
+                scatter_low(1, lambda: weave(nc.scalar.copy, words31[:], qm_raw[3, 1]))
+            elif j + 1 < D // P:
                 scatter_low(j + 1)

@@ -24,7 +24,7 @@ ASIDE = 40
 VECTOR_WEAVES = 2
 LATE_WEAVES = 2
 SCORE_BANKS = 3
-WARM_UPS = 3
+WARM_UPS = 2
 
 
 def tile_attend_gat_k_kernel(tc, qT, kT, vT, doT, rw, qm, offs, out):
@@ -189,16 +189,13 @@ def tile_attend_gat_k_kernel(tc, qT, kT, vT, doT, rw, qm, offs, out):
         for j in range(PACK - 1):
             nc.vector.tensor_copy(k_rows[:, j, :], k_planes[j][:].indirect(offsets[:]))
         weave(nc.vector.tensor_copy, k_words[:, :, 0 : PACK - 1], k_rows[:])
-        warm = ps.tile([P, N], F32, name="dk_bank", bufs=1)
-        pairs = k_words[:, high, :].rearrange("p n j -> p (n j)").bitcast(F32)
-        nc.tensor.transpose(warm[:, 0:P], pairs[:, 0 : 2 * P : 2], identity[:])
-        for i in range(WARM_UPS):
-            mm(warm[:], v_mx, block(i), E4, v_mx, slice(0, N), E4)
         for cols in (low, high):
             nc.vector.tensor_copy(k_words[:, cols, PACK - 1], k_planes[PACK - 1][:].indirect(listed(cols)))
         k_mx = [mx_pair("k_low", N // 2)]
         quantize(k_mx[0], low, k_words[:, low, :].rearrange("p n j -> p (n j)"), E4)
-        mm(warm[:], k_mx[0], block(0), E4, v_mx, slice(0, N), E4)
+        warm = ps.tile([P, N], F32, name="dk_bank", bufs=1)
+        for i in range(WARM_UPS):
+            mm(warm[:], k_mx[0], block(i), E4, v_mx, slice(0, N), E4)
         q0_dealt = [tile([P, 2, P, PACK], BF16, f"q0_dealt{u}") for u in range(2)]
         for copy, h, u, s0, s1 in q0_shares:
             copy(

@@ -70,12 +70,11 @@ def tile_attend_gat_k_kernel(tc, qT, kT, vT, doT, rw, qm, offs, out):
         q_raw.append(shared.tile([P, PACK, PASS // 2], F32, name="q3", align_bytes=64, offset=0))
         nc.sync.dma_start(out=q_raw[3][:], in_=qT[0].rearrange("(p j) r -> p j r", j=PACK)[:, :, R - PASS // 2 : R])
         qm_raw = {}
-        for u in range(2):
+        for j0, j1, names in ((0, 2, ("qm0", "qm1")), (2, 3, ("v0", "v2")), (3, 4, ("k0", "k1"))):
             for g in range(2):
-                name = (("qm0", "qm1"), ("v0", "v2"))[u][g]
-                held = load_columns(qm[0, g * PASS : (g + 1) * PASS, :], u * (D // 2), D // 2, name)
-                for i in range(2):
-                    qm_raw[2 * u + i, g] = held[:, :, i * P : (i + 1) * P]
+                held = load_columns(qm[0, g * PASS : (g + 1) * PASS, :], j0 * P, (j1 - j0) * P, names[g])
+                for j in range(j0, j1):
+                    qm_raw[j, g] = held[:, :, (j - j0) * P : (j - j0 + 1) * P]
 
         windows = []
         for j in range(D // P):
@@ -141,6 +140,16 @@ def tile_attend_gat_k_kernel(tc, qT, kT, vT, doT, rw, qm, offs, out):
             copy(
                 dst.rearrange("p (c i) j -> p c j i", i=4),
                 src.rearrange("p j (c i) -> p c j i", i=4),
+            )
+
+        def weave_aside(words, rows):
+            nc.gpsimd.tensor_scalar(
+                words.rearrange("p (c i) j -> p c i j", i=4),
+                rows.rearrange("p j (c i) -> p c i j", i=4),
+                1.0,
+                0.0,
+                ALU.mult,
+                ALU.add,
             )
 
         def scores(q_mx, k_mx, g, c):
@@ -239,10 +248,11 @@ def tile_attend_gat_k_kernel(tc, qT, kT, vT, doT, rw, qm, offs, out):
         quantize(k_mx[1], low, k_words[:, high, :].rearrange("p n j -> p (n j)"), E4)
         score = [scores(q_mx, k_mx, 0, c) for c in range(PACK)]
         ds0 = tile([P, N, PACK], BF16, "ds0")
-        for c in range(PACK):
+        for c in range(PACK - 1):
             ds_words(ds0[:, block(c), :], score[c], 0, c)
         q_mx = (tile([P, PASS], U32, "woven02"), tile([P, PASS], U8, "q1_scales"))
         quantize(q_mx, slice(0, PASS), q1_dealt[:].rearrange("p t s j -> p (t s j)"), E4)
+        ds_words(ds0[:, block(PACK - 1), :], score[PACK - 1], 0, PACK - 1)
         score = [scores(q_mx, k_mx, 1, c) for c in range(PACK)]
         qm_words = {}
         qm_mx = {}
@@ -261,67 +271,55 @@ def tile_attend_gat_k_kernel(tc, qT, kT, vT, doT, rw, qm, offs, out):
             copy(dk[:], bank[:])
             return dk
 
-        def scatter_low(j, between=None):
+        def scatter_low(j):
             dk = dk_columns(j, low, "dp_bank", 4, tile([P, N // 2], F32, ("dk_low0", "do0_dealt0", "do0_dealt1", "do1_dealt0")[j]), nc.scalar.copy)
-            if between:
-                between()
             nc.scalar.activation(windows[j][:].indirect(listed(low)), dk[:], COPY)
 
-        for j in range(2):
-            qm_words[j] = late.tile([P, 2, P, PACK], BF16, name=f"qm_words{j}", align_bytes=64, offset=j * 2048)
+        qm_words[0] = late.tile([P, 2, P, PACK], BF16, name="qm_words0", align_bytes=64, offset=0)
+        qm_words[1] = tile([P, 2, P, PACK], BF16, "q1_dealt")
+        weave_aside(qm_words[1][:, 0], qm_raw[1, 0])
         woven[1, 3] = shared.tile([P, P, PACK], F32, name="woven13", align_bytes=64, offset=0)[:]
         weave(nc.scalar.copy, woven[1, 3], dp[1][:, :, block(3)])
-        for j, g in ((0, 0), (1, 0), (0, 1), (1, 1)):
+        for j, g in ((0, 0), (0, 1), (1, 1)):
             weave(nc.scalar.copy, qm_words[j][:, g], qm_raw[j, g])
         words20 = tile([P, P, PACK], BF16, "words20")
         weave(nc.scalar.copy, words20[:], qm_raw[2, 0])
         ds0_codes = shared.tile([P, N], U32, name="ds0_codes", align_bytes=64, offset=4 * PASS)
         ds_mx = [(ds0_codes, tile([P, N], U8, "ds0_scales")), ds1_mx]
-        quantize(ds_mx[0], slice(0, N), ds0[:].rearrange("p n t -> p (n t)"), E5)
 
         ds1_low = tile([P, N // 2, PACK], BF16, "ds1_low")
         for c in (0, 1):
             ds_words(ds1_low[:, block(c), :], score[c], 1, c)
+        quantize(ds_mx[0], low, ds0[:, low, :].rearrange("p n t -> p (n t)"), E5)
         qm_quantize_both(0, qm_words[0][:], tile([P, 2 * P], U32, "woven10"))
         quantize(ds1_mx, low, ds1_low[:].rearrange("p n t -> p (n t)"), E5)
         scatter_low(0)
-        words30 = tile([P, P, PACK], BF16, "ds1_low")
-        nc.gpsimd.tensor_scalar(
-            words30[:].rearrange("p (c i) j -> p c i j", i=4),
-            qm_raw[3, 0].rearrange("p j (c i) -> p c i j", i=4),
-            1.0,
-            0.0,
-            ALU.mult,
-            ALU.add,
-        )
+
+        def qm_quantize(j, g, words, codes):
+            qm_mx[j, g] = (codes, tile([P, P], U8, f"qm_scales{j}{g}"))
+            quantize(qm_mx[j, g], slice(0, P), words.rearrange("p d j -> p (d j)"), E4)
+
+        words21 = tile([P, P, PACK], BF16, "ds1_low")
+        weave_aside(words21[:], qm_raw[2, 1])
         ds1_high = late.tile([P, N // 2, PACK], BF16, name="ds1_high", align_bytes=64, offset=0)
         for c in (2, 3):
             ds_words(ds1_high[:, block(c - 2), :], score[c], 1, c)
-        qm_quantize_both(1, qm_words[1][:], shared.tile([P, 2 * P], U32, name="codes1", align_bytes=64, offset=4096))
+        quantize(ds_mx[0], high, ds0[:, high, :].rearrange("p n t -> p (n t)"), E5)
         quantize(ds1_mx, high, ds1_high[:].rearrange("p n t -> p (n t)"), E5)
-        words21 = shared.tile([P, P, PACK], BF16, name="words21", align_bytes=64, offset=0)
-        weave(nc.vector.tensor_copy, words21[:], qm_raw[2, 1])
-        codes20 = shared.tile([P, P], U32, name="codes20", align_bytes=64, offset=4096 + 1024)
-        qm_mx[2, 0] = (codes20, tile([P, P], U8, "scales20"))
-        quantize(qm_mx[2, 0], slice(0, P), words20[:].rearrange("p d j -> p (d j)"), E4)
-        words31 = tile([P, P, PACK], BF16, "words20")
+        qm_quantize_both(1, qm_words[1][:], shared.tile([P, 2 * P], U32, name="codes1", align_bytes=64, offset=0))
         for j in range(D // P):
-            if j < 2:
-                dk = shared.tile([P, N // 2], F32, name=f"dk_high{j}", align_bytes=64, offset=(1024, 0)[j])
-            else:
-                dk = tile([P, N // 2], F32, f"k{j}")
-            dk_columns(j, high, ("dk_bank", "score0", "score1", "score2")[j], 1, dk, nc.vector.tensor_copy)
+            dk = tile([P, N // 2], F32, ("k2", "k1", "k3", "do1_dealt1")[j])
+            copy = nc.scalar.copy if j > 1 else nc.vector.tensor_copy
+            dk_columns(j, high, ("dk_bank", "score0", "score1", "score2")[j], 1, dk, copy)
             if j == 0:
-                qm_mx[2, 1] = mx_pair("qm21", P)
-                quantize(qm_mx[2, 1], slice(0, P), words21[:].rearrange("p d j -> p (d j)"), E4)
+                qm_quantize(2, 0, words20[:], shared.tile([P, P], U32, name="codes20", align_bytes=64, offset=1024))
+                qm_quantize(2, 1, words21[:], shared.tile([P, P], U32, name="codes21", align_bytes=64, offset=1536))
+                words3 = tile([P, 2, P, PACK], BF16, "ds1_low")
+                for g in range(2):
+                    weave_aside(words3[:, g], qm_raw[3, g])
             if j == 1:
-                for g, words in enumerate((words30, words31)):
-                    codes = shared.tile([P, P], U32, name=f"codes3{g}", align_bytes=64, offset=1024 + 512 * g)
-                    qm_mx[3, g] = (codes, tile([P, P], U8, f"scales3{g}"))
-                    quantize(qm_mx[3, g], slice(0, P), words[:].rearrange("p d j -> p (d j)"), E4)
+                qm_quantize_both(3, words3[:], tile([P, 2 * P], U32, "qm_codes3"))
             nc.vector.tensor_copy(windows[j][:].indirect(listed(high)), dk[:])
             nc.sync.dma_start(out=out[block(j), :], in_=windows[j][:])
-            if j == 0:
-                scatter_low(1, lambda: weave(nc.scalar.copy, words31[:], qm_raw[3, 1]))
-            elif j + 1 < D // P:
+            if j + 1 < D // P:
                 scatter_low(j + 1)

@@ -24,7 +24,6 @@ ASIDE = 40
 VECTOR_WEAVES = 2
 LATE_WEAVES = 2
 SCORE_BANKS = 3
-WARM_UPS = 2
 
 
 def tile_attend_gat_k_kernel(tc, qT, kT, vT, doT, rw, qm, offs, out):
@@ -202,9 +201,6 @@ def tile_attend_gat_k_kernel(tc, qT, kT, vT, doT, rw, qm, offs, out):
             nc.vector.tensor_copy(k_words[:, cols, PACK - 1], k_planes[PACK - 1][:].indirect(listed(cols)))
         k_mx = [mx_pair("k_low", N // 2)]
         quantize(k_mx[0], low, k_words[:, low, :].rearrange("p n j -> p (n j)"), E4)
-        warm = ps.tile([P, N], F32, name="dk_bank", bufs=1)
-        for i in range(WARM_UPS):
-            mm(warm[:], k_mx[0], block(i), E4, v_mx, slice(0, N), E4)
         q0_dealt = [tile([P, 2, P, PACK], BF16, f"q0_dealt{u}") for u in range(2)]
         for copy, h, u, s0, s1 in q0_shares:
             copy(
@@ -216,7 +212,7 @@ def tile_attend_gat_k_kernel(tc, qT, kT, vT, doT, rw, qm, offs, out):
         q1_dealt = tile([P, PACK, P, PACK], BF16, "q1_dealt")
 
         def round_aside(dst, src):
-            in_order = "p s j t -> p t s j"
+            in_order = "p s j t -> p s t j"
             nc.gpsimd.tensor_scalar(dst.rearrange(in_order), src.rearrange(in_order), 1.0, 0.0, ALU.mult, ALU.add)
 
         q1_shares = (
@@ -250,9 +246,12 @@ def tile_attend_gat_k_kernel(tc, qT, kT, vT, doT, rw, qm, offs, out):
         ds0 = tile([P, N, PACK], BF16, "ds0")
         for c in range(PACK - 1):
             ds_words(ds0[:, block(c), :], score[c], 0, c)
+        ds_mx = [mx_pair("ds0", N), ds1_mx]
+        quantize(ds_mx[0], low, ds0[:, low, :].rearrange("p n t -> p (n t)"), E5)
         q_mx = (tile([P, PASS], U32, "woven02"), tile([P, PASS], U8, "q1_scales"))
         quantize(q_mx, slice(0, PASS), q1_dealt[:].rearrange("p t s j -> p (t s j)"), E4)
         ds_words(ds0[:, block(PACK - 1), :], score[PACK - 1], 0, PACK - 1)
+        quantize(ds_mx[0], high, ds0[:, high, :].rearrange("p n t -> p (n t)"), E5)
         score = [scores(q_mx, k_mx, 1, c) for c in range(PACK)]
         qm_words = {}
         qm_mx = {}
@@ -268,7 +267,7 @@ def tile_attend_gat_k_kernel(tc, qT, kT, vT, doT, rw, qm, offs, out):
             bank = ps.tile([P, width], F32, name=bank_name, bufs=bufs)
             for g in range(2):
                 mm(bank[:], qm_mx[j, g], slice(0, P), E4, ds_mx[g], cols, E5, start=g == 0, stop=g == 1)
-            copy(dk[:], bank[:])
+            copy(dk[:, :], bank[:])
             return dk
 
         def scatter_low(j):
@@ -284,16 +283,16 @@ def tile_attend_gat_k_kernel(tc, qT, kT, vT, doT, rw, qm, offs, out):
             weave(nc.scalar.copy, qm_words[j][:, g], qm_raw[j, g])
         words20 = tile([P, P, PACK], BF16, "words20")
         weave(nc.scalar.copy, words20[:], qm_raw[2, 0])
-        ds0_codes = shared.tile([P, N], U32, name="ds0_codes", align_bytes=64, offset=4 * PASS)
-        ds_mx = [(ds0_codes, tile([P, N], U8, "ds0_scales")), ds1_mx]
 
         ds1_low = tile([P, N // 2, PACK], BF16, "ds1_low")
         for c in (0, 1):
             ds_words(ds1_low[:, block(c), :], score[c], 1, c)
-        quantize(ds_mx[0], low, ds0[:, low, :].rearrange("p n t -> p (n t)"), E5)
         qm_quantize_both(0, qm_words[0][:], tile([P, 2 * P], U32, "woven10"))
-        quantize(ds1_mx, low, ds1_low[:].rearrange("p n t -> p (n t)"), E5)
-        scatter_low(0)
+        first = tile([P, N // 2], F32, "dk_low0")
+        for c in (0, 1):
+            quantize(ds1_mx, block(c), ds1_low[:, block(c), :].rearrange("p n t -> p (n t)"), E5)
+            dk_columns(0, block(c), "dp_bank", 4, first[:, block(c)], nc.scalar.copy)
+        nc.scalar.activation(windows[0][:].indirect(listed(low)), first[:], COPY)
 
         def qm_quantize(j, g, words, codes):
             qm_mx[j, g] = (codes, tile([P, P], U8, f"qm_scales{j}{g}"))
@@ -304,13 +303,17 @@ def tile_attend_gat_k_kernel(tc, qT, kT, vT, doT, rw, qm, offs, out):
         ds1_high = late.tile([P, N // 2, PACK], BF16, name="ds1_high", align_bytes=64, offset=0)
         for c in (2, 3):
             ds_words(ds1_high[:, block(c - 2), :], score[c], 1, c)
-        quantize(ds_mx[0], high, ds0[:, high, :].rearrange("p n t -> p (n t)"), E5)
-        quantize(ds1_mx, high, ds1_high[:].rearrange("p n t -> p (n t)"), E5)
-        qm_quantize_both(1, qm_words[1][:], shared.tile([P, 2 * P], U32, name="codes1", align_bytes=64, offset=0))
+        qm_quantize_both(1, qm_words[1][:], shared.tile([P, 2 * P], U32, name="codes1", align_bytes=64, offset=4096))
+        for c in (2, 3):
+            quantize(ds1_mx, block(c), ds1_high[:, block(c - 2), :].rearrange("p n t -> p (n t)"), E5)
         for j in range(D // P):
             dk = tile([P, N // 2], F32, ("k2", "k1", "k3", "do1_dealt1")[j])
             copy = nc.scalar.copy if j > 1 else nc.vector.tensor_copy
-            dk_columns(j, high, ("dk_bank", "score0", "score1", "score2")[j], 1, dk, copy)
+            if j == 0:
+                dk_columns(0, block(2), "dk_bank", 1, dk[:, block(0)], copy)
+                dk_columns(0, block(3), "score0", 1, dk[:, block(1)], copy)
+            else:
+                dk_columns(j, high, ("dk_bank", "score2", "score1")[j - 1], 1, dk, copy)
             if j == 0:
                 qm_quantize(2, 0, words20[:], shared.tile([P, P], U32, name="codes20", align_bytes=64, offset=1024))
                 qm_quantize(2, 1, words21[:], shared.tile([P, P], U32, name="codes21", align_bytes=64, offset=1536))

@@ -19,10 +19,8 @@ COPY = mybir.ActivationFunctionType.Copy
 P = 128
 PACK = 4
 PASS = P * PACK
-SPLIT = 48
+SPLIT = 96
 ASIDE = 40
-VECTOR_WEAVES = 2
-LATE_WEAVES = 2
 SCORE_BANKS = 3
 
 
@@ -31,17 +29,16 @@ def tile_attend_gat_k_kernel(tc, qT, kT, vT, doT, rw, qm, offs, out):
     with ExitStack() as ctx:
         lists = ctx.enter_context(tc.tile_pool(name="lists", bufs=1))
         sb = ctx.enter_context(tc.tile_pool(name="sb", bufs=1))
-        shared = ctx.enter_context(tc.tile_pool(name="shared", bufs=1))
-        late = ctx.enter_context(tc.tile_pool(name="late", bufs=1))
         ps = ctx.enter_context(tc.psum_pool(name="ps", bufs=4))
 
         def tile(shape, dtype, name):
-            return sb.tile(shape, dtype, name=name, align_bytes=64)
+            return sb.tile(shape, dtype, name=name, align_bytes=256)
 
         def load_planes(pool, name, j0, count):
-            held = tile([P, count, T], F32, f"{name}{j0}")
-            nc.sync.dma_start(out=held[:], in_=pool.rearrange("(p j) t -> p j t", j=PACK)[:, j0 : j0 + count, :])
-            return [held[:, i, :] for i in range(count)]
+            held = tile([P, count * T], F32, f"{name}{j0}")
+            rows = pool.rearrange("(p j) t -> p (j t)", j=PACK)
+            nc.sync.dma_start(out=held[:], in_=rows[:, j0 * T : (j0 + count) * T])
+            return [held[:, i * T : (i + 1) * T] for i in range(count)]
 
         def load_columns(src, r0, width, name):
             raw = tile([P, PACK, width], F32, name)
@@ -51,25 +48,23 @@ def tile_attend_gat_k_kernel(tc, qT, kT, vT, doT, rw, qm, offs, out):
 
         gate_rows = tile([P, PASS], F32, "gate_rows")
         nc.gpsimd.memset(gate_rows[:], 0.0)
-        v_planes = load_planes(vT, "v", 0, 2)
+        v_planes = load_planes(vT, "v", 0, 1)
         offsets = lists.tile([P, N // 16], U16, name="offsets")
         nc.sync.dma_start(offsets[:], offs)
         nc.sync.dma_start(out=gate_rows[0:2, :], in_=rw[0].rearrange("(g r) o -> g (r o)", g=2))
         identity = tile([P, P], F32, "identity")
         make_identity(nc, identity[:])
+        v_planes.extend(load_planes(vT, "v", 1, 1))
         v_planes.extend(load_planes(vT, "v", 2, 2))
         do_raw = load_columns(doT[0], 0, R, "do")
         k_planes = []
-        for j in range(PACK):
-            k_planes.append(tile([P, T], F32, f"k{j}"))
-            nc.sync.dma_start(out=k_planes[j][:], in_=kT.rearrange("(p j) t -> p j t", j=PACK)[:, j, :])
-        q_raw = [shared.tile([P, PACK, PASS // 2], F32, name="q0", align_bytes=64, offset=4096)]
-        nc.sync.dma_start(out=q_raw[0][:], in_=qT[0].rearrange("(p j) r -> p j r", j=PACK)[:, :, 0 : PASS // 2])
-        q_raw.extend(load_columns(qT[0], i * (PASS // 2), PASS // 2, f"q{i}") for i in (1, 2))
-        q_raw.append(shared.tile([P, PACK, PASS // 2], F32, name="q3", align_bytes=64, offset=0))
-        nc.sync.dma_start(out=q_raw[3][:], in_=qT[0].rearrange("(p j) r -> p j r", j=PACK)[:, :, R - PASS // 2 : R])
+        for j in range(PACK - 1):
+            k_planes.extend(load_planes(kT, "k", j, 1))
+        q0_raw = load_columns(qT[0], 0, PASS, "q0")
+        k_planes.extend(load_planes(kT, "k", PACK - 1, 1))
+        q1_raw = [load_columns(qT[0], PASS + h * (PASS // 2), PASS // 2, f"q1{h}") for h in range(2)]
         qm_raw = {}
-        for j0, j1, names in ((0, 2, ("qm0", "qm1")), (2, 3, ("v0", "v2")), (3, 4, ("k0", "k1"))):
+        for j0, j1, names in ((0, 2, ("v0", "v1")), (2, 3, ("qm20", "qm21")), (3, 4, ("k0", "k1"))):
             for g in range(2):
                 held = load_columns(qm[0, g * PASS : (g + 1) * PASS, :], j0 * P, (j1 - j0) * P, names[g])
                 for j in range(j0, j1):
@@ -87,31 +82,18 @@ def tile_attend_gat_k_kernel(tc, qT, kT, vT, doT, rw, qm, offs, out):
         def quantize(pair, cols, src, fmt):
             nc.vector.quantize_mx(out=pair[0][:, cols].bitcast(fmt), scales=pair[1][:, cols], in_=src)
 
-        def gather(planes, name):
-            words = tile([P, N, PACK], BF16, name + "_words")
-            for j in range(PACK):
-                nc.vector.tensor_copy(words[:, :, j], planes[j].indirect(offsets[:]))
-            pair = mx_pair(name, N)
-            quantize(pair, slice(0, N), words[:].rearrange("p n j -> p (n j)"), E4)
-            return pair
+        def scalar_gather(dst, src):
+            nc.scalar.activation(dst, src, COPY)
 
-        def deal_into(halves, raw, shares):
+        def deal(dealt, raw, s_at, shares):
             for copy, u, s0, s1 in shares:
                 copy(
-                    halves[u][:, :, s0:s1, :].rearrange("p t s j -> p s j t"),
+                    dealt[:, 2 * u : 2 * u + 2, s_at + s0 : s_at + s1, :].rearrange("p t s j -> p s j t"),
                     raw.rearrange("p j (s t) -> p s j t", t=PACK)[:, s0:s1, :, 2 * u : 2 * u + 2],
                 )
 
-        def deal(raw, name, shares):
-            halves = [tile([P, 2, P, PACK], BF16, f"{name}_dealt{u}") for u in range(2)]
-            deal_into(halves, raw, shares)
-            return halves
-
-        def deal_quantize(halves, name, fmt):
-            pair = mx_pair(name, PASS)
-            for u, half in enumerate(halves):
-                quantize(pair, slice(2 * u * P, 2 * (u + 1) * P), half[:].rearrange("p t s j -> p (t s j)"), fmt)
-            return pair
+        def quantize_places(pair, dealt, t0, t1, fmt):
+            quantize(pair, slice(t0 * P, t1 * P), dealt[:, t0:t1].rearrange("p t s j -> p (t s j)"), fmt)
 
         def mm(acc, lhs, lcols, lfmt, rhs, rcols, rfmt, start=True, stop=True):
             nc.tensor.matmul_mx(
@@ -126,14 +108,6 @@ def tile_attend_gat_k_kernel(tc, qT, kT, vT, doT, rw, qm, offs, out):
 
         def block(i):
             return slice(i * P, (i + 1) * P)
-
-        def dp_rows(do_mx, v_mx, g):
-            rows = tile([P, PACK, N], F32, f"dp{g}")
-            for t in range(PACK):
-                bank = ps.tile([P, N], F32, name="dp_bank", bufs=4)
-                mm(bank[:], do_mx, block(t), E5, v_mx, slice(0, N), E4)
-                nc.scalar.activation(rows[:, t, :], bank[:], COPY, scale=gate2[:, g, t : t + 1])
-            return rows
 
         def weave(copy, dst, src):
             copy(
@@ -151,10 +125,82 @@ def tile_attend_gat_k_kernel(tc, qT, kT, vT, doT, rw, qm, offs, out):
                 ALU.add,
             )
 
-        def scores(q_mx, k_mx, g, c):
-            bank = ps.tile([P, PACK, P], F32, name=f"score{(g * PACK + c) % SCORE_BANKS}", bufs=1)
+        def round_aside(dst, src):
+            in_order = "p s j t -> p s t j"
+            nc.gpsimd.tensor_scalar(dst.rearrange(in_order), src.rearrange(in_order), 1.0, 0.0, ALU.mult, ALU.add)
+
+        def quarter_product(bank, rows_mx, rows_fmt, slots_mx, c):
             for t in range(PACK):
-                mm(bank[:, t, :], q_mx, block(t), E4, k_mx[c // 2], block(c % 2), E4)
+                mm(bank[:, t, :], rows_mx, block(t), rows_fmt, slots_mx, block(c), E4)
+
+        low, high = slice(0, N // 2), slice(N // 2, N)
+
+        def listed(cols):
+            return offsets[:, cols.start // 16 : cols.stop // 16]
+
+        gate2 = tile([P, 2, PACK], F32, "gate2")
+        turned = ps.tile([P, PACK, P], F32, name="dk_bank", bufs=1)
+        for t in range(PACK):
+            nc.tensor.transpose(turned[:, t, :], gate_rows[:, t:PASS:PACK], identity[:])
+        nc.vector.tensor_scalar(gate2[:], turned[:, :, 0:2].rearrange("p t g -> p g t"), 2.0, None, ALU.mult)
+
+        v_words = tile([P, N, PACK], BF16, "v_words")
+        for j in range(PACK):
+            copy = scalar_gather if j < 2 else nc.vector.tensor_copy
+            copy(v_words[:, :, j], v_planes[j].indirect(offsets[:]))
+        v_mx = mx_pair("v", N)
+        quantize(v_mx, slice(0, N), v_words[:].rearrange("p n j -> p (n j)"), E4)
+
+        both = ((nc.vector.tensor_copy, 0, 0, P), (nc.scalar.copy, 1, 0, P))
+        do_dealt = [tile([P, PACK, P, PACK], BF16, f"do_dealt{g}") for g in range(2)]
+        do_mx = [mx_pair(f"do{g}", PASS) for g in range(2)]
+        for g in range(2):
+            deal(do_dealt[g], do_raw[:, :, g * PASS : (g + 1) * PASS], 0, both)
+        for g in range(2):
+            for u in range(2):
+                quantize_places(do_mx[g], do_dealt[g], 2 * u, 2 * u + 2, E5)
+        gated = {}
+        for g in range(2):
+            for c in range(PACK):
+                bank = ps.tile([P, PACK, P], F32, name="dp_bank", bufs=4)
+                quarter_product(bank, do_mx[g], E5, v_mx, c)
+                gated[g, c] = tile([P, P, PACK], F32, f"gated{g}{c}")
+                nc.vector.tensor_tensor(
+                    gated[g, c][:],
+                    bank[:].rearrange("p t n -> p n t"),
+                    gate2[:, g : g + 1, :].to_broadcast([P, P, PACK]),
+                    ALU.mult,
+                )
+
+        k_words = tile([P, N, PACK], BF16, "k_words")
+        for j in range(PACK - 1):
+            scalar_gather(k_words[:, :, j], k_planes[j].indirect(offsets[:]))
+        q0_dealt = tile([P, PACK, P, PACK], BF16, "q0_dealt")
+        q0_shares = ((nc.vector.tensor_copy, 0, 0, P), (nc.scalar.copy, 1, 0, SPLIT), (nc.vector.tensor_copy, 1, SPLIT, P))
+        deal(q0_dealt, q0_raw[:], 0, q0_shares)
+        q_mx = [mx_pair(f"q{g}", PASS) for g in range(2)]
+        for u in range(2):
+            quantize_places(q_mx[0], q0_dealt, 2 * u, 2 * u + 2, E4)
+
+        k_mx = {}
+        for c in range(PACK):
+            scalar_gather(k_words[:, block(c), PACK - 1], k_planes[PACK - 1].indirect(listed(block(c))))
+        q1_dealt = tile([P, PACK, P, PACK], BF16, "q1_dealt")
+        deal(q1_dealt, q1_raw[0][:], 0, ((nc.scalar.copy, 0, 0, P // 2), (nc.scalar.copy, 1, 0, P // 2)))
+        late_shares = (
+            (nc.scalar.copy, 0, 0, P // 2),
+            (nc.scalar.copy, 1, 0, P // 2 - ASIDE),
+            (round_aside, 1, P // 2 - ASIDE, P // 2),
+        )
+        deal(q1_dealt, q1_raw[1][:], P // 2, late_shares)
+
+        def key_codes(c, name):
+            k_mx[c] = (tile([P, P], U32, name), tile([P, P], U8, f"k_scales{c}"))
+            quantize(k_mx[c], block(0), k_words[:, block(c), :].rearrange("p n j -> p (n j)"), E4)
+
+        def scores(g, c):
+            bank = ps.tile([P, PACK, P], F32, name=f"score{(g * PACK + c) % SCORE_BANKS}", bufs=1)
+            quarter_product(bank, q_mx[g], E4, k_mx[c], 0)
             return bank
 
         def ds_words(words, bank, g, c):
@@ -162,97 +208,26 @@ def tile_attend_gat_k_kernel(tc, qT, kT, vT, doT, rw, qm, offs, out):
                 out=words,
                 in0=bank[:].rearrange("p t n -> p n t"),
                 scalar=0.0,
-                in1=woven[g, c],
+                in1=gated[g, c][:],
                 op0=ALU.max,
                 op1=ALU.mult,
             )
 
-        low, high = slice(0, N // 2), slice(N // 2, N)
-
-        def listed(cols):
-            return offsets[:, cols.start // 16 : cols.stop // 16]
-
-        q0_shares = (
-            (nc.scalar.copy, 0, 0, 0, P // 2),
-            (nc.scalar.copy, 0, 1, 0, P // 2),
-            (nc.scalar.copy, 1, 1, 0, SPLIT),
-            (nc.vector.tensor_copy, 1, 0, 0, P // 2),
-            (nc.vector.tensor_copy, 1, 1, SPLIT, P // 2),
-        )
-
-        ds1_mx = mx_pair("ds1", N)
-        gate2 = tile([P, 2, PACK], F32, "gate2")
-        turned = ps.tile([P, PACK, P], F32, name="dk_bank", bufs=1)
-        for t in range(PACK):
-            nc.tensor.transpose(turned[:, t, :], gate_rows[:, t:PASS:PACK], identity[:])
-        nc.vector.tensor_scalar(gate2[:], turned[:, :, 0:2].rearrange("p t g -> p g t"), 2.0, None, ALU.mult)
-        v_mx = gather(v_planes, "v")
-        both = ((nc.vector.tensor_copy, 0, 0, P), (nc.scalar.copy, 1, 0, P))
-        do_dealt = [deal(do_raw[:, :, g * PASS : (g + 1) * PASS], f"do{g}", both) for g in range(2)]
-        do_mx = [deal_quantize(do_dealt[g], f"do{g}", E5) for g in range(2)]
-        dp = [dp_rows(do_mx[g], v_mx, g) for g in range(2)]
-
-        k_rows = tile([P, PACK - 1, N], BF16, "k_rows")
-        k_words = tile([P, N, PACK], BF16, "k_words")
-        for j in range(PACK - 1):
-            nc.vector.tensor_copy(k_rows[:, j, :], k_planes[j][:].indirect(offsets[:]))
-        weave(nc.vector.tensor_copy, k_words[:, :, 0 : PACK - 1], k_rows[:])
-        for cols in (low, high):
-            nc.vector.tensor_copy(k_words[:, cols, PACK - 1], k_planes[PACK - 1][:].indirect(listed(cols)))
-        k_mx = [mx_pair("k_low", N // 2)]
-        quantize(k_mx[0], low, k_words[:, low, :].rearrange("p n j -> p (n j)"), E4)
-        q0_dealt = [tile([P, 2, P, PACK], BF16, f"q0_dealt{u}") for u in range(2)]
-        for copy, h, u, s0, s1 in q0_shares:
-            copy(
-                q0_dealt[u][:, :, h * (P // 2) + s0 : h * (P // 2) + s1, :].rearrange("p t s j -> p s j t"),
-                q_raw[h][:].rearrange("p j (s t) -> p s j t", t=PACK)[:, s0:s1, :, 2 * u : 2 * u + 2],
-            )
-        woven = {(1, 2): shared.tile([P, P, PACK], F32, name="woven12", align_bytes=64, offset=4096)[:]}
-        weave(nc.scalar.copy, woven[1, 2], dp[1][:, :, block(2)])
-        q1_dealt = tile([P, PACK, P, PACK], BF16, "q1_dealt")
-
-        def round_aside(dst, src):
-            in_order = "p s j t -> p s t j"
-            nc.gpsimd.tensor_scalar(dst.rearrange(in_order), src.rearrange(in_order), 1.0, 0.0, ALU.mult, ALU.add)
-
-        q1_shares = (
-            (nc.scalar.copy, 0, 0, 0, P // 2),
-            (nc.scalar.copy, 0, 1, 0, P // 2),
-            (nc.scalar.copy, 1, 0, 0, P // 2),
-            (nc.scalar.copy, 1, 1, 0, P // 2 - ASIDE),
-            (round_aside, 1, 1, P // 2 - ASIDE, P // 2),
-        )
-        for copy, h, u, s0, s1 in q1_shares:
-            copy(
-                q1_dealt[:, 2 * u : 2 * u + 2, h * (P // 2) + s0 : h * (P // 2) + s1, :].rearrange("p t s j -> p s j t"),
-                q_raw[2 + h][:].rearrange("p j (s t) -> p s j t", t=PACK)[:, s0:s1, :, 2 * u : 2 * u + 2],
-            )
-
-        for g in range(2):
-            for c in range(PACK - g * LATE_WEAVES):
-                woven[g, c] = tile([P, P, PACK], F32, f"woven{g}{c}")[:]
-                copy = nc.vector.tensor_copy if g == 0 and c < VECTOR_WEAVES else nc.scalar.copy
-                weave(copy, woven[g, c], dp[g][:, :, block(c)])
-
-        q_mx = mx_pair("q0", PASS)
-        for h in range(2):
-            for t in range(PACK):
-                s0 = h * (P // 2)
-                words = q0_dealt[t // 2][:, t % 2, s0 : s0 + P // 2, :].rearrange("p s j -> p (s j)")
-                quantize(q_mx, slice(t * P + s0, t * P + s0 + P // 2), words, E4)
-        k_mx.append((tile([P, N // 2], U32, "q0_dealt1"), tile([P, N // 2], U8, "k_high_scales")))
-        quantize(k_mx[1], low, k_words[:, high, :].rearrange("p n j -> p (n j)"), E4)
-        score = [scores(q_mx, k_mx, 0, c) for c in range(PACK)]
+        ds_mx = [mx_pair(f"ds{g}", N) for g in range(2)]
         ds0 = tile([P, N, PACK], BF16, "ds0")
         for c in range(PACK - 1):
+            key_codes(c, f"k_codes{c}")
+        score = [scores(0, c) for c in range(PACK - 1)]
+        ds_words(ds0[:, block(0), :], score[0], 0, 0)
+        ds_words(ds0[:, block(1), :], score[1], 0, 1)
+        key_codes(PACK - 1, "gated00")
+        score.append(scores(0, PACK - 1))
+        for c in range(2, PACK):
             ds_words(ds0[:, block(c), :], score[c], 0, c)
-        ds_mx = [mx_pair("ds0", N), ds1_mx]
-        quantize(ds_mx[0], low, ds0[:, low, :].rearrange("p n t -> p (n t)"), E5)
-        q_mx = (tile([P, PASS], U32, "woven02"), tile([P, PASS], U8, "q1_scales"))
-        quantize(q_mx, slice(0, PASS), q1_dealt[:].rearrange("p t s j -> p (t s j)"), E4)
-        ds_words(ds0[:, block(PACK - 1), :], score[PACK - 1], 0, PACK - 1)
-        quantize(ds_mx[0], high, ds0[:, high, :].rearrange("p n t -> p (n t)"), E5)
-        score = [scores(q_mx, k_mx, 1, c) for c in range(PACK)]
+        quantize_places(q_mx[1], q1_dealt, 0, PACK, E4)
+        quantize(ds_mx[0], slice(0, N), ds0[:].rearrange("p n t -> p (n t)"), E5)
+        score = [scores(1, c) for c in range(PACK)]
+
         qm_words = {}
         qm_mx = {}
 
@@ -267,30 +242,25 @@ def tile_attend_gat_k_kernel(tc, qT, kT, vT, doT, rw, qm, offs, out):
             bank = ps.tile([P, width], F32, name=bank_name, bufs=bufs)
             for g in range(2):
                 mm(bank[:], qm_mx[j, g], slice(0, P), E4, ds_mx[g], cols, E5, start=g == 0, stop=g == 1)
-            copy(dk[:, :], bank[:])
-            return dk
+            copy(dk, bank[:])
 
         def scatter_low(j):
-            dk = dk_columns(j, low, "dp_bank", 4, tile([P, N // 2], F32, ("dk_low0", "do0_dealt0", "do0_dealt1", "do1_dealt0")[j]), nc.scalar.copy)
+            dk = tile([P, N // 2], F32, f"dk_low{j}")
+            dk_columns(j, low, "dp_bank", 4, dk[:], nc.scalar.copy)
             nc.scalar.activation(windows[j][:].indirect(listed(low)), dk[:], COPY)
 
-        qm_words[0] = late.tile([P, 2, P, PACK], BF16, name="qm_words0", align_bytes=64, offset=0)
-        qm_words[1] = tile([P, 2, P, PACK], BF16, "q1_dealt")
-        weave_aside(qm_words[1][:, 0], qm_raw[1, 0])
-        woven[1, 3] = shared.tile([P, P, PACK], F32, name="woven13", align_bytes=64, offset=0)[:]
-        weave(nc.scalar.copy, woven[1, 3], dp[1][:, :, block(3)])
-        for j, g in ((0, 0), (0, 1), (1, 1)):
+        for j in range(3):
+            qm_words[j] = tile([P, 2, P, PACK], BF16, f"qm_words{j}")
+        for j, g in ((0, 0), (1, 0), (0, 1), (1, 1), (2, 0)):
             weave(nc.scalar.copy, qm_words[j][:, g], qm_raw[j, g])
-        words20 = tile([P, P, PACK], BF16, "words20")
-        weave(nc.scalar.copy, words20[:], qm_raw[2, 0])
 
-        ds1_low = tile([P, N // 2, PACK], BF16, "ds1_low")
+        ds1 = [tile([P, P, PACK], BF16, f"ds1{c}") for c in range(2)]
         for c in (0, 1):
-            ds_words(ds1_low[:, block(c), :], score[c], 1, c)
-        qm_quantize_both(0, qm_words[0][:], tile([P, 2 * P], U32, "woven10"))
+            ds_words(ds1[c][:], score[c], 1, c)
+        qm_quantize_both(0, qm_words[0][:], tile([P, 2 * P], U32, "gated10"))
         first = tile([P, N // 2], F32, "dk_low0")
         for c in (0, 1):
-            quantize(ds1_mx, block(c), ds1_low[:, block(c), :].rearrange("p n t -> p (n t)"), E5)
+            quantize(ds_mx[1], block(c), ds1[c][:].rearrange("p n t -> p (n t)"), E5)
             dk_columns(0, block(c), "dp_bank", 4, first[:, block(c)], nc.scalar.copy)
         nc.scalar.activation(windows[0][:].indirect(listed(low)), first[:], COPY)
 
@@ -298,26 +268,27 @@ def tile_attend_gat_k_kernel(tc, qT, kT, vT, doT, rw, qm, offs, out):
             qm_mx[j, g] = (codes, tile([P, P], U8, f"qm_scales{j}{g}"))
             quantize(qm_mx[j, g], slice(0, P), words.rearrange("p d j -> p (d j)"), E4)
 
-        words21 = tile([P, P, PACK], BF16, "ds1_low")
+        words21 = tile([P, P, PACK], BF16, "ds11")
         weave_aside(words21[:], qm_raw[2, 1])
-        ds1_high = late.tile([P, N // 2, PACK], BF16, name="ds1_high", align_bytes=64, offset=0)
+        ds1.append(tile([P, P, PACK], BF16, "qm_words0"))
+        ds1.append(tile([P, P, PACK], BF16, "ds13"))
         for c in (2, 3):
-            ds_words(ds1_high[:, block(c - 2), :], score[c], 1, c)
-        qm_quantize_both(1, qm_words[1][:], shared.tile([P, 2 * P], U32, name="codes1", align_bytes=64, offset=4096))
+            ds_words(ds1[c][:], score[c], 1, c)
         for c in (2, 3):
-            quantize(ds1_mx, block(c), ds1_high[:, block(c - 2), :].rearrange("p n t -> p (n t)"), E5)
+            quantize(ds_mx[1], block(c), ds1[c][:].rearrange("p n t -> p (n t)"), E5)
+        qm_quantize_both(1, qm_words[1][:], tile([P, 2 * P], U32, "qm_words0"))
         for j in range(D // P):
-            dk = tile([P, N // 2], F32, ("k2", "k1", "k3", "do1_dealt1")[j])
+            dk = tile([P, N // 2], F32, ("k2", "k1", "k3", "dk_high3")[j])
             copy = nc.scalar.copy if j > 1 else nc.vector.tensor_copy
             if j == 0:
                 dk_columns(0, block(2), "dk_bank", 1, dk[:, block(0)], copy)
                 dk_columns(0, block(3), "score0", 1, dk[:, block(1)], copy)
             else:
-                dk_columns(j, high, ("dk_bank", "score2", "score1")[j - 1], 1, dk, copy)
+                dk_columns(j, high, ("dk_bank", "score2", "score1")[j - 1], 1, dk[:], copy)
             if j == 0:
-                qm_quantize(2, 0, words20[:], shared.tile([P, P], U32, name="codes20", align_bytes=64, offset=1024))
-                qm_quantize(2, 1, words21[:], shared.tile([P, P], U32, name="codes21", align_bytes=64, offset=1536))
-                words3 = tile([P, 2, P, PACK], BF16, "ds1_low")
+                qm_quantize(2, 0, qm_words[2][:, 0], tile([P, P], U32, "ds13"))
+                qm_quantize(2, 1, words21[:], tile([P, P], U32, "gated13"))
+                words3 = tile([P, 2, P, PACK], BF16, "ds11")
                 for g in range(2):
                     weave_aside(words3[:, g], qm_raw[3, g])
             if j == 1:

@@ -20,7 +20,7 @@ P = 128
 PACK = 4
 PASS = P * PACK
 SPLIT = 96
-ASIDE = 40
+ASIDE = 48
 SCORE_BANKS = 3
 
 
@@ -173,8 +173,12 @@ def tile_attend_gat_k_kernel(tc, qT, kT, vT, doT, rw, qm, offs, out):
                 )
 
         k_words = tile([P, N, PACK], BF16, "k_words")
-        for j in range(PACK - 1):
+        for j in range(2):
             scalar_gather(k_words[:, :, j], k_planes[j].indirect(offsets[:]))
+        most, last = slice(0, N - P), block(PACK - 1)
+        scalar_gather(k_words[:, most, 2], k_planes[2].indirect(listed(most)))
+        k_rows = tile([P, 2, P], BF16, "k_rows")
+        nc.vector.tensor_copy(k_rows[:, 0, :], k_planes[2].indirect(listed(last)))
         q0_dealt = tile([P, PACK, P, PACK], BF16, "q0_dealt")
         q0_shares = ((nc.vector.tensor_copy, 0, 0, P), (nc.scalar.copy, 1, 0, SPLIT), (nc.vector.tensor_copy, 1, SPLIT, P))
         deal(q0_dealt, q0_raw[:], 0, q0_shares)
@@ -183,8 +187,9 @@ def tile_attend_gat_k_kernel(tc, qT, kT, vT, doT, rw, qm, offs, out):
             quantize_places(q_mx[0], q0_dealt, 2 * u, 2 * u + 2, E4)
 
         k_mx = {}
-        for c in range(PACK):
+        for c in range(PACK - 1):
             scalar_gather(k_words[:, block(c), PACK - 1], k_planes[PACK - 1].indirect(listed(block(c))))
+        nc.vector.tensor_copy(k_rows[:, 1, :], k_planes[PACK - 1].indirect(listed(last)))
         q1_dealt = tile([P, PACK, P, PACK], BF16, "q1_dealt")
         deal(q1_dealt, q1_raw[0][:], 0, ((nc.scalar.copy, 0, 0, P // 2), (nc.scalar.copy, 1, 0, P // 2)))
         late_shares = (
@@ -213,19 +218,18 @@ def tile_attend_gat_k_kernel(tc, qT, kT, vT, doT, rw, qm, offs, out):
                 op1=ALU.mult,
             )
 
-        ds_mx = [mx_pair(f"ds{g}", N) for g in range(2)]
+        ds_mx = {(g, h): mx_pair(f"ds{g}{h}", N // 2) for g, h in ((0, 0), (1, 0), (1, 1))}
         ds0 = tile([P, N, PACK], BF16, "ds0")
-        for c in range(PACK - 1):
+        key_codes(0, "k_codes0")
+        nc.vector.tensor_copy(k_words[:, last, 2:PACK], k_rows[:].rearrange("p j n -> p n j"))
+        for c in (1, 3, 2):
             key_codes(c, f"k_codes{c}")
-        score = [scores(0, c) for c in range(PACK - 1)]
-        ds_words(ds0[:, block(0), :], score[0], 0, 0)
-        ds_words(ds0[:, block(1), :], score[1], 0, 1)
-        key_codes(PACK - 1, "gated00")
-        score.append(scores(0, PACK - 1))
-        for c in range(2, PACK):
+        score = [scores(0, c) for c in range(PACK)]
+        for c in range(PACK - 1):
             ds_words(ds0[:, block(c), :], score[c], 0, c)
+        quantize(ds_mx[0, 0], low, ds0[:, low, :].rearrange("p n t -> p (n t)"), E5)
         quantize_places(q_mx[1], q1_dealt, 0, PACK, E4)
-        quantize(ds_mx[0], slice(0, N), ds0[:].rearrange("p n t -> p (n t)"), E5)
+        ds_words(ds0[:, block(PACK - 1), :], score[PACK - 1], 0, PACK - 1)
         score = [scores(1, c) for c in range(PACK)]
 
         qm_words = {}
@@ -240,8 +244,10 @@ def tile_attend_gat_k_kernel(tc, qT, kT, vT, doT, rw, qm, offs, out):
         def dk_columns(j, cols, bank_name, bufs, dk, copy):
             width = cols.stop - cols.start
             bank = ps.tile([P, width], F32, name=bank_name, bufs=bufs)
+            h = cols.start // (N // 2)
+            within = slice(cols.start - h * (N // 2), cols.stop - h * (N // 2))
             for g in range(2):
-                mm(bank[:], qm_mx[j, g], slice(0, P), E4, ds_mx[g], cols, E5, start=g == 0, stop=g == 1)
+                mm(bank[:], qm_mx[j, g], slice(0, P), E4, ds_mx[g, h], within, E5, start=g == 0, stop=g == 1)
             copy(dk, bank[:])
 
         def scatter_low(j):
@@ -257,10 +263,12 @@ def tile_attend_gat_k_kernel(tc, qT, kT, vT, doT, rw, qm, offs, out):
         ds1 = [tile([P, P, PACK], BF16, f"ds1{c}") for c in range(2)]
         for c in (0, 1):
             ds_words(ds1[c][:], score[c], 1, c)
-        qm_quantize_both(0, qm_words[0][:], tile([P, 2 * P], U32, "gated10"))
+        ds_mx[0, 1] = (tile([P, N // 2], U32, "gated10"), tile([P, N // 2], U8, "ds01_scales"))
+        quantize(ds_mx[0, 1], low, ds0[:, high, :].rearrange("p n t -> p (n t)"), E5)
+        qm_quantize_both(0, qm_words[0][:], tile([P, 2 * P], U32, "gated11"))
         first = tile([P, N // 2], F32, "dk_low0")
         for c in (0, 1):
-            quantize(ds_mx[1], block(c), ds1[c][:].rearrange("p n t -> p (n t)"), E5)
+            quantize(ds_mx[1, 0], block(c), ds1[c][:].rearrange("p n t -> p (n t)"), E5)
             dk_columns(0, block(c), "dp_bank", 4, first[:, block(c)], nc.scalar.copy)
         nc.scalar.activation(windows[0][:].indirect(listed(low)), first[:], COPY)
 
@@ -275,7 +283,7 @@ def tile_attend_gat_k_kernel(tc, qT, kT, vT, doT, rw, qm, offs, out):
         for c in (2, 3):
             ds_words(ds1[c][:], score[c], 1, c)
         for c in (2, 3):
-            quantize(ds_mx[1], block(c), ds1[c][:].rearrange("p n t -> p (n t)"), E5)
+            quantize(ds_mx[1, 1], block(c - 2), ds1[c][:].rearrange("p n t -> p (n t)"), E5)
         qm_quantize_both(1, qm_words[1][:], tile([P, 2 * P], U32, "qm_words0"))
         for j in range(D // P):
             dk = tile([P, N // 2], F32, ("k2", "k1", "k3", "dk_high3")[j])

@@ -64,11 +64,10 @@ def tile_attend_gat_k_kernel(tc, qT, kT, vT, doT, rw, qm, offs, out):
         k_planes.extend(load_planes(kT, "k", PACK - 1, 1))
         q1_raw = [load_columns(qT[0], PASS + h * (PASS // 2), PASS // 2, f"q1{h}") for h in range(2)]
         qm_raw = {}
-        for j0, j1, names in ((0, 2, ("v0", "v1")), (2, 3, ("qm20", "qm21")), (3, 4, ("k0", "k1"))):
-            for g in range(2):
-                held = load_columns(qm[0, g * PASS : (g + 1) * PASS, :], j0 * P, (j1 - j0) * P, names[g])
-                for j in range(j0, j1):
-                    qm_raw[j, g] = held[:, :, (j - j0) * P : (j - j0 + 1) * P]
+        for g, j0, j1, name in ((0, 0, 1, "qm00"), (1, 0, 2, "v0"), (0, 1, 3, "v1"), (1, 2, 3, "qm21"), (0, 3, 4, "k0"), (1, 3, 4, "k1")):
+            held = load_columns(qm[0, g * PASS : (g + 1) * PASS, :], j0 * P, (j1 - j0) * P, name)
+            for j in range(j0, j1):
+                qm_raw[j, g] = held[:, :, (j - j0) * P : (j - j0 + 1) * P]
 
         windows = []
         for j in range(D // P):
@@ -88,12 +87,16 @@ def tile_attend_gat_k_kernel(tc, qT, kT, vT, doT, rw, qm, offs, out):
         def deal(dealt, raw, s_at, shares):
             for copy, u, s0, s1 in shares:
                 copy(
-                    dealt[:, 2 * u : 2 * u + 2, s_at + s0 : s_at + s1, :].rearrange("p t s j -> p s j t"),
+                    dealt[u][:, :, s_at + s0 : s_at + s1, :].rearrange("p t s j -> p s j t"),
                     raw.rearrange("p j (s t) -> p s j t", t=PACK)[:, s0:s1, :, 2 * u : 2 * u + 2],
                 )
 
-        def quantize_places(pair, dealt, t0, t1, fmt):
-            quantize(pair, slice(t0 * P, t1 * P), dealt[:, t0:t1].rearrange("p t s j -> p (t s j)"), fmt)
+        def dealt_tiles(name):
+            return [tile([P, 2, P, PACK], BF16, f"{name}_dealt{u}") for u in range(2)]
+
+        def quantize_dealt(pair, dealt, fmt):
+            for u in range(2):
+                quantize(pair, slice(2 * u * P, 2 * (u + 1) * P), dealt[u][:].rearrange("p t s j -> p (t s j)"), fmt)
 
         def mm(acc, lhs, lcols, lfmt, rhs, rcols, rfmt, start=True, stop=True):
             nc.tensor.matmul_mx(
@@ -152,13 +155,12 @@ def tile_attend_gat_k_kernel(tc, qT, kT, vT, doT, rw, qm, offs, out):
         quantize(v_mx, slice(0, N), v_words[:].rearrange("p n j -> p (n j)"), E4)
 
         both = ((nc.vector.tensor_copy, 0, 0, P), (nc.scalar.copy, 1, 0, P))
-        do_dealt = [tile([P, PACK, P, PACK], BF16, f"do_dealt{g}") for g in range(2)]
+        do_dealt = [dealt_tiles(f"do{g}") for g in range(2)]
         do_mx = [mx_pair(f"do{g}", PASS) for g in range(2)]
         for g in range(2):
             deal(do_dealt[g], do_raw[:, :, g * PASS : (g + 1) * PASS], 0, both)
         for g in range(2):
-            for u in range(2):
-                quantize_places(do_mx[g], do_dealt[g], 2 * u, 2 * u + 2, E5)
+            quantize_dealt(do_mx[g], do_dealt[g], E5)
         gated = {}
         for g in range(2):
             for c in range(PACK):
@@ -179,18 +181,21 @@ def tile_attend_gat_k_kernel(tc, qT, kT, vT, doT, rw, qm, offs, out):
         scalar_gather(k_words[:, most, 2], k_planes[2].indirect(listed(most)))
         k_rows = tile([P, 2, P], BF16, "k_rows")
         nc.vector.tensor_copy(k_rows[:, 0, :], k_planes[2].indirect(listed(last)))
-        q0_dealt = tile([P, PACK, P, PACK], BF16, "q0_dealt")
+        q0_dealt = dealt_tiles("q0")
         q0_shares = ((nc.vector.tensor_copy, 0, 0, P), (nc.scalar.copy, 1, 0, SPLIT), (nc.vector.tensor_copy, 1, SPLIT, P))
         deal(q0_dealt, q0_raw[:], 0, q0_shares)
         q_mx = [mx_pair(f"q{g}", PASS) for g in range(2)]
-        for u in range(2):
-            quantize_places(q_mx[0], q0_dealt, 2 * u, 2 * u + 2, E4)
+        quantize_dealt(q_mx[0], q0_dealt, E4)
+
+        unread = ps.tile([P, N], F32, name="dk_bank", bufs=1)
+        for t in range(2):
+            mm(unread[:], q_mx[0], block(t), E4, v_mx, slice(0, N), E4)
 
         k_mx = {}
         for c in range(PACK - 1):
             scalar_gather(k_words[:, block(c), PACK - 1], k_planes[PACK - 1].indirect(listed(block(c))))
         nc.vector.tensor_copy(k_rows[:, 1, :], k_planes[PACK - 1].indirect(listed(last)))
-        q1_dealt = tile([P, PACK, P, PACK], BF16, "q1_dealt")
+        q1_dealt = dealt_tiles("q1")
         deal(q1_dealt, q1_raw[0][:], 0, ((nc.scalar.copy, 0, 0, P // 2), (nc.scalar.copy, 1, 0, P // 2)))
         late_shares = (
             (nc.scalar.copy, 0, 0, P // 2),
@@ -219,7 +224,7 @@ def tile_attend_gat_k_kernel(tc, qT, kT, vT, doT, rw, qm, offs, out):
             )
 
         ds_mx = {(g, h): mx_pair(f"ds{g}{h}", N // 2) for g, h in ((0, 0), (1, 0), (1, 1))}
-        ds0 = tile([P, N, PACK], BF16, "ds0")
+        ds0 = tile([P, N - P, PACK], BF16, "ds0")
         key_codes(0, "k_codes0")
         nc.vector.tensor_copy(k_words[:, last, 2:PACK], k_rows[:].rearrange("p j n -> p n j"))
         for c in (1, 3, 2):
@@ -228,8 +233,9 @@ def tile_attend_gat_k_kernel(tc, qT, kT, vT, doT, rw, qm, offs, out):
         for c in range(PACK - 1):
             ds_words(ds0[:, block(c), :], score[c], 0, c)
         quantize(ds_mx[0, 0], low, ds0[:, low, :].rearrange("p n t -> p (n t)"), E5)
-        quantize_places(q_mx[1], q1_dealt, 0, PACK, E4)
-        ds_words(ds0[:, block(PACK - 1), :], score[PACK - 1], 0, PACK - 1)
+        quantize_dealt(q_mx[1], q1_dealt, E4)
+        ds03 = tile([P, P, PACK], BF16, "q1_dealt0")
+        ds_words(ds03[:], score[PACK - 1], 0, PACK - 1)
         score = [scores(1, c) for c in range(PACK)]
 
         qm_words = {}
@@ -255,36 +261,37 @@ def tile_attend_gat_k_kernel(tc, qT, kT, vT, doT, rw, qm, offs, out):
             dk_columns(j, low, "dp_bank", 4, dk[:], nc.scalar.copy)
             nc.scalar.activation(windows[j][:].indirect(listed(low)), dk[:], COPY)
 
-        for j in range(3):
+        for j in range(2):
             qm_words[j] = tile([P, 2, P, PACK], BF16, f"qm_words{j}")
-        for j, g in ((0, 0), (1, 0), (0, 1), (1, 1), (2, 0)):
+        for j, g in ((0, 0), (0, 1), (1, 1), (1, 0)):
             weave(nc.scalar.copy, qm_words[j][:, g], qm_raw[j, g])
 
         ds1 = [tile([P, P, PACK], BF16, f"ds1{c}") for c in range(2)]
         for c in (0, 1):
             ds_words(ds1[c][:], score[c], 1, c)
-        ds_mx[0, 1] = (tile([P, N // 2], U32, "gated10"), tile([P, N // 2], U8, "ds01_scales"))
-        quantize(ds_mx[0, 1], low, ds0[:, high, :].rearrange("p n t -> p (n t)"), E5)
-        qm_quantize_both(0, qm_words[0][:], tile([P, 2 * P], U32, "gated11"))
+        qm_quantize_both(0, qm_words[0][:], tile([P, 2 * P], U32, "gated10"))
         first = tile([P, N // 2], F32, "dk_low0")
         for c in (0, 1):
             quantize(ds_mx[1, 0], block(c), ds1[c][:].rearrange("p n t -> p (n t)"), E5)
             dk_columns(0, block(c), "dp_bank", 4, first[:, block(c)], nc.scalar.copy)
+        half = P // 2
+        early20 = tile([P, half, PACK], BF16, "ds11")
+        weave(nc.scalar.copy, early20[:], qm_raw[2, 0][:, :, 0:half])
         nc.scalar.activation(windows[0][:].indirect(listed(low)), first[:], COPY)
+        ds_mx[0, 1] = (tile([P, N // 2], U32, "qm_words0"), tile([P, N // 2], U8, "ds01_scales"))
+        for c, words in ((1, ds03[:]), (0, ds0[:, block(2), :])):
+            quantize(ds_mx[0, 1], block(c), words.rearrange("p n t -> p (n t)"), E5)
 
-        def qm_quantize(j, g, words, codes):
-            qm_mx[j, g] = (codes, tile([P, P], U8, f"qm_scales{j}{g}"))
-            quantize(qm_mx[j, g], slice(0, P), words.rearrange("p d j -> p (d j)"), E4)
-
-        words21 = tile([P, P, PACK], BF16, "ds11")
-        weave_aside(words21[:], qm_raw[2, 1])
-        ds1.append(tile([P, P, PACK], BF16, "qm_words0"))
+        late2 = tile([P, half + P, PACK], BF16, "ds0")
+        weave_aside(late2[:, 0:half], qm_raw[2, 0][:, :, half:P])
+        weave_aside(late2[:, half:], qm_raw[2, 1])
+        ds1.append(tile([P, P, PACK], BF16, "ds10"))
         ds1.append(tile([P, P, PACK], BF16, "ds13"))
         for c in (2, 3):
             ds_words(ds1[c][:], score[c], 1, c)
         for c in (2, 3):
             quantize(ds_mx[1, 1], block(c - 2), ds1[c][:].rearrange("p n t -> p (n t)"), E5)
-        qm_quantize_both(1, qm_words[1][:], tile([P, 2 * P], U32, "qm_words0"))
+        qm_quantize_both(1, qm_words[1][:], tile([P, 2 * P], U32, "ds10"))
         for j in range(D // P):
             dk = tile([P, N // 2], F32, ("k2", "k1", "k3", "dk_high3")[j])
             copy = nc.scalar.copy if j > 1 else nc.vector.tensor_copy
@@ -294,9 +301,13 @@ def tile_attend_gat_k_kernel(tc, qT, kT, vT, doT, rw, qm, offs, out):
             else:
                 dk_columns(j, high, ("dk_bank", "score2", "score1")[j - 1], 1, dk[:], copy)
             if j == 0:
-                qm_quantize(2, 0, qm_words[2][:, 0], tile([P, P], U32, "ds13"))
-                qm_quantize(2, 1, words21[:], tile([P, P], U32, "gated13"))
-                words3 = tile([P, 2, P, PACK], BF16, "ds11")
+                pair = (tile([P, 2 * P], U32, "ds13"), tile([P, 2 * P], U8, "qm_scales2"))
+                quantize(pair, slice(0, half), early20[:].rearrange("p d j -> p (d j)"), E4)
+                quantize(pair, slice(half, P), late2[:, 0:half].rearrange("p d j -> p (d j)"), E4)
+                quantize(pair, block(1), late2[:, half:].rearrange("p d j -> p (d j)"), E4)
+                for g in range(2):
+                    qm_mx[2, g] = (pair[0][:, block(g)], pair[1][:, block(g)])
+                words3 = tile([P, 2, P, PACK], BF16, "ds0")
                 for g in range(2):
                     weave_aside(words3[:, g], qm_raw[3, g])
             if j == 1:

@@ -20,7 +20,7 @@ P = 128
 PACK = 4
 PASS = P * PACK
 SPLIT = 96
-ASIDE = 48
+ASIDE = (28, 16)
 SCORE_BANKS = 3
 
 
@@ -198,9 +198,10 @@ def tile_attend_gat_k_kernel(tc, qT, kT, vT, doT, rw, qm, offs, out):
         q1_dealt = dealt_tiles("q1")
         deal(q1_dealt, q1_raw[0][:], 0, ((nc.scalar.copy, 0, 0, P // 2), (nc.scalar.copy, 1, 0, P // 2)))
         late_shares = (
-            (nc.scalar.copy, 0, 0, P // 2),
-            (nc.scalar.copy, 1, 0, P // 2 - ASIDE),
-            (round_aside, 1, P // 2 - ASIDE, P // 2),
+            (nc.scalar.copy, 0, 0, P // 2 - ASIDE[0]),
+            (round_aside, 0, P // 2 - ASIDE[0], P // 2),
+            (nc.scalar.copy, 1, 0, P // 2 - ASIDE[1]),
+            (round_aside, 1, P // 2 - ASIDE[1], P // 2),
         )
         deal(q1_dealt, q1_raw[1][:], P // 2, late_shares)
 
@@ -223,7 +224,7 @@ def tile_attend_gat_k_kernel(tc, qT, kT, vT, doT, rw, qm, offs, out):
                 op1=ALU.mult,
             )
 
-        ds_mx = {(g, h): mx_pair(f"ds{g}{h}", N // 2) for g, h in ((0, 0), (1, 0), (1, 1))}
+        ds_mx = {(g, h): mx_pair(f"ds{g}{h}", N // 2) for g, h in ((1, 0), (1, 1))}
         ds0 = tile([P, N - P, PACK], BF16, "ds0")
         key_codes(0, "k_codes0")
         nc.vector.tensor_copy(k_words[:, last, 2:PACK], k_rows[:].rearrange("p j n -> p n j"))
@@ -232,9 +233,10 @@ def tile_attend_gat_k_kernel(tc, qT, kT, vT, doT, rw, qm, offs, out):
         score = [scores(0, c) for c in range(PACK)]
         for c in range(PACK - 1):
             ds_words(ds0[:, block(c), :], score[c], 0, c)
-        quantize(ds_mx[0, 0], low, ds0[:, low, :].rearrange("p n t -> p (n t)"), E5)
         quantize_dealt(q_mx[1], q1_dealt, E4)
-        ds03 = tile([P, P, PACK], BF16, "q1_dealt0")
+        ds_mx[0, 0] = (tile([P, N // 2], U32, "q1_dealt0"), tile([P, N // 2], U8, "ds00_scales"))
+        quantize(ds_mx[0, 0], low, ds0[:, low, :].rearrange("p n t -> p (n t)"), E5)
+        ds03 = tile([P, P, PACK], BF16, "q1_dealt1")
         ds_words(ds03[:], score[PACK - 1], 0, PACK - 1)
         score = [scores(1, c) for c in range(PACK)]
 

@@ -21,7 +21,6 @@ PACK = 4
 PASS = P * PACK
 SPLIT = 96
 ASIDE = (28, 16)
-SCORE_BANKS = 3
 
 
 def tile_attend_gat_k_kernel(tc, qT, kT, vT, doT, rw, qm, offs, out):
@@ -29,10 +28,14 @@ def tile_attend_gat_k_kernel(tc, qT, kT, vT, doT, rw, qm, offs, out):
     with ExitStack() as ctx:
         lists = ctx.enter_context(tc.tile_pool(name="lists", bufs=1))
         sb = ctx.enter_context(tc.tile_pool(name="sb", bufs=1))
+        late = ctx.enter_context(tc.tile_pool(name="late", bufs=1))
         ps = ctx.enter_context(tc.psum_pool(name="ps", bufs=4))
 
         def tile(shape, dtype, name):
             return sb.tile(shape, dtype, name=name, align_bytes=256)
+
+        def placed(shape, dtype, name, offset):
+            return late.tile(shape, dtype, name=name, align_bytes=64, offset=offset)
 
         def load_planes(pool, name, j0, count):
             held = tile([P, count * T], F32, f"{name}{j0}")
@@ -210,7 +213,10 @@ def tile_attend_gat_k_kernel(tc, qT, kT, vT, doT, rw, qm, offs, out):
             quantize(k_mx[c], block(0), k_words[:, block(c), :].rearrange("p n j -> p (n j)"), E4)
 
         def scores(g, c):
-            bank = ps.tile([P, PACK, P], F32, name=f"score{(g * PACK + c) % SCORE_BANKS}", bufs=1)
+            if (g, c) == (0, PACK - 1):
+                bank = ps.tile([P, PACK, P], F32, name="dp_bank", bufs=4)
+            else:
+                bank = ps.tile([P, PACK, P], F32, name=f"score{c % 2 if g else c}", bufs=1)
             quarter_product(bank, q_mx[g], E4, k_mx[c], 0)
             return bank
 
@@ -236,11 +242,11 @@ def tile_attend_gat_k_kernel(tc, qT, kT, vT, doT, rw, qm, offs, out):
         quantize_dealt(q_mx[1], q1_dealt, E4)
         ds_mx[0, 0] = (tile([P, N // 2], U32, "q1_dealt0"), tile([P, N // 2], U8, "ds00_scales"))
         quantize(ds_mx[0, 0], low, ds0[:, low, :].rearrange("p n t -> p (n t)"), E5)
-        ds03 = tile([P, P, PACK], BF16, "q1_dealt1")
-        ds_words(ds03[:], score[PACK - 1], 0, PACK - 1)
+        ds_mx[0, 1] = (tile([P, N // 2], U32, "q1_dealt1"), tile([P, N // 2], U8, "ds01_scales"))
+        quantize(ds_mx[0, 1], block(0), ds0[:, block(2), :].rearrange("p n t -> p (n t)"), E5)
+        score03 = score[PACK - 1]
         score = [scores(1, c) for c in range(PACK)]
 
-        qm_words = {}
         qm_mx = {}
 
         def qm_quantize_both(j, words, codes):
@@ -263,55 +269,68 @@ def tile_attend_gat_k_kernel(tc, qT, kT, vT, doT, rw, qm, offs, out):
             dk_columns(j, low, "dp_bank", 4, dk[:], nc.scalar.copy)
             nc.scalar.activation(windows[j][:].indirect(listed(low)), dk[:], COPY)
 
-        for j in range(2):
-            qm_words[j] = tile([P, 2, P, PACK], BF16, f"qm_words{j}")
-        for j, g in ((0, 0), (0, 1), (1, 1), (1, 0)):
-            weave(nc.scalar.copy, qm_words[j][:, g], qm_raw[j, g])
+        def flat(words):
+            return words.rearrange("p n t -> p (n t)")
 
-        ds1 = [tile([P, P, PACK], BF16, f"ds1{c}") for c in range(2)]
+        words0 = tile([P, 2, P, PACK], BF16, "qm_words0")
+        words11 = tile([P, P, PACK], BF16, "qm_words11")
+        for g in range(2):
+            weave(nc.scalar.copy, words0[:, g], qm_raw[0, g])
+        weave(nc.scalar.copy, words11[:], qm_raw[1, 1])
+
+        pair = (tile([P, P], U32, "qm_codes00"), tile([P, P], U8, "qm_scales00"))
+        quantize(pair, block(0), flat(words0[:, 0]), E4)
+        qm_mx[0, 0] = pair
+
+        half = P // 2
+        ds1 = [tile([P, P, PACK], BF16, "ds10"), placed([P, P, PACK], BF16, "ds11", 448)]
         for c in (0, 1):
             ds_words(ds1[c][:], score[c], 1, c)
-        qm_quantize_both(0, qm_words[0][:], tile([P, 2 * P], U32, "gated10"))
+        qm_mx[0, 1] = (tile([P, P], U32, "gated10"), tile([P, P], U8, "qm_scales01"))
+        quantize(qm_mx[0, 1], block(0), flat(words0[:, 1]), E4)
         first = tile([P, N // 2], F32, "dk_low0")
         for c in (0, 1):
-            quantize(ds_mx[1, 0], block(c), ds1[c][:].rearrange("p n t -> p (n t)"), E5)
+            quantize(ds_mx[1, 0], block(c), flat(ds1[c][:]), E5)
             dk_columns(0, block(c), "dp_bank", 4, first[:, block(c)], nc.scalar.copy)
-        half = P // 2
-        early20 = tile([P, half, PACK], BF16, "ds11")
+        early20 = placed([P, half, PACK], BF16, "early20", 0)
         weave(nc.scalar.copy, early20[:], qm_raw[2, 0][:, :, 0:half])
         nc.scalar.activation(windows[0][:].indirect(listed(low)), first[:], COPY)
-        ds_mx[0, 1] = (tile([P, N // 2], U32, "qm_words0"), tile([P, N // 2], U8, "ds01_scales"))
-        for c, words in ((1, ds03[:]), (0, ds0[:, block(2), :])):
-            quantize(ds_mx[0, 1], block(c), words.rearrange("p n t -> p (n t)"), E5)
 
-        late2 = tile([P, half + P, PACK], BF16, "ds0")
-        weave_aside(late2[:, 0:half], qm_raw[2, 0][:, :, half:P])
-        weave_aside(late2[:, half:], qm_raw[2, 1])
-        ds1.append(tile([P, P, PACK], BF16, "ds10"))
+        aside = placed([P, 2 * P + half, PACK], BF16, "aside", 512)
+        words10, late20, words21 = aside[:, 0:P], aside[:, P : P + half], aside[:, P + half :]
+        weave_aside(words10, qm_raw[1, 0])
+        weave_aside(late20, qm_raw[2, 0][:, :, half:P])
+        weave_aside(words21, qm_raw[2, 1])
+        ds03 = tile([P, P, PACK], BF16, "ds10")
+        ds_words(ds03[:], score03, 0, PACK - 1)
+        ds1.append(tile([P, P, PACK], BF16, "qm_words0"))
         ds1.append(tile([P, P, PACK], BF16, "ds13"))
         for c in (2, 3):
             ds_words(ds1[c][:], score[c], 1, c)
+        quantize(ds_mx[0, 1], block(1), flat(ds03[:]), E5)
         for c in (2, 3):
-            quantize(ds_mx[1, 1], block(c - 2), ds1[c][:].rearrange("p n t -> p (n t)"), E5)
-        qm_quantize_both(1, qm_words[1][:], tile([P, 2 * P], U32, "ds10"))
+            quantize(ds_mx[1, 1], block(c - 2), flat(ds1[c][:]), E5)
+        pair = (tile([P, 2 * P], U32, "qm_words0"), tile([P, 2 * P], U8, "qm_scales1"))
+        for g, words in enumerate((words10, words11[:])):
+            quantize(pair, block(g), flat(words), E4)
+            qm_mx[1, g] = (pair[0][:, block(g)], pair[1][:, block(g)])
         for j in range(D // P):
             dk = tile([P, N // 2], F32, ("k2", "k1", "k3", "dk_high3")[j])
             copy = nc.scalar.copy if j > 1 else nc.vector.tensor_copy
             if j == 0:
-                dk_columns(0, block(2), "dk_bank", 1, dk[:, block(0)], copy)
-                dk_columns(0, block(3), "score0", 1, dk[:, block(1)], copy)
-            else:
-                dk_columns(j, high, ("dk_bank", "score2", "score1")[j - 1], 1, dk[:], copy)
-            if j == 0:
+                dk_columns(0, block(2), "dk_bank", 1, dk[:, block(0)], nc.vector.tensor_copy)
+                dk_columns(0, block(3), "score2", 1, dk[:, block(1)], nc.scalar.copy)
                 pair = (tile([P, 2 * P], U32, "ds13"), tile([P, 2 * P], U8, "qm_scales2"))
-                quantize(pair, slice(0, half), early20[:].rearrange("p d j -> p (d j)"), E4)
-                quantize(pair, slice(half, P), late2[:, 0:half].rearrange("p d j -> p (d j)"), E4)
-                quantize(pair, block(1), late2[:, half:].rearrange("p d j -> p (d j)"), E4)
+                quantize(pair, slice(0, half), flat(early20[:]), E4)
+                quantize(pair, slice(half, P), flat(late20), E4)
+                quantize(pair, block(1), flat(words21), E4)
                 for g in range(2):
                     qm_mx[2, g] = (pair[0][:, block(g)], pair[1][:, block(g)])
-                words3 = tile([P, 2, P, PACK], BF16, "ds0")
+                words3 = placed([P, 2, P, PACK], BF16, "words3", 512)
                 for g in range(2):
                     weave_aside(words3[:, g], qm_raw[3, g])
+            else:
+                dk_columns(j, high, ("dk_bank", "score2", "score0")[j - 1], 1, dk[:], copy)
             if j == 1:
                 qm_quantize_both(3, words3[:], tile([P, 2 * P], U32, "qm_codes3"))
             nc.vector.tensor_copy(windows[j][:].indirect(listed(high)), dk[:])

@@ -286,20 +286,22 @@ def tile_attend_gat_k_kernel(tc, qT, kT, vT, doT, rw, qm, offs, out):
         ds1 = [tile([P, P, PACK], BF16, "ds10"), placed([P, P, PACK], BF16, "ds11", 448)]
         for c in (0, 1):
             ds_words(ds1[c][:], score[c], 1, c)
+        quantize(ds_mx[1, 0], block(0), flat(ds1[0][:]), E5)
         qm_mx[0, 1] = (tile([P, P], U32, "gated10"), tile([P, P], U8, "qm_scales01"))
         quantize(qm_mx[0, 1], block(0), flat(words0[:, 1]), E4)
+        quantize(ds_mx[1, 0], block(1), flat(ds1[1][:]), E5)
+        late20 = tile([P, half, PACK], BF16, "late20")
+        weave(nc.scalar.copy, late20[:], qm_raw[2, 0][:, :, half:P])
         first = tile([P, N // 2], F32, "dk_low0")
         for c in (0, 1):
-            quantize(ds_mx[1, 0], block(c), flat(ds1[c][:]), E5)
             dk_columns(0, block(c), "dp_bank", 4, first[:, block(c)], nc.scalar.copy)
         early20 = placed([P, half, PACK], BF16, "early20", 0)
         weave(nc.scalar.copy, early20[:], qm_raw[2, 0][:, :, 0:half])
         nc.scalar.activation(windows[0][:].indirect(listed(low)), first[:], COPY)
 
-        aside = placed([P, 2 * P + half, PACK], BF16, "aside", 512)
-        words10, late20, words21 = aside[:, 0:P], aside[:, P : P + half], aside[:, P + half :]
+        aside = placed([P, 2 * P, PACK], BF16, "aside", 512)
+        words10, words21 = aside[:, 0:P], aside[:, P:]
         weave_aside(words10, qm_raw[1, 0])
-        weave_aside(late20, qm_raw[2, 0][:, :, half:P])
         weave_aside(words21, qm_raw[2, 1])
         ds03 = tile([P, P, PACK], BF16, "ds10")
         ds_words(ds03[:], score03, 0, PACK - 1)
@@ -322,7 +324,7 @@ def tile_attend_gat_k_kernel(tc, qT, kT, vT, doT, rw, qm, offs, out):
                 dk_columns(0, block(3), "score2", 1, dk[:, block(1)], nc.scalar.copy)
                 pair = (tile([P, 2 * P], U32, "ds13"), tile([P, 2 * P], U8, "qm_scales2"))
                 quantize(pair, slice(0, half), flat(early20[:]), E4)
-                quantize(pair, slice(half, P), flat(late20), E4)
+                quantize(pair, slice(half, P), flat(late20[:]), E4)
                 quantize(pair, block(1), flat(words21), E4)
                 for g in range(2):
                     qm_mx[2, g] = (pair[0][:, block(g)], pair[1][:, block(g)])

from contextlib import ExitStack

import concourse.mybir as mybir
from concourse.masks import make_identity

N, T, D, DV, R = 512, 2048, 512, 512, 1024
FLOPS = 2 * R * N * (D + DV + D)

F32 = mybir.dt.float32
BF16 = mybir.dt.bfloat16
U32 = mybir.dt.uint32
U16 = mybir.dt.uint16
U8 = mybir.dt.uint8
E4 = mybir.dt.float8_e4m3fn_x4
E5 = mybir.dt.float8_e5m2_x4
ALU = mybir.AluOpType
COPY = mybir.ActivationFunctionType.Copy

P = 128
PACK = 4
PASS = P * PACK
SPLIT = 96
ASIDE = (28, 16)


def tile_attend_gat_k_kernel(tc, qT, kT, vT, doT, rw, qm, offs, out):
    nc = tc.nc
    with ExitStack() as ctx:
        lists = ctx.enter_context(tc.tile_pool(name="lists", bufs=1))
        sb = ctx.enter_context(tc.tile_pool(name="sb", bufs=1))
        late = ctx.enter_context(tc.tile_pool(name="late", bufs=1))
        ps = ctx.enter_context(tc.psum_pool(name="ps", bufs=4))

        def tile(shape, dtype, name):
            return sb.tile(shape, dtype, name=name, align_bytes=256)

        def placed(shape, dtype, name, offset):
            return late.tile(shape, dtype, name=name, align_bytes=64, offset=offset)

        def load_planes(pool, name, j0, count):
            held = tile([P, count * T], F32, f"{name}{j0}")
            rows = pool.rearrange("(p j) t -> p (j t)", j=PACK)
            nc.sync.dma_start(out=held[:], in_=rows[:, j0 * T : (j0 + count) * T])
            return [held[:, i * T : (i + 1) * T] for i in range(count)]

        def load_columns(src, r0, width, name):
            raw = tile([P, PACK, width], F32, name)
            rows = src.rearrange("(p j) r -> p j r", j=PACK)
            nc.sync.dma_start(out=raw[:], in_=rows[:, :, r0 : r0 + width])
            return raw

        gate_rows = tile([P, PASS], F32, "gate_rows")
        nc.gpsimd.memset(gate_rows[:], 0.0)
        v_planes = load_planes(vT, "v", 0, 1)
        offsets = lists.tile([P, N // 16], U16, name="offsets")
        nc.sync.dma_start(offsets[:], offs)
        nc.sync.dma_start(out=gate_rows[0:2, :], in_=rw[0].rearrange("(g r) o -> g (r o)", g=2))
        identity = tile([P, P], F32, "identity")
        make_identity(nc, identity[:])
        v_planes.extend(load_planes(vT, "v", 1, 1))
        v_planes.extend(load_planes(vT, "v", 2, 2))
        do_raw = load_columns(doT[0], 0, R, "do")
        k_planes = []
        for j in range(PACK - 1):
            k_planes.extend(load_planes(kT, "k", j, 1))
        q0_raw = load_columns(qT[0], 0, PASS, "q0")
        k_planes.extend(load_planes(kT, "k", PACK - 1, 1))
        q1_raw = [load_columns(qT[0], PASS + h * (PASS // 2), PASS // 2, f"q1{h}") for h in range(2)]
        qm_raw = {}
        for g, j0, j1, name in ((0, 0, 1, "qm00"), (1, 0, 2, "v0"), (0, 1, 3, "v1"), (1, 2, 3, "qm21"), (0, 3, 4, "k0"), (1, 3, 4, "k1")):
            held = load_columns(qm[0, g * PASS : (g + 1) * PASS, :], j0 * P, (j1 - j0) * P, name)
            for j in range(j0, j1):
                qm_raw[j, g] = held[:, :, (j - j0) * P : (j - j0 + 1) * P]

        windows = []
        for j in range(D // P):
            window = tile([P, T], F32, f"window{j}")
            nc.vector.memset(window[:], 0.0)
            windows.append(window)

        def mx_pair(name, width):
            return tile([P, width], U32, name + "_codes"), tile([P, width], U8, name + "_scales")

        def quantize(pair, cols, src, fmt):
            nc.vector.quantize_mx(out=pair[0][:, cols].bitcast(fmt), scales=pair[1][:, cols], in_=src)

        def scalar_gather(dst, src):
            nc.scalar.activation(dst, src, COPY)

        def deal(dealt, raw, s_at, shares):
            for copy, u, s0, s1 in shares:
                copy(
                    dealt[u][:, :, s_at + s0 : s_at + s1, :].rearrange("p t s j -> p s j t"),
                    raw.rearrange("p j (s t) -> p s j t", t=PACK)[:, s0:s1, :, 2 * u : 2 * u + 2],
                )

        def dealt_tiles(name):
            return [tile([P, 2, P, PACK], BF16, f"{name}_dealt{u}") for u in range(2)]

        def quantize_dealt(pair, dealt, fmt):
            for u in range(2):
                quantize(pair, slice(2 * u * P, 2 * (u + 1) * P), dealt[u][:].rearrange("p t s j -> p (t s j)"), fmt)

        def mm(acc, lhs, lcols, lfmt, rhs, rcols, rfmt, start=True, stop=True):
            nc.tensor.matmul_mx(
                out=acc,
                lhsT=lhs[0][:, lcols].bitcast(lfmt),
                lhsT_scale=lhs[1][:, lcols],
                rhs=rhs[0][:, rcols].bitcast(rfmt),
                rhs_scale=rhs[1][:, rcols],
                start=start,
                stop=stop,
            )

        def block(i):
            return slice(i * P, (i + 1) * P)

        def weave(copy, dst, src):
            copy(
                dst.rearrange("p (c i) j -> p c j i", i=4),
                src.rearrange("p j (c i) -> p c j i", i=4),
            )

        def weave_aside(words, rows):
            nc.gpsimd.tensor_scalar(
                words.rearrange("p (c i) j -> p c i j", i=4),
                rows.rearrange("p j (c i) -> p c i j", i=4),
                1.0,
                0.0,
                ALU.mult,
                ALU.add,
            )

        def round_aside(dst, src):
            in_order = "p s j t -> p s t j"
            nc.gpsimd.tensor_scalar(dst.rearrange(in_order), src.rearrange(in_order), 1.0, 0.0, ALU.mult, ALU.add)

        def quarter_product(bank, rows_mx, rows_fmt, slots_mx, c):
            for t in range(PACK):
                mm(bank[:, t, :], rows_mx, block(t), rows_fmt, slots_mx, block(c), E4)

        low, high = slice(0, N // 2), slice(N // 2, N)

        def listed(cols):
            return offsets[:, cols.start // 16 : cols.stop // 16]

        gate2 = tile([P, 2, PACK], F32, "gate2")
        turned = ps.tile([P, PACK, P], F32, name="dk_bank", bufs=1)
        for t in range(PACK):
            nc.tensor.transpose(turned[:, t, :], gate_rows[:, t:PASS:PACK], identity[:])
        nc.vector.tensor_scalar(gate2[:], turned[:, :, 0:2].rearrange("p t g -> p g t"), 2.0, None, ALU.mult)

        v_words = tile([P, N, PACK], BF16, "v_words")
        for j in range(PACK):
            copy = scalar_gather if j < 2 else nc.vector.tensor_copy
            copy(v_words[:, :, j], v_planes[j].indirect(offsets[:]))
        v_mx = mx_pair("v", N)
        quantize(v_mx, slice(0, N), v_words[:].rearrange("p n j -> p (n j)"), E4)

        both = ((nc.vector.tensor_copy, 0, 0, P), (nc.scalar.copy, 1, 0, P))
        do_dealt = [dealt_tiles(f"do{g}") for g in range(2)]
        do_mx = [mx_pair(f"do{g}", PASS) for g in range(2)]
        for g in range(2):
            deal(do_dealt[g], do_raw[:, :, g * PASS : (g + 1) * PASS], 0, both)
        for g in range(2):
            quantize_dealt(do_mx[g], do_dealt[g], E5)
        gated = {}
        for g in range(2):
            for c in range(PACK):
                bank = ps.tile([P, PACK, P], F32, name="dp_bank", bufs=4)
                quarter_product(bank, do_mx[g], E5, v_mx, c)
                gated[g, c] = tile([P, P, PACK], F32, f"gated{g}{c}")
                nc.vector.tensor_tensor(
                    gated[g, c][:],
                    bank[:].rearrange("p t n -> p n t"),
                    gate2[:, g : g + 1, :].to_broadcast([P, P, PACK]),
                    ALU.mult,
                )

        k_words = tile([P, N, PACK], BF16, "k_words")
        for j in range(2):
            scalar_gather(k_words[:, :, j], k_planes[j].indirect(offsets[:]))
        most, last = slice(0, N - P), block(PACK - 1)
        scalar_gather(k_words[:, most, 2], k_planes[2].indirect(listed(most)))
        k_rows = tile([P, 2, P], BF16, "k_rows")
        nc.vector.tensor_copy(k_rows[:, 0, :], k_planes[2].indirect(listed(last)))
        q0_dealt = dealt_tiles("q0")
        q0_shares = ((nc.vector.tensor_copy, 0, 0, P), (nc.scalar.copy, 1, 0, SPLIT), (nc.vector.tensor_copy, 1, SPLIT, P))
        deal(q0_dealt, q0_raw[:], 0, q0_shares)
        q_mx = [mx_pair(f"q{g}", PASS) for g in range(2)]
        quantize_dealt(q_mx[0], q0_dealt, E4)

        unread = ps.tile([P, N], F32, name="dk_bank", bufs=1)
        for t in range(2):
            mm(unread[:], q_mx[0], block(t), E4, v_mx, slice(0, N), E4)

        k_mx = {}
        for c in range(PACK - 1):
            scalar_gather(k_words[:, block(c), PACK - 1], k_planes[PACK - 1].indirect(listed(block(c))))
        nc.vector.tensor_copy(k_rows[:, 1, :], k_planes[PACK - 1].indirect(listed(last)))
        q1_dealt = dealt_tiles("q1")
        deal(q1_dealt, q1_raw[0][:], 0, ((nc.scalar.copy, 0, 0, P // 2), (nc.scalar.copy, 1, 0, P // 2)))
        late_shares = (
            (nc.scalar.copy, 0, 0, P // 2 - ASIDE[0]),
            (round_aside, 0, P // 2 - ASIDE[0], P // 2),
            (nc.scalar.copy, 1, 0, P // 2 - ASIDE[1]),
            (round_aside, 1, P // 2 - ASIDE[1], P // 2),
        )
        deal(q1_dealt, q1_raw[1][:], P // 2, late_shares)

        def key_codes(c, name):
            k_mx[c] = (tile([P, P], U32, name), tile([P, P], U8, f"k_scales{c}"))
            quantize(k_mx[c], block(0), k_words[:, block(c), :].rearrange("p n j -> p (n j)"), E4)

        def scores(g, c):
            if (g, c) == (0, PACK - 1):
                bank = ps.tile([P, PACK, P], F32, name="dp_bank", bufs=4)
            else:
                bank = ps.tile([P, PACK, P], F32, name=f"score{c % 2 if g else c}", bufs=1)
            quarter_product(bank, q_mx[g], E4, k_mx[c], 0)
            return bank

        def ds_words(words, bank, g, c):
            nc.vector.scalar_tensor_tensor(
                out=words,
                in0=bank[:].rearrange("p t n -> p n t"),
                scalar=0.0,
                in1=gated[g, c][:],
                op0=ALU.max,
                op1=ALU.mult,
            )

        ds_mx = {(g, h): mx_pair(f"ds{g}{h}", N // 2) for g, h in ((1, 0), (1, 1))}
        ds0 = tile([P, N - P, PACK], BF16, "ds0")
        key_codes(0, "k_codes0")
        nc.vector.tensor_copy(k_words[:, last, 2:PACK], k_rows[:].rearrange("p j n -> p n j"))
        for c in (1, 3, 2):
            key_codes(c, f"k_codes{c}")
        score = [scores(0, c) for c in range(PACK)]
        for c in range(PACK - 1):
            ds_words(ds0[:, block(c), :], score[c], 0, c)
        quantize_dealt(q_mx[1], q1_dealt, E4)
        ds_mx[0, 0] = (tile([P, N // 2], U32, "q1_dealt0"), tile([P, N // 2], U8, "ds00_scales"))
        quantize(ds_mx[0, 0], low, ds0[:, low, :].rearrange("p n t -> p (n t)"), E5)
        ds_mx[0, 1] = (tile([P, N // 2], U32, "q1_dealt1"), tile([P, N // 2], U8, "ds01_scales"))
        quantize(ds_mx[0, 1], block(0), ds0[:, block(2), :].rearrange("p n t -> p (n t)"), E5)
        score03 = score[PACK - 1]
        score = [scores(1, c) for c in range(PACK)]

        qm_mx = {}

        def qm_quantize_both(j, words, codes):
            scales = tile([P, 2 * P], U8, f"qm_scales{j}")
            quantize((codes, scales), slice(0, 2 * P), words.rearrange("p g d j -> p (g d j)"), E4)
            for g in range(2):
                qm_mx[j, g] = (codes[:, block(g)], scales[:, block(g)])

        def dk_columns(j, cols, bank_name, bufs, dk, copy):
            width = cols.stop - cols.start
            bank = ps.tile([P, width], F32, name=bank_name, bufs=bufs)
            h = cols.start // (N // 2)
            within = slice(cols.start - h * (N // 2), cols.stop - h * (N // 2))
            for g in range(2):
                mm(bank[:], qm_mx[j, g], slice(0, P), E4, ds_mx[g, h], within, E5, start=g == 0, stop=g == 1)
            copy(dk, bank[:])

        def scatter_low(j):
            dk = tile([P, N // 2], F32, f"dk_low{j}")
            dk_columns(j, low, "dp_bank", 4, dk[:], nc.scalar.copy)
            nc.scalar.activation(windows[j][:].indirect(listed(low)), dk[:], COPY)

        def flat(words):
            return words.rearrange("p n t -> p (n t)")

        words0 = tile([P, 2, P, PACK], BF16, "qm_words0")
        words11 = tile([P, P, PACK], BF16, "qm_words11")
        for g in range(2):
            weave(nc.scalar.copy, words0[:, g], qm_raw[0, g])
        weave(nc.scalar.copy, words11[:], qm_raw[1, 1])

        pair = (tile([P, P], U32, "qm_codes00"), tile([P, P], U8, "qm_scales00"))
        quantize(pair, block(0), flat(words0[:, 0]), E4)
        qm_mx[0, 0] = pair

        half = P // 2
        ds1 = [tile([P, P, PACK], BF16, "ds10"), placed([P, P, PACK], BF16, "ds11", 448)]
        for c in (0, 1):
            ds_words(ds1[c][:], score[c], 1, c)
        quantize(ds_mx[1, 0], block(0), flat(ds1[0][:]), E5)
        qm_mx[0, 1] = (tile([P, P], U32, "gated10"), tile([P, P], U8, "qm_scales01"))
        quantize(qm_mx[0, 1], block(0), flat(words0[:, 1]), E4)
        quantize(ds_mx[1, 0], block(1), flat(ds1[1][:]), E5)
        late20 = tile([P, half, PACK], BF16, "late20")
        weave(nc.scalar.copy, late20[:], qm_raw[2, 0][:, :, half:P])
        first = tile([P, N // 2], F32, "dk_low0")
        for c in (0, 1):
            dk_columns(0, block(c), "dp_bank", 4, first[:, block(c)], nc.scalar.copy)
        early20 = placed([P, half, PACK], BF16, "early20", 0)
        weave(nc.scalar.copy, early20[:], qm_raw[2, 0][:, :, 0:half])
        nc.scalar.activation(windows[0][:].indirect(listed(low)), first[:], COPY)

        aside = placed([P, 2 * P, PACK], BF16, "aside", 512)
        words10, words21 = aside[:, 0:P], aside[:, P:]
        weave_aside(words10, qm_raw[1, 0])
        weave_aside(words21, qm_raw[2, 1])
        ds03 = tile([P, P, PACK], BF16, "ds10")
        ds_words(ds03[:], score03, 0, PACK - 1)
        ds1.append(tile([P, P, PACK], BF16, "qm_words0"))
        ds1.append(tile([P, P, PACK], BF16, "ds13"))
        for c in (2, 3):
            ds_words(ds1[c][:], score[c], 1, c)
        quantize(ds_mx[0, 1], block(1), flat(ds03[:]), E5)
        for c in (2, 3):
            quantize(ds_mx[1, 1], block(c - 2), flat(ds1[c][:]), E5)
        pair = (tile([P, 2 * P], U32, "qm_words0"), tile([P, 2 * P], U8, "qm_scales1"))
        for g, words in enumerate((words10, words11[:])):
            quantize(pair, block(g), flat(words), E4)
            qm_mx[1, g] = (pair[0][:, block(g)], pair[1][:, block(g)])
        for j in range(D // P):
            dk = tile([P, N // 2], F32, ("k2", "k1", "k3", "dk_high3")[j])
            copy = nc.scalar.copy if j > 1 else nc.vector.tensor_copy
            if j == 0:
                dk_columns(0, block(2), "dk_bank", 1, dk[:, block(0)], nc.vector.tensor_copy)
                dk_columns(0, block(3), "score2", 1, dk[:, block(1)], nc.scalar.copy)
                pair = (tile([P, 2 * P], U32, "ds13"), tile([P, 2 * P], U8, "qm_scales2"))
                quantize(pair, slice(0, half), flat(early20[:]), E4)
                quantize(pair, slice(half, P), flat(late20[:]), E4)
                quantize(pair, block(1), flat(words21), E4)
                for g in range(2):
                    qm_mx[2, g] = (pair[0][:, block(g)], pair[1][:, block(g)])
                words3 = placed([P, 2, P, PACK], BF16, "words3", 512)
                for g in range(2):
                    weave_aside(words3[:, g], qm_raw[3, g])
            else:
                dk_columns(j, high, ("dk_bank", "score2", "score0")[j - 1], 1, dk[:], copy)
            if j == 1:
                qm_quantize_both(3, words3[:], tile([P, 2 * P], U32, "qm_codes3"))
            nc.vector.tensor_copy(windows[j][:].indirect(listed(high)), dk[:])
            nc.sync.dma_start(out=out[block(j), :], in_=windows[j][:])
            if j + 1 < D // P:
                scatter_low(j + 1)
